import numpy as np
import ml_dtypes


def mxq(x, axis, fmt="e4m3"):
    dtype, down = {"e4m3": (ml_dtypes.float8_e4m3fn, 7), "e5m2": (ml_dtypes.float8_e5m2, 14)}[fmt]
    v = np.moveaxis(np.asarray(x, np.float32).astype(ml_dtypes.bfloat16).astype(np.float64), axis, -1)
    blocks = v.reshape(v.shape[:-1] + (-1, 32))
    amax = np.abs(blocks).max(-1, keepdims=True)
    byte = np.maximum(np.where(amax > 0, np.frexp(amax)[1] - 1 + 127, 0) - down, 1)
    scale = np.exp2(byte - 127.0)
    codes = (blocks / scale).astype(np.float32).astype(dtype).astype(np.float64)
    return np.moveaxis((codes * scale).reshape(v.shape), -1, axis)


WIDE = False


def mx_kscale(k):
    if not WIDE:
        return np.ones(k)
    levels = np.array([18, -18])
    if k % 512:
        return np.exp2(np.random.permutation(np.resize(levels, k // 32))).repeat(32)
    a = np.empty((k // 512, 16))
    for p in range(k // 512):
        a[p, :8] = np.random.permutation(np.resize(levels, 8))
        for g in range(8):
            far = levels[np.abs(levels - a[p, g]) >= 10]
            a[p, g + 8] = far[np.random.randint(len(far))]
    return np.exp2(a.ravel()).repeat(32)


def f64(x):
    return np.asarray(x).astype(np.float64)


def striped(idx):
    return np.tile(np.asarray(idx).reshape(-1, 16).T, (8, 1)).astype(np.uint16)


def unstriped(offs):
    return offs[:16].T.reshape(-1).astype(np.int64)


B, N, T, D, R = 1, 512, 2048, 512, 1024


def setup_inputs():
    n = np.random.standard_normal
    idx = np.random.permutation(T)[:B * N]
    s = mx_kscale(D)[:, None]
    u = np.ones(T)
    u[idx] = mx_kscale(B * N)
    r = np.random.uniform(0.5, 2.0, T) * u
    x = n((B, D, R))
    return {
        "xT": (x * s).astype(np.float32),
        "wT": (n((D, T)) * (1.00 / np.sqrt(D)) / s / r).astype(np.float32),
        "y": n((B, R, N)).astype(np.float32),
        "wt": (np.random.uniform(0.5, 1.5, (B, R, 1)) * 1.0 / np.sqrt(R)).astype(np.float32),
        "ts": np.tile(r, (128, 1)).astype(np.float32),
        "offs": striped(idx),
    }


def reference(xT, wT, y, wt, ts, offs):
    idx = unstriped(offs)
    pick = lambda x: x[:, idx].reshape(x.shape[0], B, N).transpose(1, 0, 2)
    w = pick(f64(wT))
    a = mxq(f64(xT), 1, "e4m3").transpose(0, 2, 1) @ mxq(w, 1, "e4m3")
    ts_ = pick(f64(ts))[:, :1, :]
    a = a * ts_
    q = a - f64(y)
    g = f64(wt) * q * np.exp(-0.5 * q * q)
    g = g * ts_
    gx = mxq(g, 2, "e5m2") @ mxq(w, 2, "e4m3").transpose(0, 2, 1)
    return gx

@@ -1,0 +1,286 @@
+from contextlib import ExitStack
+
+import concourse.mybir as mybir
+
+F32 = mybir.dt.float32
+BF16 = mybir.dt.bfloat16
+U32 = mybir.dt.uint32
+U16 = mybir.dt.uint16
+U8 = mybir.dt.uint8
+E4M3X4 = mybir.dt.float8_e4m3fn_x4
+E5M2X4 = mybir.dt.float8_e5m2_x4
+ACT = mybir.ActivationFunctionType
+MULT = mybir.AluOpType.mult
+
+P = 128
+PACK = 4
+SLOTS = 512
+ITEMS = 2048
+FEATS = 512
+ROWS = 1024
+CHUNKS = ROWS // P
+RUN = ITEMS // P
+ADD = mybir.AluOpType.add
+IS_EQUAL = mybir.AluOpType.is_equal
+QUAD = 32
+ROW_LOADS = ((0, 2), (2, 2), (4, 2), (6, 2))
+
+FLOPS = 2 * 2 * ROWS * SLOTS * FEATS
+BYTES = 4 * (FEATS * ROWS + FEATS * ITEMS + ROWS * SLOTS + ROWS + ITEMS + ROWS * FEATS) + 2 * P * SLOTS // 16
+
+
+def tile_attend_gwel_x_ts_kernel(tc, xT, wT, y, wt, ts, offs, out):
+    nc = tc.nc
+    with ExitStack() as ctx:
+        keep = ctx.enter_context(tc.tile_pool(name="keep", bufs=1))
+        work = ctx.enter_context(tc.tile_pool(name="work", bufs=3))
+        psum = ctx.enter_context(tc.psum_pool(name="psum", bufs=1))
+
+        offsets = keep.tile([P, SLOTS // 16], U16, name="offsets")
+        nc.sync.dma_start(offsets[:], offs)
+
+        ts_runs = keep.tile([P, RUN], F32, name="ts_runs")
+        nc.sync.dma_start(out=ts_runs[:], in_=ts[0].rearrange("(n k) -> n k", k=RUN))
+        wt_col = keep.tile([P, CHUNKS], F32, name="wt_col")
+        with nc.allow_non_contiguous_dma(reason="one weight a partition and chunk"):
+            nc.scalar.dma_start(out=wt_col[:], in_=wt[0].rearrange("(c p) o -> p (c o)", p=P))
+
+        w_planes = wT.rearrange("(p t) n -> t p n", t=PACK)
+        w_window = []
+        for t in range(PACK):
+            plane = keep.tile([P, ITEMS], F32, name="w_window%d" % t)
+            nc.sync.dma_start(out=plane[:], in_=w_planes[t])
+            w_window.append(plane)
+
+        x_view = xT[0].rearrange("(p t) r -> p t r", t=PACK)
+        y_view = y[0].rearrange("(c p) n -> p c n", p=P)
+        x_raw = {}
+        y_sb = {}
+
+        def load_x(first, count):
+            raw = keep.tile([P, PACK, count * P], F32, name="x_raw%d" % first)
+            nc.sync.dma_start(out=raw[:], in_=x_view[:, :, first * P : (first + count) * P])
+            for c in range(first, first + count):
+                x_raw[c] = raw[:, :, (c - first) * P : (c - first + 1) * P]
+
+        def load_y(first, count):
+            raw = keep.tile([P, count, SLOTS], F32, name="y_raw%d" % first)
+            nc.sync.dma_start(out=raw[:], in_=y_view[:, first : first + count, :])
+            for c in range(first, first + count):
+                y_sb[c] = raw[:, c - first, :]
+
+        for first, count in ROW_LOADS:
+            load_x(first, count)
+            load_y(first, count)
+
+        ones = keep.tile([P, QUAD], F32, name="ones")
+        nc.vector.memset(ones[:], 1.0)
+        ident = keep.tile([P, P], F32, name="ident")
+        nc.vector.memset(ident[:], 0.0)
+        column = keep.tile([P, QUAD], F32, name="column", align_bytes=64)
+        nc.vector.tensor_tensor_scan(out=column[:], data0=ones[:], data1=ones[:], initial=0.0, op0=MULT, op1=ADD)
+        row = keep.tile([P, QUAD], F32, name="row", align_bytes=64)
+        nc.vector.transpose(out=row[:], in_=column[:])
+        for q in range(P // QUAD):
+            band = slice(q * QUAD, (q + 1) * QUAD)
+            nc.vector.tensor_tensor(out=ident[band, band], in0=column[band, :], in1=row[band, :], op=IS_EQUAL)
+        ident_bf = keep.tile([P, P], BF16, name="ident_bf")
+        nc.vector.tensor_copy(out=ident_bf[:], in_=ident[:])
+
+        ts_window = keep.tile([P, ITEMS], F32, name="ts_window")
+        ts_lines = ts_window[:].rearrange("p (n b k) -> p n b k", b=RUN // PACK, k=PACK)
+        for b in range(RUN // PACK):
+            spread = psum.tile([P, PACK, P], F32, name="spread", tag="resid", bufs=3)
+            for k in range(PACK):
+                col = PACK * b + k
+                nc.tensor.transpose(spread[:, k, :], ts_runs[:, col : col + 1].to_broadcast([P, P]), ident[:])
+            if b % 2 == 0:
+                nc.scalar.activation(out=ts_lines[:, :, b, :], in_=spread[:].rearrange("p k n -> p n k"), func=ACT.Copy)
+            else:
+                nc.vector.tensor_copy(out=ts_lines[:, :, b, :], in_=spread[:].rearrange("p k n -> p n k"))
+        nts_listed = keep.tile([P, SLOTS], F32, name="nts_listed")
+        nts = keep.tile([P, PACK, P], F32, name="nts")
+
+        def gather_scales():
+            nc.vector.tensor_scalar(
+                out=nts_listed[:], in0=ts_window[:].indirect(offsets[:]), scalar1=-1.0, scalar2=0.0, op0=MULT, op1=ADD
+            )
+            nc.scalar.copy(out=nts[:].rearrange("p j s -> p s j"), in_=nts_listed[:].rearrange("p (s j) -> p s j", j=PACK))
+
+        nts_flat = nts[:].rearrange("p j s -> p (j s)")
+
+        w_d = keep.tile([P, PACK, P, PACK], BF16, name="w_d", align_bytes=64)
+        w_i = keep.tile([P, PACK, P, PACK], BF16, name="w_i", align_bytes=64)
+        wi_codes = keep.tile([P, FEATS], U32, name="wi_codes", align_bytes=64)
+        wi_scales = keep.tile([P, FEATS], U8, name="wi_scales", align_bytes=64)
+        wd_codes = keep.tile([P, SLOTS], U32, name="wd_codes", align_bytes=64)
+        wd_scales = keep.tile([P, SLOTS], U8, name="wd_scales", align_bytes=64)
+
+        def gather_plane(t):
+            nc.vector.tensor_copy(
+                out=w_d[:, :, :, t].rearrange("p j s -> p s j"), in_=w_window[t][:].indirect(offsets[:])
+            )
+
+        def turn_plane(t):
+            turned = psum.tile([P, PACK, P], BF16, name="turned", tag="misc", bufs=1)
+            for j in range(PACK):
+                nc.tensor.transpose(turned[:, j, :], w_d[:, j, :, t], ident_bf[:])
+            nc.scalar.copy(out=w_i[:, t, :, :], in_=turned[:].rearrange("s j p -> s p j"))
+            nc.vector.quantize_mx(
+                out=wi_codes[:, t * P : (t + 1) * P].bitcast(E4M3X4),
+                scales=wi_scales[:, t * P : (t + 1) * P],
+                in_=w_i[:, t, :, :].rearrange("s p j -> s (p j)"),
+            )
+
+        x_bf = {}
+        x_codes = {}
+        x_scales = {}
+
+        def cast_x(c):
+            x_bf[c] = work.tile([P, P, PACK], BF16, name="x_bf", align_bytes=64)
+            nc.scalar.copy(
+                out=x_bf[c][:].rearrange("p (a i) t -> p a t i", i=4),
+                in_=x_raw[c].rearrange("p t (a i) -> p a t i", i=4),
+            )
+
+        def quantize_x(c):
+            x_codes[c] = keep.tile([P, P], U32, name="x_codes%d" % c, align_bytes=64)
+            x_scales[c] = keep.tile([P, P], U8, name="x_scales%d" % c, align_bytes=64)
+            nc.vector.quantize_mx(
+                out=x_codes[c][:].bitcast(E4M3X4), scales=x_scales[c][:], in_=x_bf[c][:].rearrange("p r t -> p (r t)")
+            )
+
+        factor = {}
+
+        def prepare_factor(c):
+            rowwise = work.tile([P, SLOTS], F32, name="rowwise")
+            nc.gpsimd.tensor_scalar(
+                out=rowwise[:], in0=nts_flat, scalar1=wt_col[:, c : c + 1], scalar2=0.0, op0=MULT, op1=ADD
+            )
+            f_ps = psum.tile([P, PACK, P], F32, name="f_ps", tag="grad", bufs=2)
+            for j in range(PACK):
+                nc.tensor.transpose(f_ps[:, j, :], rowwise[:, j * P : (j + 1) * P], ident[:])
+            factor[c] = keep.tile([P, P, PACK], F32, name="factor%d" % c)
+            nc.scalar.copy(out=factor[c][:], in_=f_ps[:].rearrange("s j r -> s r j"))
+
+        score, neg_a, neg_q, square, scaled, bell, h, h_codes, h_scales, grad = ({} for i in range(10))
+
+        def multiply_scores(c):
+            score[c] = psum.tile([P, SLOTS], F32, name="score", tag="score", bufs=2)
+            nc.tensor.matmul_mx(
+                out=score[c][:],
+                lhsT=x_codes[c][:].bitcast(E4M3X4),
+                lhsT_scale=x_scales[c][:],
+                rhs=wd_codes[:].bitcast(E4M3X4),
+                rhs_scale=wd_scales[:],
+                start=True,
+                stop=True,
+            )
+
+        def turn_targets(c):
+            neg_q[c] = psum.tile([P, PACK, P], F32, name="neg_q", tag="resid", bufs=3)
+            for j in range(PACK):
+                nc.tensor.matmul(
+                    out=neg_q[c][:, j, :],
+                    lhsT=y_sb[c][:, j::PACK],
+                    rhs=ident[:],
+                    start=(j == 0),
+                    stop=False,
+                    is_transpose=True,
+                )
+
+        def scale_scores(c):
+            neg_a[c] = work.tile([P, SLOTS], F32, name="neg_a")
+            nc.vector.tensor_tensor(out=neg_a[c][:], in0=score[c][:], in1=nts_flat, op=MULT)
+
+        def turn_scores(c):
+            for j in range(PACK):
+                nc.tensor.matmul(
+                    out=neg_q[c][:, j, :],
+                    lhsT=neg_a[c][:, j * P : (j + 1) * P],
+                    rhs=ident[:],
+                    start=False,
+                    stop=(j == PACK - 1),
+                    is_transpose=True,
+                )
+
+        def square_residual(c):
+            square[c] = work.tile([P, P, PACK], F32, name="square")
+            nc.scalar.activation(out=square[c][:], in_=neg_q[c][:].rearrange("s j r -> s r j"), func=ACT.Square)
+
+        def scale_residual(c):
+            scaled[c] = work.tile([P, P, PACK], F32, name="scaled")
+            nc.vector.tensor_tensor(
+                out=scaled[c][:], in0=neg_q[c][:].rearrange("s j r -> s r j"), in1=factor[c][:], op=MULT
+            )
+
+        def exponentiate(c):
+            bell[c] = work.tile([P, P, PACK], F32, name="bell")
+            nc.scalar.activation(out=bell[c][:], in_=square[c][:], func=ACT.Exp, scale=-0.5)
+
+        def form_h(c):
+            h[c] = work.tile([P, P, PACK], BF16, name="h", align_bytes=64)
+            nc.vector.tensor_tensor(out=h[c][:], in0=scaled[c][:], in1=bell[c][:], op=MULT)
+
+        def quantize_h(c):
+            h_codes[c] = work.tile([P, P], U32, name="h_codes", align_bytes=64)
+            h_scales[c] = work.tile([P, P], U8, name="h_scales", align_bytes=64)
+            nc.vector.quantize_mx(
+                out=h_codes[c][:].bitcast(E5M2X4), scales=h_scales[c][:], in_=h[c][:].rearrange("s r j -> s (r j)")
+            )
+
+        def multiply_gradient(c):
+            grad[c] = psum.tile([P, PACK, P], F32, name="grad", tag="grad", bufs=2)
+            nc.tensor.matmul_mx(
+                out=grad[c][:].rearrange("r t p -> r (t p)"),
+                lhsT=h_codes[c][:].bitcast(E5M2X4),
+                lhsT_scale=h_scales[c][:],
+                rhs=wi_codes[:].bitcast(E4M3X4),
+                rhs_scale=wi_scales[:],
+                start=True,
+                stop=True,
+            )
+
+        def store_gradient(c):
+            result = work.tile([P, P, PACK], F32, name="result")
+            nc.scalar.copy(out=result[:], in_=grad[c][:].rearrange("r t p -> r p t"))
+            nc.sync.dma_start(out=out[0, c * P : (c + 1) * P, :], in_=result[:].rearrange("r p t -> r (p t)"))
+
+        gather_plane(0)
+        gather_scales()
+        for t in range(1, PACK):
+            turn_plane(t - 1)
+            gather_plane(t)
+        cast_x(0)
+        quantize_x(0)
+        nc.vector.quantize_mx(
+            out=wd_codes[:].bitcast(E4M3X4), scales=wd_scales[:], in_=w_d[:].rearrange("p j s t -> p (j s t)")
+        )
+        multiply_scores(0)
+        turn_targets(0)
+        cast_x(1)
+        quantize_x(1)
+        turn_plane(PACK - 1)
+        for c in range(CHUNKS):
+            prepare_factor(c)
+        cast_x(2)
+
+        pipeline = (
+            (multiply_gradient, -3),
+            (scale_scores, 0),
+            (square_residual, -1),
+            (multiply_scores, 1),
+            (turn_targets, 1),
+            (form_h, -2),
+            (exponentiate, -1),
+            (turn_scores, 0),
+            (scale_residual, -1),
+            (store_gradient, -3),
+            (quantize_h, -2),
+            (quantize_x, 2),
+            (cast_x, 3),
+        )
+        for step in range(CHUNKS + 3):
+            for stage, shift in pipeline:
+                if 0 <= step + shift < CHUNKS:
+                    stage(step + shift)

@@ -23,6 +23,7 @@ RUN = ITEMS // P
 ADD = mybir.AluOpType.add
 IS_EQUAL = mybir.AluOpType.is_equal
 QUAD = 32
+SUBTRACT = mybir.AluOpType.subtract
 ROW_LOADS = ((0, 2), (2, 2), (4, 2), (6, 2))
 
 FLOPS = 2 * 2 * ROWS * SLOTS * FEATS
@@ -48,7 +49,7 @@ def tile_attend_gwel_x_ts_kernel(tc, xT, wT, y, wt, ts, offs, out):
         w_planes = wT.rearrange("(p t) n -> t p n", t=PACK)
         w_window = []
         for t in range(PACK):
-            plane = keep.tile([P, ITEMS], F32, name="w_window%d" % t)
+            plane = keep.tile([P, ITEMS], F32, name="w_window%d" % t, tag="w_slot%d" % t)
             nc.sync.dma_start(out=plane[:], in_=w_planes[t])
             w_window.append(plane)
 
@@ -90,7 +91,7 @@ def tile_attend_gwel_x_ts_kernel(tc, xT, wT, y, wt, ts, offs, out):
         ts_window = keep.tile([P, ITEMS], F32, name="ts_window")
         ts_lines = ts_window[:].rearrange("p (n b k) -> p n b k", b=RUN // PACK, k=PACK)
         for b in range(RUN // PACK):
-            spread = psum.tile([P, PACK, P], F32, name="spread", tag="resid", bufs=3)
+            spread = psum.tile([P, PACK, P], F32, name="spread", tag="turn", bufs=4)
             for k in range(PACK):
                 col = PACK * b + k
                 nc.tensor.transpose(spread[:, k, :], ts_runs[:, col : col + 1].to_broadcast([P, P]), ident[:])
@@ -98,39 +99,30 @@ def tile_attend_gwel_x_ts_kernel(tc, xT, wT, y, wt, ts, offs, out):
                 nc.scalar.activation(out=ts_lines[:, :, b, :], in_=spread[:].rearrange("p k n -> p n k"), func=ACT.Copy)
             else:
                 nc.vector.tensor_copy(out=ts_lines[:, :, b, :], in_=spread[:].rearrange("p k n -> p n k"))
-        nts_listed = keep.tile([P, SLOTS], F32, name="nts_listed")
-        nts = keep.tile([P, PACK, P], F32, name="nts")
+        ts_col = keep.tile([P, PACK], F32, name="ts_col")
 
-        def gather_scales():
-            nc.vector.tensor_scalar(
-                out=nts_listed[:], in0=ts_window[:].indirect(offsets[:]), scalar1=-1.0, scalar2=0.0, op0=MULT, op1=ADD
-            )
-            nc.scalar.copy(out=nts[:].rearrange("p j s -> p s j"), in_=nts_listed[:].rearrange("p (s j) -> p s j", j=PACK))
 
-        nts_flat = nts[:].rearrange("p j s -> p (j s)")
-
-        w_d = keep.tile([P, PACK, P, PACK], BF16, name="w_d", align_bytes=64)
-        w_i = keep.tile([P, PACK, P, PACK], BF16, name="w_i", align_bytes=64)
+        w_d = keep.tile([P, SLOTS, PACK], BF16, name="w_d", align_bytes=64)
+        w_i = keep.tile([P, FEATS, PACK], BF16, name="w_i", align_bytes=64)
         wi_codes = keep.tile([P, FEATS], U32, name="wi_codes", align_bytes=64)
         wi_scales = keep.tile([P, FEATS], U8, name="wi_scales", align_bytes=64)
         wd_codes = keep.tile([P, SLOTS], U32, name="wd_codes", align_bytes=64)
         wd_scales = keep.tile([P, SLOTS], U8, name="wd_scales", align_bytes=64)
 
-        def gather_plane(t):
-            nc.vector.tensor_copy(
-                out=w_d[:, :, :, t].rearrange("p j s -> p s j"), in_=w_window[t][:].indirect(offsets[:])
-            )
+        w_listed = [keep.tile([P, 2, SLOTS], BF16, name="w_listed%d" % u) for u in range(2)]
 
-        def turn_plane(t):
-            turned = psum.tile([P, PACK, P], BF16, name="turned", tag="misc", bufs=1)
+        def gather_plane(t):
+            nc.vector.tensor_copy(out=w_listed[t // 2][:, t % 2, :], in_=w_window[t][:].indirect(offsets[:]))
+
+        def weave_pair(u):
+            nc.vector.tensor_copy(out=w_d[:, :, 2 * u : 2 * u + 2], in_=w_listed[u][:].rearrange("p e i -> p i e"))
+
+        def turn_plane(t, bank):
+            turned = psum.tile([P, PACK, P], BF16, name="turned", tag=bank, bufs=2)
             for j in range(PACK):
-                nc.tensor.transpose(turned[:, j, :], w_d[:, j, :, t], ident_bf[:])
-            nc.scalar.copy(out=w_i[:, t, :, :], in_=turned[:].rearrange("s j p -> s p j"))
-            nc.vector.quantize_mx(
-                out=wi_codes[:, t * P : (t + 1) * P].bitcast(E4M3X4),
-                scales=wi_scales[:, t * P : (t + 1) * P],
-                in_=w_i[:, t, :, :].rearrange("s p j -> s (p j)"),
-            )
+                nc.tensor.transpose(turned[:, j, :], w_listed[t // 2][:, t % 2, j::PACK], ident_bf[:])
+            cols = slice(t * P, (t + 1) * P)
+            nc.scalar.copy(out=w_i[:, cols, :], in_=turned[:].rearrange("s j p -> s p j"))
 
         x_bf = {}
         x_codes = {}
@@ -150,20 +142,7 @@ def tile_attend_gwel_x_ts_kernel(tc, xT, wT, y, wt, ts, offs, out):
                 out=x_codes[c][:].bitcast(E4M3X4), scales=x_scales[c][:], in_=x_bf[c][:].rearrange("p r t -> p (r t)")
             )
 
-        factor = {}
-
-        def prepare_factor(c):
-            rowwise = work.tile([P, SLOTS], F32, name="rowwise")
-            nc.gpsimd.tensor_scalar(
-                out=rowwise[:], in0=nts_flat, scalar1=wt_col[:, c : c + 1], scalar2=0.0, op0=MULT, op1=ADD
-            )
-            f_ps = psum.tile([P, PACK, P], F32, name="f_ps", tag="grad", bufs=2)
-            for j in range(PACK):
-                nc.tensor.transpose(f_ps[:, j, :], rowwise[:, j * P : (j + 1) * P], ident[:])
-            factor[c] = keep.tile([P, P, PACK], F32, name="factor%d" % c)
-            nc.scalar.copy(out=factor[c][:], in_=f_ps[:].rearrange("s j r -> s r j"))
-
-        score, neg_a, neg_q, square, scaled, bell, h, h_codes, h_scales, grad = ({} for i in range(10))
+        score, scaled, resid, square, bell, g, g_turned, h, h_codes, h_scales, grad = ({} for i in range(11))
 
         def multiply_scores(c):
             score[c] = psum.tile([P, SLOTS], F32, name="score", tag="score", bufs=2)
@@ -177,50 +156,41 @@ def tile_attend_gwel_x_ts_kernel(tc, xT, wT, y, wt, ts, offs, out):
                 stop=True,
             )
 
-        def turn_targets(c):
-            neg_q[c] = psum.tile([P, PACK, P], F32, name="neg_q", tag="resid", bufs=3)
-            for j in range(PACK):
-                nc.tensor.matmul(
-                    out=neg_q[c][:, j, :],
-                    lhsT=y_sb[c][:, j::PACK],
-                    rhs=ident[:],
-                    start=(j == 0),
-                    stop=False,
-                    is_transpose=True,
-                )
-
         def scale_scores(c):
-            neg_a[c] = work.tile([P, SLOTS], F32, name="neg_a")
-            nc.vector.tensor_tensor(out=neg_a[c][:], in0=score[c][:], in1=nts_flat, op=MULT)
+            scaled[c] = work.tile([P, SLOTS], F32, name="scaled")
+            nc.vector.tensor_tensor(out=scaled[c][:], in0=score[c][:], in1=ts_listed[:], op=MULT)
 
-        def turn_scores(c):
-            for j in range(PACK):
-                nc.tensor.matmul(
-                    out=neg_q[c][:, j, :],
-                    lhsT=neg_a[c][:, j * P : (j + 1) * P],
-                    rhs=ident[:],
-                    start=False,
-                    stop=(j == PACK - 1),
-                    is_transpose=True,
-                )
+        def subtract_targets(c):
+            resid[c] = work.tile([P, SLOTS], F32, name="resid")
+            nc.vector.tensor_tensor(out=resid[c][:], in0=scaled[c][:], in1=y_sb[c], op=SUBTRACT)
 
         def square_residual(c):
-            square[c] = work.tile([P, P, PACK], F32, name="square")
-            nc.scalar.activation(out=square[c][:], in_=neg_q[c][:].rearrange("s j r -> s r j"), func=ACT.Square)
-
-        def scale_residual(c):
-            scaled[c] = work.tile([P, P, PACK], F32, name="scaled")
-            nc.vector.tensor_tensor(
-                out=scaled[c][:], in0=neg_q[c][:].rearrange("s j r -> s r j"), in1=factor[c][:], op=MULT
-            )
+            square[c] = work.tile([P, SLOTS], F32, name="square")
+            nc.scalar.activation(out=square[c][:], in_=resid[c][:], func=ACT.Square)
 
         def exponentiate(c):
-            bell[c] = work.tile([P, P, PACK], F32, name="bell")
+            bell[c] = work.tile([P, SLOTS], F32, name="bell")
             nc.scalar.activation(out=bell[c][:], in_=square[c][:], func=ACT.Exp, scale=-0.5)
+
+        def form_g(c):
+            g[c] = work.tile([P, SLOTS], F32, name="g")
+            nc.vector.scalar_tensor_tensor(
+                out=g[c][:], in0=resid[c][:], scalar=wt_col[:, c : c + 1], in1=bell[c][:], op0=MULT, op1=MULT
+            )
+
+        def turn_g(c):
+            g_turned[c] = psum.tile([P, PACK, P], F32, name="g_turned", tag="turn", bufs=4)
+            for j in range(PACK):
+                nc.tensor.transpose(g_turned[c][:, j, :], g[c][:, j::PACK], ident[:])
 
         def form_h(c):
             h[c] = work.tile([P, P, PACK], BF16, name="h", align_bytes=64)
-            nc.vector.tensor_tensor(out=h[c][:], in0=scaled[c][:], in1=bell[c][:], op=MULT)
+            nc.vector.tensor_tensor(
+                out=h[c][:],
+                in0=g_turned[c][:].rearrange("s j r -> s r j"),
+                in1=ts_col[:].unsqueeze(1).to_broadcast([P, P, PACK]),
+                op=MULT,
+            )
 
         def quantize_h(c):
             h_codes[c] = work.tile([P, P], U32, name="h_codes", align_bytes=64)
@@ -230,9 +200,9 @@ def tile_attend_gwel_x_ts_kernel(tc, xT, wT, y, wt, ts, offs, out):
             )
 
         def multiply_gradient(c):
-            grad[c] = psum.tile([P, PACK, P], F32, name="grad", tag="grad", bufs=2)
+            grad[c] = psum.tile([P, FEATS], F32, name="grad", tag="grad", bufs=2)
             nc.tensor.matmul_mx(
-                out=grad[c][:].rearrange("r t p -> r (t p)"),
+                out=grad[c][:],
                 lhsT=h_codes[c][:].bitcast(E5M2X4),
                 lhsT_scale=h_scales[c][:],
                 rhs=wi_codes[:].bitcast(E4M3X4),
@@ -242,41 +212,49 @@ def tile_attend_gwel_x_ts_kernel(tc, xT, wT, y, wt, ts, offs, out):
             )
 
         def store_gradient(c):
-            result = work.tile([P, P, PACK], F32, name="result")
-            nc.scalar.copy(out=result[:], in_=grad[c][:].rearrange("r t p -> r p t"))
-            nc.sync.dma_start(out=out[0, c * P : (c + 1) * P, :], in_=result[:].rearrange("r p t -> r (p t)"))
+            result = work.tile([P, FEATS], F32, name="result")
+            nc.scalar.copy(
+                out=result[:].rearrange("r (p t) -> r p t", t=PACK),
+                in_=grad[c][:].rearrange("r (t p) -> r p t", t=PACK),
+            )
+            nc.sync.dma_start(out=out[0, c * P : (c + 1) * P, :], in_=result[:])
 
         gather_plane(0)
-        gather_scales()
-        for t in range(1, PACK):
-            turn_plane(t - 1)
-            gather_plane(t)
+        ts_listed = keep.tile([P, SLOTS], F32, name="ts_listed", tag="w_slot0")
+        nc.vector.tensor_copy(out=ts_listed[:], in_=ts_window[:].indirect(offsets[:]))
+        ts_ps = psum.tile([P, PACK, P], F32, name="ts_ps", tag="grad", bufs=2)
+        for j in range(PACK):
+            nc.tensor.transpose(ts_ps[:, j, :], ts_listed[:, j::PACK], ident[:])
+        nc.scalar.copy(out=ts_col[:], in_=ts_ps[:, :, 0])
+        gather_plane(1)
+        gather_plane(2)
+        gather_plane(3)
+        weave_pair(0)
+        weave_pair(1)
         cast_x(0)
         quantize_x(0)
         nc.vector.quantize_mx(
-            out=wd_codes[:].bitcast(E4M3X4), scales=wd_scales[:], in_=w_d[:].rearrange("p j s t -> p (j s t)")
+            out=wd_codes[:].bitcast(E4M3X4), scales=wd_scales[:], in_=w_d[:].rearrange("p i t -> p (i t)")
         )
         multiply_scores(0)
-        turn_targets(0)
+        turn_plane(0, "grad")
+        turn_plane(1, "grad")
         cast_x(1)
         quantize_x(1)
-        turn_plane(PACK - 1)
-        for c in range(CHUNKS):
-            prepare_factor(c)
         cast_x(2)
 
         pipeline = (
-            (multiply_gradient, -3),
             (scale_scores, 0),
-            (square_residual, -1),
+            (quantize_h, -3),
             (multiply_scores, 1),
-            (turn_targets, 1),
-            (form_h, -2),
-            (exponentiate, -1),
-            (turn_scores, 0),
-            (scale_residual, -1),
+            (multiply_gradient, -3),
+            (form_g, -1),
+            (turn_g, -1),
+            (subtract_targets, 0),
+            (square_residual, 0),
+            (exponentiate, 0),
             (store_gradient, -3),
-            (quantize_h, -2),
+            (form_h, -2),
             (quantize_x, 2),
             (cast_x, 3),
         )
@@ -284,3 +262,10 @@ def tile_attend_gwel_x_ts_kernel(tc, xT, wT, y, wt, ts, offs, out):
             for stage, shift in pipeline:
                 if 0 <= step + shift < CHUNKS:
                     stage(step + shift)
+            if step == 0:
+                turn_plane(2, "score")
+                turn_plane(3, "score")
+            if step == 2:
+                nc.vector.quantize_mx(
+                    out=wi_codes[:].bitcast(E4M3X4), scales=wi_scales[:], in_=w_i[:].rearrange("s f j -> s (f j)")
+                )

@@ -23,6 +23,7 @@ RUN = ITEMS // P
 ADD = mybir.AluOpType.add
 IS_EQUAL = mybir.AluOpType.is_equal
 QUAD = 32
+LAST = CHUNKS - 1
 SUBTRACT = mybir.AluOpType.subtract
 ROW_LOADS = ((0, 2), (2, 2), (4, 2), (6, 2))
 
@@ -49,7 +50,7 @@ def tile_attend_gwel_x_ts_kernel(tc, xT, wT, y, wt, ts, offs, out):
         w_planes = wT.rearrange("(p t) n -> t p n", t=PACK)
         w_window = []
         for t in range(PACK):
-            plane = keep.tile([P, ITEMS], F32, name="w_window%d" % t, tag="w_slot%d" % t)
+            plane = keep.tile([P, ITEMS], F32, name="w_window%d" % t)
             nc.sync.dma_start(out=plane[:], in_=w_planes[t])
             w_window.append(plane)
 
@@ -95,10 +96,7 @@ def tile_attend_gwel_x_ts_kernel(tc, xT, wT, y, wt, ts, offs, out):
             for k in range(PACK):
                 col = PACK * b + k
                 nc.tensor.transpose(spread[:, k, :], ts_runs[:, col : col + 1].to_broadcast([P, P]), ident[:])
-            if b % 2 == 0:
-                nc.scalar.activation(out=ts_lines[:, :, b, :], in_=spread[:].rearrange("p k n -> p n k"), func=ACT.Copy)
-            else:
-                nc.vector.tensor_copy(out=ts_lines[:, :, b, :], in_=spread[:].rearrange("p k n -> p n k"))
+            nc.vector.tensor_copy(out=ts_lines[:, :, b, :], in_=spread[:].rearrange("p k n -> p n k"))
         ts_col = keep.tile([P, PACK], F32, name="ts_col")
 
 
@@ -114,11 +112,11 @@ def tile_attend_gwel_x_ts_kernel(tc, xT, wT, y, wt, ts, offs, out):
         def gather_plane(t):
             nc.vector.tensor_copy(out=w_listed[t // 2][:, t % 2, :], in_=w_window[t][:].indirect(offsets[:]))
 
-        def weave_pair(u):
-            nc.vector.tensor_copy(out=w_d[:, :, 2 * u : 2 * u + 2], in_=w_listed[u][:].rearrange("p e i -> p i e"))
+        def weave_pair(u, copy):
+            copy(out=w_d[:, :, 2 * u : 2 * u + 2], in_=w_listed[u][:].rearrange("p e i -> p i e"))
 
-        def turn_plane(t, bank):
-            turned = psum.tile([P, PACK, P], BF16, name="turned", tag=bank, bufs=2)
+        def turn_plane(t, bank, bufs):
+            turned = psum.tile([P, PACK, P], BF16, name="turned", tag=bank, bufs=bufs)
             for j in range(PACK):
                 nc.tensor.transpose(turned[:, j, :], w_listed[t // 2][:, t % 2, j::PACK], ident_bf[:])
             cols = slice(t * P, (t + 1) * P)
@@ -145,7 +143,7 @@ def tile_attend_gwel_x_ts_kernel(tc, xT, wT, y, wt, ts, offs, out):
         score, scaled, resid, square, bell, g, g_turned, h, h_codes, h_scales, grad = ({} for i in range(11))
 
         def multiply_scores(c):
-            score[c] = psum.tile([P, SLOTS], F32, name="score", tag="score", bufs=2)
+            score[c] = psum.tile([P, SLOTS], F32, name="score", tag="grad" if c < 2 else "score", bufs=2)
             nc.tensor.matmul_mx(
                 out=score[c][:],
                 lhsT=x_codes[c][:].bitcast(E4M3X4),
@@ -174,14 +172,16 @@ def tile_attend_gwel_x_ts_kernel(tc, xT, wT, y, wt, ts, offs, out):
 
         def form_g(c):
             g[c] = work.tile([P, SLOTS], F32, name="g")
+            places = g[c][:].rearrange("r (j s) -> r s j", j=PACK) if c == LAST else g[c][:]
             nc.vector.scalar_tensor_tensor(
-                out=g[c][:], in0=resid[c][:], scalar=wt_col[:, c : c + 1], in1=bell[c][:], op0=MULT, op1=MULT
+                out=places, in0=resid[c][:], scalar=wt_col[:, c : c + 1], in1=bell[c][:], op0=MULT, op1=MULT
             )
 
         def turn_g(c):
             g_turned[c] = psum.tile([P, PACK, P], F32, name="g_turned", tag="turn", bufs=4)
             for j in range(PACK):
-                nc.tensor.transpose(g_turned[c][:, j, :], g[c][:, j::PACK], ident[:])
+                columns = g[c][:, j * P : (j + 1) * P] if c == LAST else g[c][:, j::PACK]
+                nc.tensor.transpose(g_turned[c][:, j, :], columns, ident[:])
 
         def form_h(c):
             h[c] = work.tile([P, P, PACK], BF16, name="h", align_bytes=64)
@@ -219,26 +219,28 @@ def tile_attend_gwel_x_ts_kernel(tc, xT, wT, y, wt, ts, offs, out):
             )
             nc.sync.dma_start(out=out[0, c * P : (c + 1) * P, :], in_=result[:])
 
-        gather_plane(0)
-        ts_listed = keep.tile([P, SLOTS], F32, name="ts_listed", tag="w_slot0")
+        w_window_bf = keep.tile([P, ITEMS], BF16, name="w_window_bf")
+        nc.scalar.activation(out=w_window_bf[:], in_=w_window[0][:], func=ACT.Copy)
+        nc.scalar.activation(out=w_listed[0][:, 0, :], in_=w_window_bf[:].indirect(offsets[:]), func=ACT.Copy)
+        ts_listed = keep.tile([P, SLOTS], F32, name="ts_listed")
         nc.vector.tensor_copy(out=ts_listed[:], in_=ts_window[:].indirect(offsets[:]))
-        ts_ps = psum.tile([P, PACK, P], F32, name="ts_ps", tag="grad", bufs=2)
+        ts_ps = psum.tile([P, PACK, P], F32, name="ts_ps", tag="turn", bufs=4)
         for j in range(PACK):
             nc.tensor.transpose(ts_ps[:, j, :], ts_listed[:, j::PACK], ident[:])
         nc.scalar.copy(out=ts_col[:], in_=ts_ps[:, :, 0])
         gather_plane(1)
         gather_plane(2)
         gather_plane(3)
-        weave_pair(0)
-        weave_pair(1)
+        weave_pair(0, nc.scalar.copy)
+        weave_pair(1, nc.vector.tensor_copy)
         cast_x(0)
         quantize_x(0)
         nc.vector.quantize_mx(
             out=wd_codes[:].bitcast(E4M3X4), scales=wd_scales[:], in_=w_d[:].rearrange("p i t -> p (i t)")
         )
         multiply_scores(0)
-        turn_plane(0, "grad")
-        turn_plane(1, "grad")
+        turn_plane(0, "turn", 4)
+        turn_plane(1, "turn", 4)
         cast_x(1)
         quantize_x(1)
         cast_x(2)
@@ -246,16 +248,16 @@ def tile_attend_gwel_x_ts_kernel(tc, xT, wT, y, wt, ts, offs, out):
         pipeline = (
             (scale_scores, 0),
             (quantize_h, -3),
+            (quantize_x, 2),
             (multiply_scores, 1),
             (multiply_gradient, -3),
-            (form_g, -1),
-            (turn_g, -1),
             (subtract_targets, 0),
             (square_residual, 0),
             (exponentiate, 0),
+            (form_g, -1),
+            (turn_g, -1),
             (store_gradient, -3),
             (form_h, -2),
-            (quantize_x, 2),
             (cast_x, 3),
         )
         for step in range(CHUNKS + 3):
@@ -263,8 +265,9 @@ def tile_attend_gwel_x_ts_kernel(tc, xT, wT, y, wt, ts, offs, out):
                 if 0 <= step + shift < CHUNKS:
                     stage(step + shift)
             if step == 0:
-                turn_plane(2, "score")
-                turn_plane(3, "score")
+                turn_plane(2, "grad", 2)
+            if step == 1:
+                turn_plane(3, "grad", 2)
             if step == 2:
                 nc.vector.quantize_mx(
                     out=wi_codes[:].bitcast(E4M3X4), scales=wi_scales[:], in_=w_i[:].rearrange("s f j -> s (f j)")

@@ -11,6 +11,8 @@ E4M3X4 = mybir.dt.float8_e4m3fn_x4
 E5M2X4 = mybir.dt.float8_e5m2_x4
 ACT = mybir.ActivationFunctionType
 MULT = mybir.AluOpType.mult
+ADD = mybir.AluOpType.add
+IS_EQUAL = mybir.AluOpType.is_equal
 
 P = 128
 PACK = 4
@@ -19,13 +21,8 @@ ITEMS = 2048
 FEATS = 512
 ROWS = 1024
 CHUNKS = ROWS // P
-RUN = ITEMS // P
-ADD = mybir.AluOpType.add
-IS_EQUAL = mybir.AluOpType.is_equal
 QUAD = 32
-LAST = CHUNKS - 1
-SUBTRACT = mybir.AluOpType.subtract
-ROW_LOADS = ((0, 2), (2, 2), (4, 2), (6, 2))
+EARLY = 6
 
 FLOPS = 2 * 2 * ROWS * SLOTS * FEATS
 BYTES = 4 * (FEATS * ROWS + FEATS * ITEMS + ROWS * SLOTS + ROWS + ITEMS + ROWS * FEATS) + 2 * P * SLOTS // 16
@@ -40,40 +37,12 @@ def tile_attend_gwel_x_ts_kernel(tc, xT, wT, y, wt, ts, offs, out):
 
         offsets = keep.tile([P, SLOTS // 16], U16, name="offsets")
         nc.sync.dma_start(offsets[:], offs)
-
-        ts_runs = keep.tile([P, RUN], F32, name="ts_runs")
-        nc.sync.dma_start(out=ts_runs[:], in_=ts[0].rearrange("(n k) -> n k", k=RUN))
-        wt_col = keep.tile([P, CHUNKS], F32, name="wt_col")
-        with nc.allow_non_contiguous_dma(reason="one weight a partition and chunk"):
-            nc.scalar.dma_start(out=wt_col[:], in_=wt[0].rearrange("(c p) o -> p (c o)", p=P))
-
-        w_planes = wT.rearrange("(p t) n -> t p n", t=PACK)
-        w_window = []
-        for t in range(PACK):
-            plane = keep.tile([P, ITEMS], F32, name="w_window%d" % t)
-            nc.sync.dma_start(out=plane[:], in_=w_planes[t])
-            w_window.append(plane)
-
-        x_view = xT[0].rearrange("(p t) r -> p t r", t=PACK)
-        y_view = y[0].rearrange("(c p) n -> p c n", p=P)
-        x_raw = {}
-        y_sb = {}
-
-        def load_x(first, count):
-            raw = keep.tile([P, PACK, count * P], F32, name="x_raw%d" % first)
-            nc.sync.dma_start(out=raw[:], in_=x_view[:, :, first * P : (first + count) * P])
-            for c in range(first, first + count):
-                x_raw[c] = raw[:, :, (c - first) * P : (c - first + 1) * P]
-
-        def load_y(first, count):
-            raw = keep.tile([P, count, SLOTS], F32, name="y_raw%d" % first)
-            nc.sync.dma_start(out=raw[:], in_=y_view[:, first : first + count, :])
-            for c in range(first, first + count):
-                y_sb[c] = raw[:, c - first, :]
-
-        for first, count in ROW_LOADS:
-            load_x(first, count)
-            load_y(first, count)
+        ts_row = keep.tile([1, ITEMS], F32, name="ts_row")
+        nc.sync.dma_start(out=ts_row[:], in_=ts[0:1, :])
+        wt_runs = keep.tile([P, CHUNKS], F32, name="wt_runs")
+        nc.sync.dma_start(out=wt_runs[:], in_=wt[0].rearrange("(p k) o -> p (k o)", k=CHUNKS))
+        ts_window = keep.tile([P, ITEMS], F32, name="ts_window", tag="stage1", align_bytes=64)
+        nc.gpsimd.memset(ts_window[:], 0.0)
 
         ones = keep.tile([P, QUAD], F32, name="ones")
         nc.vector.memset(ones[:], 1.0)
@@ -87,47 +56,95 @@ def tile_attend_gwel_x_ts_kernel(tc, xT, wT, y, wt, ts, offs, out):
             band = slice(q * QUAD, (q + 1) * QUAD)
             nc.vector.tensor_tensor(out=ident[band, band], in0=column[band, :], in1=row[band, :], op=IS_EQUAL)
         ident_bf = keep.tile([P, P], BF16, name="ident_bf")
-        nc.vector.tensor_copy(out=ident_bf[:], in_=ident[:])
+        nc.scalar.copy(out=ident_bf[:], in_=ident[:])
+        nc.vector.tensor_copy(out=ts_window[0:1, :], in_=ts_row[:])
 
-        ts_window = keep.tile([P, ITEMS], F32, name="ts_window")
-        ts_lines = ts_window[:].rearrange("p (n b k) -> p n b k", b=RUN // PACK, k=PACK)
-        for b in range(RUN // PACK):
-            spread = psum.tile([P, PACK, P], F32, name="spread", tag="turn", bufs=4)
+
+        w_planes = wT.rearrange("(p t) n -> t p n", t=PACK)
+        w_window = []
+        for t in range(PACK):
+            plane = keep.tile([P, ITEMS], F32, name="w_window%d" % t, tag="plane%d" % t, align_bytes=64)
+            nc.sync.dma_start(out=plane[:], in_=w_planes[t])
+            w_window.append(plane)
+
+        x_view = xT[0].rearrange("(p t) r -> p t r", t=PACK)
+        y_view = y[0].rearrange("(c p) n -> p c n", p=P)
+        x_raw = {}
+        y_raw = {}
+
+        def load_x(first, count, tag):
+            raw = keep.tile([P, PACK, count * P], F32, name="x_raw", tag=tag, align_bytes=64)
+            nc.sync.dma_start(out=raw[:], in_=x_view[:, :, first * P : (first + count) * P])
+            for c in range(first, first + count):
+                x_raw[c] = raw[:, :, (c - first) * P : (c - first + 1) * P]
+
+        def load_y(first, count, tag):
+            raw = keep.tile([P, count, SLOTS], F32, name="y_raw", tag=tag, align_bytes=64)
+            nc.sync.dma_start(out=raw[:], in_=y_view[:, first : first + count, :])
+            for c in range(first, first + count):
+                y_raw[c] = raw[:, c - first, :]
+
+
+        for first in range(0, CHUNKS, 2):
+            load_x(first, 2, "x_rows%d" % first)
+            load_y(first, 2, "y_rows%d" % first)
+
+        wt_early = keep.tile([P, EARLY * P], F32, name="wt_early", tag="stage3")
+        wt_late = keep.tile([P, (CHUNKS - EARLY) * P], F32, name="wt_late")
+        cut = EARLY * P // CHUNKS
+        for b in range(CHUNKS // PACK):
+            spread = psum.tile([P, PACK, P], F32, name="spread", tag="resid", bufs=4)
             for k in range(PACK):
                 col = PACK * b + k
-                nc.tensor.transpose(spread[:, k, :], ts_runs[:, col : col + 1].to_broadcast([P, P]), ident[:])
-            nc.vector.tensor_copy(out=ts_lines[:, :, b, :], in_=spread[:].rearrange("p k n -> p n k"))
-        ts_col = keep.tile([P, PACK], F32, name="ts_col")
+                nc.tensor.transpose(spread[:, k, :], wt_runs[:, col : col + 1].to_broadcast([P, P]), ident[:])
+            for part, runs in ((wt_early, slice(0, cut)), (wt_late, slice(cut, P))):
+                lines = part[:].rearrange("s (p b k) -> s p b k", b=CHUNKS // PACK, k=PACK)
+                nc.scalar.copy(out=lines[:, :, b, :], in_=spread[:, :, runs].rearrange("s k p -> s p k"))
 
+        ts_listed = keep.tile([P, SLOTS], F32, name="ts_listed")
+        nc.vector.tensor_copy(out=ts_listed[:], in_=ts_window[:].indirect(offsets[:]))
+        ts_turned = psum.tile([P, PACK, P], F32, name="ts_turned", tag="resid", bufs=4)
+        for j in range(PACK):
+            nc.tensor.transpose(ts_turned[:, j, :], ts_listed[:, j::PACK], ident[:])
 
         w_d = keep.tile([P, SLOTS, PACK], BF16, name="w_d", align_bytes=64)
-        w_i = keep.tile([P, FEATS, PACK], BF16, name="w_i", align_bytes=64)
-        wi_codes = keep.tile([P, FEATS], U32, name="wi_codes", align_bytes=64)
         wi_scales = keep.tile([P, FEATS], U8, name="wi_scales", align_bytes=64)
-        wd_codes = keep.tile([P, SLOTS], U32, name="wd_codes", align_bytes=64)
         wd_scales = keep.tile([P, SLOTS], U8, name="wd_scales", align_bytes=64)
+        w_pair = {0: keep.tile([P, 2, SLOTS], BF16, name="w_pair0", tag="stage1", align_bytes=64)}
 
-        w_listed = [keep.tile([P, 2, SLOTS], BF16, name="w_listed%d" % u) for u in range(2)]
+        def dealt(t):
+            return w_pair[t // 2][:, t % 2, :].rearrange("p (j s) -> p s j", j=PACK)
 
         def gather_plane(t):
-            nc.vector.tensor_copy(out=w_listed[t // 2][:, t % 2, :], in_=w_window[t][:].indirect(offsets[:]))
+            nc.vector.tensor_copy(out=dealt(t), in_=w_window[t][:].indirect(offsets[:]))
 
         def weave_pair(u, copy):
-            copy(out=w_d[:, :, 2 * u : 2 * u + 2], in_=w_listed[u][:].rearrange("p e i -> p i e"))
+            copy(out=w_d[:, :, 2 * u : 2 * u + 2], in_=w_pair[u][:].rearrange("p e i -> p i e"))
 
         def turn_plane(t, bank, bufs):
             turned = psum.tile([P, PACK, P], BF16, name="turned", tag=bank, bufs=bufs)
             for j in range(PACK):
-                nc.tensor.transpose(turned[:, j, :], w_listed[t // 2][:, t % 2, j::PACK], ident_bf[:])
-            cols = slice(t * P, (t + 1) * P)
-            nc.scalar.copy(out=w_i[:, cols, :], in_=turned[:].rearrange("s j p -> s p j"))
+                nc.tensor.transpose(turned[:, j, :], w_pair[t // 2][:, t % 2, j * P : (j + 1) * P], ident_bf[:])
+            nc.scalar.copy(out=w_i[:, t * P : (t + 1) * P, :], in_=turned[:].rearrange("s j p -> s p j"))
 
-        x_bf = {}
-        x_codes = {}
-        x_scales = {}
+        x_bf, x_codes, x_scales, factor, y_dealt = ({} for i in range(5))
+        score, scaled, resid, square, bell, weighted, h, h_codes, h_scales, grad = ({} for i in range(10))
+
+        def form_factor(c):
+            factor[c] = keep.tile([P, P, PACK], F32, name="factor", tag="factor%d" % c if c < EARLY else "pass%d" % (c - EARLY))
+            weights = wt_early[:, c * P : (c + 1) * P] if c < EARLY else wt_late[:, (c - EARLY) * P : (c - EARLY + 1) * P]
+            nc.vector.tensor_tensor(
+                out=factor[c][:],
+                in0=weights.unsqueeze(2).to_broadcast([P, P, PACK]),
+                in1=nts_col[:].unsqueeze(1).to_broadcast([P, P, PACK]),
+                op=MULT,
+            )
 
         def cast_x(c):
-            x_bf[c] = work.tile([P, P, PACK], BF16, name="x_bf", align_bytes=64)
+            if c == 0:
+                x_bf[c] = keep.tile([P, P, PACK], BF16, name="x_bf_first", tag="first_rows", align_bytes=64)
+            else:
+                x_bf[c] = work.tile([P, P, PACK], BF16, name="x_bf", align_bytes=64, bufs=2)
             nc.scalar.copy(
                 out=x_bf[c][:].rearrange("p (a i) t -> p a t i", i=4),
                 in_=x_raw[c].rearrange("p t (a i) -> p a t i", i=4),
@@ -140,10 +157,15 @@ def tile_attend_gwel_x_ts_kernel(tc, xT, wT, y, wt, ts, offs, out):
                 out=x_codes[c][:].bitcast(E4M3X4), scales=x_scales[c][:], in_=x_bf[c][:].rearrange("p r t -> p (r t)")
             )
 
-        score, scaled, resid, square, bell, g, g_turned, h, h_codes, h_scales, grad = ({} for i in range(11))
+        def deal_targets(c):
+            y_dealt[c] = work.tile([P, SLOTS], F32, name="y_dealt", bufs=2)
+            nc.vector.tensor_copy(
+                out=y_dealt[c][:].rearrange("r (j s) -> r s j", j=PACK),
+                in_=y_raw[c].rearrange("r (s j) -> r s j", j=PACK),
+            )
 
         def multiply_scores(c):
-            score[c] = psum.tile([P, SLOTS], F32, name="score", tag="grad" if c < 2 else "score", bufs=2)
+            score[c] = psum.tile([P, SLOTS], F32, name="score", tag="score", bufs=2)
             nc.tensor.matmul_mx(
                 out=score[c][:],
                 lhsT=x_codes[c][:].bitcast(E4M3X4),
@@ -155,42 +177,41 @@ def tile_attend_gwel_x_ts_kernel(tc, xT, wT, y, wt, ts, offs, out):
             )
 
         def scale_scores(c):
-            scaled[c] = work.tile([P, SLOTS], F32, name="scaled")
-            nc.vector.tensor_tensor(out=scaled[c][:], in0=score[c][:], in1=ts_listed[:], op=MULT)
+            scaled[c] = keep.tile([P, SLOTS], F32, name="scaled", tag="pass%d" % c)
+            nc.vector.tensor_tensor(out=scaled[c][:], in0=score[c][:], in1=nts_row[:], op=MULT)
 
-        def subtract_targets(c):
-            resid[c] = work.tile([P, SLOTS], F32, name="resid")
-            nc.vector.tensor_tensor(out=resid[c][:], in0=scaled[c][:], in1=y_sb[c], op=SUBTRACT)
+        def turn_targets(c):
+            resid[c] = psum.tile([P, PACK, P], F32, name="resid", tag="resid", bufs=4)
+            for j in range(PACK):
+                nc.tensor.matmul(
+                    resid[c][:, j, :], y_dealt[c][:, j * P : (j + 1) * P], ident[:],
+                    start=(j == 0), stop=False, is_transpose=True,
+                )
+
+        def turn_scores(c):
+            for j in range(PACK):
+                nc.tensor.matmul(
+                    resid[c][:, j, :], scaled[c][:, j * P : (j + 1) * P], ident[:],
+                    start=False, stop=(j == PACK - 1), is_transpose=True,
+                )
 
         def square_residual(c):
-            square[c] = work.tile([P, SLOTS], F32, name="square")
-            nc.scalar.activation(out=square[c][:], in_=resid[c][:], func=ACT.Square)
+            square[c] = work.tile([P, P, PACK], F32, name="square")
+            nc.scalar.activation(out=square[c][:], in_=resid[c][:].rearrange("s j r -> s r j"), func=ACT.Square)
 
         def exponentiate(c):
-            bell[c] = work.tile([P, SLOTS], F32, name="bell")
+            bell[c] = work.tile([P, P, PACK], F32, name="bell")
             nc.scalar.activation(out=bell[c][:], in_=square[c][:], func=ACT.Exp, scale=-0.5)
 
-        def form_g(c):
-            g[c] = work.tile([P, SLOTS], F32, name="g")
-            places = g[c][:].rearrange("r (j s) -> r s j", j=PACK) if c == LAST else g[c][:]
-            nc.vector.scalar_tensor_tensor(
-                out=places, in0=resid[c][:], scalar=wt_col[:, c : c + 1], in1=bell[c][:], op0=MULT, op1=MULT
+        def weigh_residual(c):
+            weighted[c] = work.tile([P, P, PACK], F32, name="weighted")
+            nc.vector.tensor_tensor(
+                out=weighted[c][:], in0=resid[c][:].rearrange("s j r -> s r j"), in1=factor[c][:], op=MULT
             )
-
-        def turn_g(c):
-            g_turned[c] = psum.tile([P, PACK, P], F32, name="g_turned", tag="turn", bufs=4)
-            for j in range(PACK):
-                columns = g[c][:, j * P : (j + 1) * P] if c == LAST else g[c][:, j::PACK]
-                nc.tensor.transpose(g_turned[c][:, j, :], columns, ident[:])
 
         def form_h(c):
             h[c] = work.tile([P, P, PACK], BF16, name="h", align_bytes=64)
-            nc.vector.tensor_tensor(
-                out=h[c][:],
-                in0=g_turned[c][:].rearrange("s j r -> s r j"),
-                in1=ts_col[:].unsqueeze(1).to_broadcast([P, P, PACK]),
-                op=MULT,
-            )
+            nc.vector.tensor_tensor(out=h[c][:], in0=weighted[c][:], in1=bell[c][:], op=MULT)
 
         def quantize_h(c):
             h_codes[c] = work.tile([P, P], U32, name="h_codes", align_bytes=64)
@@ -219,46 +240,56 @@ def tile_attend_gwel_x_ts_kernel(tc, xT, wT, y, wt, ts, offs, out):
             )
             nc.sync.dma_start(out=out[0, c * P : (c + 1) * P, :], in_=result[:])
 
-        w_window_bf = keep.tile([P, ITEMS], BF16, name="w_window_bf")
-        nc.scalar.activation(out=w_window_bf[:], in_=w_window[0][:], func=ACT.Copy)
-        nc.scalar.activation(out=w_listed[0][:, 0, :], in_=w_window_bf[:].indirect(offsets[:]), func=ACT.Copy)
-        ts_listed = keep.tile([P, SLOTS], F32, name="ts_listed")
-        nc.vector.tensor_copy(out=ts_listed[:], in_=ts_window[:].indirect(offsets[:]))
-        ts_ps = psum.tile([P, PACK, P], F32, name="ts_ps", tag="turn", bufs=4)
-        for j in range(PACK):
-            nc.tensor.transpose(ts_ps[:, j, :], ts_listed[:, j::PACK], ident[:])
-        nc.scalar.copy(out=ts_col[:], in_=ts_ps[:, :, 0])
-        gather_plane(1)
+        gather_plane(0)
+        nts_col = keep.tile([P, PACK], F32, name="nts_col", tag="plane0", align_bytes=64)
+        nc.vector.tensor_scalar(out=nts_col[:], in0=ts_turned[:, :, 0], scalar1=-1.0, scalar2=None, op0=MULT)
+        w_window_bf = keep.tile([P, ITEMS], BF16, name="w_window_bf", tag="plane_bf")
+        nc.scalar.activation(out=w_window_bf[:], in_=w_window[1][:], func=ACT.Copy)
+        nc.scalar.activation(out=dealt(1), in_=w_window_bf[:].indirect(offsets[:]), func=ACT.Copy)
+        for c in range(EARLY):
+            form_factor(c)
+        w_pair[1] = keep.tile([P, 2, SLOTS], BF16, name="w_pair1", tag="stage3")
         gather_plane(2)
         gather_plane(3)
         weave_pair(0, nc.scalar.copy)
+        ts_spread = psum.tile([P, PACK, P], F32, name="ts_spread", tag="resid", bufs=4)
+        for j in range(PACK):
+            nc.tensor.transpose(ts_spread[:, j, :], nts_col[:, j : j + 1].to_broadcast([P, P]), ident[:])
+        nts_row = keep.tile([P, SLOTS], F32, name="nts_row", tag="plane_bf")
+        nc.scalar.copy(out=nts_row[:], in_=ts_spread[:].rearrange("r j s -> r (j s)"))
         weave_pair(1, nc.vector.tensor_copy)
         cast_x(0)
         quantize_x(0)
+        wd_codes = keep.tile([P, SLOTS], U32, name="wd_codes", tag="first_rows", align_bytes=64)
         nc.vector.quantize_mx(
             out=wd_codes[:].bitcast(E4M3X4), scales=wd_scales[:], in_=w_d[:].rearrange("p i t -> p (i t)")
         )
         multiply_scores(0)
-        turn_plane(0, "turn", 4)
-        turn_plane(1, "turn", 4)
+        deal_targets(0)
+        turn_targets(0)
         cast_x(1)
         quantize_x(1)
+        w_i = keep.tile([P, FEATS, PACK], BF16, name="w_i", tag="x_rows0", align_bytes=64)
+        turn_plane(0, "grad", 2)
+        turn_plane(1, "grad", 2)
         cast_x(2)
 
         pipeline = (
             (scale_scores, 0),
             (quantize_h, -3),
-            (quantize_x, 2),
             (multiply_scores, 1),
             (multiply_gradient, -3),
-            (subtract_targets, 0),
+            (turn_scores, 0),
             (square_residual, 0),
             (exponentiate, 0),
-            (form_g, -1),
-            (turn_g, -1),
-            (store_gradient, -3),
+            (deal_targets, 1),
+            (turn_targets, 1),
+            (weigh_residual, -1),
+            (quantize_x, 2),
             (form_h, -2),
+            (store_gradient, -3),
             (cast_x, 3),
+            (form_factor, EARLY),
         )
         for step in range(CHUNKS + 3):
             for stage, shift in pipeline:
@@ -266,9 +297,9 @@ def tile_attend_gwel_x_ts_kernel(tc, xT, wT, y, wt, ts, offs, out):
                     stage(step + shift)
             if step == 0:
                 turn_plane(2, "grad", 2)
-            if step == 1:
                 turn_plane(3, "grad", 2)
-            if step == 2:
+            if step == 1:
+                wi_codes = keep.tile([P, FEATS], U32, name="wi_codes", tag="y_rows0", align_bytes=64)
                 nc.vector.quantize_mx(
                     out=wi_codes[:].bitcast(E4M3X4), scales=wi_scales[:], in_=w_i[:].rearrange("s f j -> s (f j)")
                 )

@@ -22,7 +22,7 @@ FEATS = 512
 ROWS = 1024
 CHUNKS = ROWS // P
 QUAD = 32
-EARLY = 6
+LAG = 3
 
 FLOPS = 2 * 2 * ROWS * SLOTS * FEATS
 BYTES = 4 * (FEATS * ROWS + FEATS * ITEMS + ROWS * SLOTS + ROWS + ITEMS + ROWS * FEATS) + 2 * P * SLOTS // 16
@@ -89,62 +89,66 @@ def tile_attend_gwel_x_ts_kernel(tc, xT, wT, y, wt, ts, offs, out):
             load_x(first, 2, "x_rows%d" % first)
             load_y(first, 2, "y_rows%d" % first)
 
-        wt_early = keep.tile([P, EARLY * P], F32, name="wt_early", tag="stage3")
-        wt_late = keep.tile([P, (CHUNKS - EARLY) * P], F32, name="wt_late")
-        cut = EARLY * P // CHUNKS
+        wt_row = keep.tile([P, ROWS], F32, name="wt_row")
+        wt_lines = wt_row[:].rearrange("s (p b k) -> s p b k", b=CHUNKS // PACK, k=PACK)
         for b in range(CHUNKS // PACK):
             spread = psum.tile([P, PACK, P], F32, name="spread", tag="resid", bufs=4)
             for k in range(PACK):
                 col = PACK * b + k
                 nc.tensor.transpose(spread[:, k, :], wt_runs[:, col : col + 1].to_broadcast([P, P]), ident[:])
-            for part, runs in ((wt_early, slice(0, cut)), (wt_late, slice(cut, P))):
-                lines = part[:].rearrange("s (p b k) -> s p b k", b=CHUNKS // PACK, k=PACK)
-                nc.scalar.copy(out=lines[:, :, b, :], in_=spread[:, :, runs].rearrange("s k p -> s p k"))
+            nc.scalar.copy(out=wt_lines[:, :, b, :], in_=spread[:].rearrange("s k p -> s p k"))
 
         ts_listed = keep.tile([P, SLOTS], F32, name="ts_listed")
         nc.vector.tensor_copy(out=ts_listed[:], in_=ts_window[:].indirect(offsets[:]))
         ts_turned = psum.tile([P, PACK, P], F32, name="ts_turned", tag="resid", bufs=4)
         for j in range(PACK):
             nc.tensor.transpose(ts_turned[:, j, :], ts_listed[:, j::PACK], ident[:])
+        nts_col = keep.tile([P, PACK], F32, name="nts_col")
+        nc.scalar.activation(out=nts_col[:], in_=ts_turned[:, :, 0], func=ACT.Copy, scale=-1.0)
+        factor = keep.tile([P, PACK, ROWS], F32, name="factor")
+        for j in range(PACK):
+            nc.scalar.activation(out=factor[:, j, :], in_=wt_row[:], func=ACT.Copy, scale=nts_col[:, j : j + 1])
+        ts_spread = psum.tile([P, PACK, P], F32, name="ts_spread", tag="resid", bufs=4)
+        for j in range(PACK):
+            nc.tensor.transpose(ts_spread[:, j, :], nts_col[:, j : j + 1].to_broadcast([P, P]), ident[:])
+        nts_row = keep.tile([P, SLOTS], F32, name="nts_row")
+        nc.scalar.copy(out=nts_row[:], in_=ts_spread[:].rearrange("r j s -> r (j s)"))
 
         w_d = keep.tile([P, SLOTS, PACK], BF16, name="w_d", align_bytes=64)
         wi_scales = keep.tile([P, FEATS], U8, name="wi_scales", align_bytes=64)
         wd_scales = keep.tile([P, SLOTS], U8, name="wd_scales", align_bytes=64)
-        w_pair = {0: keep.tile([P, 2, SLOTS], BF16, name="w_pair0", tag="stage1", align_bytes=64)}
-
-        def dealt(t):
-            return w_pair[t // 2][:, t % 2, :].rearrange("p (j s) -> p s j", j=PACK)
+        w_pair = [
+            keep.tile([P, 2, SLOTS], BF16, name="w_pair0", tag="stage1", align_bytes=64),
+            keep.tile([P, 2, SLOTS], BF16, name="w_pair1"),
+        ]
 
         def gather_plane(t):
-            nc.vector.tensor_copy(out=dealt(t), in_=w_window[t][:].indirect(offsets[:]))
+            nc.vector.tensor_copy(out=w_pair[t // 2][:, t % 2, :], in_=w_window[t][:].indirect(offsets[:]))
 
-        def weave_pair(u, copy):
-            copy(out=w_d[:, :, 2 * u : 2 * u + 2], in_=w_pair[u][:].rearrange("p e i -> p i e"))
-
-        def turn_plane(t, bank, bufs):
-            turned = psum.tile([P, PACK, P], BF16, name="turned", tag=bank, bufs=bufs)
-            for j in range(PACK):
-                nc.tensor.transpose(turned[:, j, :], w_pair[t // 2][:, t % 2, j * P : (j + 1) * P], ident_bf[:])
-            nc.scalar.copy(out=w_i[:, t * P : (t + 1) * P, :], in_=turned[:].rearrange("s j p -> s p j"))
-
-        x_bf, x_codes, x_scales, factor, y_dealt = ({} for i in range(5))
-        score, scaled, resid, square, bell, weighted, h, h_codes, h_scales, grad = ({} for i in range(10))
-
-        def form_factor(c):
-            factor[c] = keep.tile([P, P, PACK], F32, name="factor", tag="factor%d" % c if c < EARLY else "pass%d" % (c - EARLY))
-            weights = wt_early[:, c * P : (c + 1) * P] if c < EARLY else wt_late[:, (c - EARLY) * P : (c - EARLY + 1) * P]
-            nc.vector.tensor_tensor(
-                out=factor[c][:],
-                in0=weights.unsqueeze(2).to_broadcast([P, P, PACK]),
-                in1=nts_col[:].unsqueeze(1).to_broadcast([P, P, PACK]),
-                op=MULT,
+        def weave_pair(u):
+            nc.vector.tensor_copy(
+                out=w_d[:, :, 2 * u : 2 * u + 2].rearrange("p (j s) e -> p j s e", j=PACK),
+                in_=w_pair[u][:].rearrange("p e (s j) -> p j s e", j=PACK),
             )
+
+        def turn_pair(u):
+            turned = psum.tile([P, 2, PACK, P], BF16, name="turned", tag="grad", bufs=2)
+            for e in range(2):
+                for j in range(PACK):
+                    columns = w_pair[0][:, e, j::PACK] if u == 0 else w_d[:, j * P : (j + 1) * P, 2 + e]
+                    nc.tensor.transpose(turned[:, e, j, :], columns, ident_bf[:])
+            nc.scalar.copy(
+                out=w_i[:, :, u, :].rearrange("s p (e j) -> s p e j", j=PACK), in_=turned[:].rearrange("s e j p -> s p e j")
+            )
+
+        x_bf, x_codes, x_scales, y_dealt = ({} for i in range(4))
+        score, scaled, resid, square, bell, weighted, h, h_codes, h_scales, grad = ({} for i in range(10))
 
         def cast_x(c):
             if c == 0:
                 x_bf[c] = keep.tile([P, P, PACK], BF16, name="x_bf_first", tag="first_rows", align_bytes=64)
             else:
-                x_bf[c] = work.tile([P, P, PACK], BF16, name="x_bf", align_bytes=64, bufs=2)
+                x_bf[c] = work.tile([P, P, PACK], BF16, name="x_bf", align_bytes=64, bufs=3)
             nc.scalar.copy(
                 out=x_bf[c][:].rearrange("p (a i) t -> p a t i", i=4),
                 in_=x_raw[c].rearrange("p t (a i) -> p a t i", i=4),
@@ -160,8 +164,8 @@ def tile_attend_gwel_x_ts_kernel(tc, xT, wT, y, wt, ts, offs, out):
         def deal_targets(c):
             y_dealt[c] = work.tile([P, SLOTS], F32, name="y_dealt", bufs=2)
             nc.vector.tensor_copy(
-                out=y_dealt[c][:].rearrange("r (j s) -> r s j", j=PACK),
-                in_=y_raw[c].rearrange("r (s j) -> r s j", j=PACK),
+                out=y_dealt[c][:].rearrange("r (j a i) -> r a j i", j=PACK, i=4),
+                in_=y_raw[c].rearrange("r (a i j) -> r a j i", j=PACK, i=4),
             )
 
         def multiply_scores(c):
@@ -177,7 +181,7 @@ def tile_attend_gwel_x_ts_kernel(tc, xT, wT, y, wt, ts, offs, out):
             )
 
         def scale_scores(c):
-            scaled[c] = keep.tile([P, SLOTS], F32, name="scaled", tag="pass%d" % c)
+            scaled[c] = work.tile([P, SLOTS], F32, name="scaled")
             nc.vector.tensor_tensor(out=scaled[c][:], in0=score[c][:], in1=nts_row[:], op=MULT)
 
         def turn_targets(c):
@@ -196,22 +200,27 @@ def tile_attend_gwel_x_ts_kernel(tc, xT, wT, y, wt, ts, offs, out):
                 )
 
         def square_residual(c):
-            square[c] = work.tile([P, P, PACK], F32, name="square")
-            nc.scalar.activation(out=square[c][:], in_=resid[c][:].rearrange("s j r -> s r j"), func=ACT.Square)
+            square[c] = work.tile([P, PACK, P], F32, name="square")
+            nc.scalar.activation(out=square[c][:], in_=resid[c][:], func=ACT.Square)
 
         def exponentiate(c):
-            bell[c] = work.tile([P, P, PACK], F32, name="bell")
+            bell[c] = work.tile([P, PACK, P], F32, name="bell", bufs=LAG + 2)
             nc.scalar.activation(out=bell[c][:], in_=square[c][:], func=ACT.Exp, scale=-0.5)
 
         def weigh_residual(c):
-            weighted[c] = work.tile([P, P, PACK], F32, name="weighted")
+            weighted[c] = work.tile([P, PACK, P], F32, name="weighted", bufs=LAG + 2)
             nc.vector.tensor_tensor(
-                out=weighted[c][:], in0=resid[c][:].rearrange("s j r -> s r j"), in1=factor[c][:], op=MULT
+                out=weighted[c][:], in0=resid[c][:], in1=factor[:, :, c * P : (c + 1) * P], op=MULT
             )
 
         def form_h(c):
             h[c] = work.tile([P, P, PACK], BF16, name="h", align_bytes=64)
-            nc.vector.tensor_tensor(out=h[c][:], in0=weighted[c][:], in1=bell[c][:], op=MULT)
+            nc.vector.tensor_tensor(
+                out=h[c][:].rearrange("s (a i) j -> s a j i", i=4),
+                in0=weighted[c][:].rearrange("s j (a i) -> s a j i", i=4),
+                in1=bell[c][:].rearrange("s j (a i) -> s a j i", i=4),
+                op=MULT,
+            )
 
         def quantize_h(c):
             h_codes[c] = work.tile([P, P], U32, name="h_codes", align_bytes=64)
@@ -234,30 +243,17 @@ def tile_attend_gwel_x_ts_kernel(tc, xT, wT, y, wt, ts, offs, out):
 
         def store_gradient(c):
             result = work.tile([P, FEATS], F32, name="result")
-            nc.scalar.copy(
-                out=result[:].rearrange("r (p t) -> r p t", t=PACK),
-                in_=grad[c][:].rearrange("r (t p) -> r p t", t=PACK),
-            )
+            nc.scalar.copy(out=result[:], in_=grad[c][:])
             nc.sync.dma_start(out=out[0, c * P : (c + 1) * P, :], in_=result[:])
 
+        w_i = keep.tile([P, P, 2, 2 * PACK], BF16, name="w_i", align_bytes=64)
         gather_plane(0)
-        nts_col = keep.tile([P, PACK], F32, name="nts_col", tag="plane0", align_bytes=64)
-        nc.vector.tensor_scalar(out=nts_col[:], in0=ts_turned[:, :, 0], scalar1=-1.0, scalar2=None, op0=MULT)
-        w_window_bf = keep.tile([P, ITEMS], BF16, name="w_window_bf", tag="plane_bf")
-        nc.scalar.activation(out=w_window_bf[:], in_=w_window[1][:], func=ACT.Copy)
-        nc.scalar.activation(out=dealt(1), in_=w_window_bf[:].indirect(offsets[:]), func=ACT.Copy)
-        for c in range(EARLY):
-            form_factor(c)
-        w_pair[1] = keep.tile([P, 2, SLOTS], BF16, name="w_pair1", tag="stage3")
+        gather_plane(1)
+        weave_pair(0)
+        turn_pair(0)
         gather_plane(2)
         gather_plane(3)
-        weave_pair(0, nc.scalar.copy)
-        ts_spread = psum.tile([P, PACK, P], F32, name="ts_spread", tag="resid", bufs=4)
-        for j in range(PACK):
-            nc.tensor.transpose(ts_spread[:, j, :], nts_col[:, j : j + 1].to_broadcast([P, P]), ident[:])
-        nts_row = keep.tile([P, SLOTS], F32, name="nts_row", tag="plane_bf")
-        nc.scalar.copy(out=nts_row[:], in_=ts_spread[:].rearrange("r j s -> r (j s)"))
-        weave_pair(1, nc.vector.tensor_copy)
+        weave_pair(1)
         cast_x(0)
         quantize_x(0)
         wd_codes = keep.tile([P, SLOTS], U32, name="wd_codes", tag="first_rows", align_bytes=64)
@@ -269,37 +265,32 @@ def tile_attend_gwel_x_ts_kernel(tc, xT, wT, y, wt, ts, offs, out):
         turn_targets(0)
         cast_x(1)
         quantize_x(1)
-        w_i = keep.tile([P, FEATS, PACK], BF16, name="w_i", tag="x_rows0", align_bytes=64)
-        turn_plane(0, "grad", 2)
-        turn_plane(1, "grad", 2)
         cast_x(2)
 
         pipeline = (
+            (cast_x, 3),
             (scale_scores, 0),
-            (quantize_h, -3),
+            (quantize_h, -LAG - 1),
             (multiply_scores, 1),
-            (multiply_gradient, -3),
+            (multiply_gradient, -LAG - 1),
             (turn_scores, 0),
             (square_residual, 0),
             (exponentiate, 0),
             (deal_targets, 1),
             (turn_targets, 1),
-            (weigh_residual, -1),
             (quantize_x, 2),
-            (form_h, -2),
-            (store_gradient, -3),
-            (cast_x, 3),
-            (form_factor, EARLY),
+            (form_h, -LAG),
+            (weigh_residual, -1),
+            (store_gradient, -LAG - 1),
         )
-        for step in range(CHUNKS + 3):
+        for step in range(CHUNKS + LAG + 1):
             for stage, shift in pipeline:
                 if 0 <= step + shift < CHUNKS:
                     stage(step + shift)
             if step == 0:
-                turn_plane(2, "grad", 2)
-                turn_plane(3, "grad", 2)
+                turn_pair(1)
             if step == 1:
                 wi_codes = keep.tile([P, FEATS], U32, name="wi_codes", tag="y_rows0", align_bytes=64)
                 nc.vector.quantize_mx(
-                    out=wi_codes[:].bitcast(E4M3X4), scales=wi_scales[:], in_=w_i[:].rearrange("s f j -> s (f j)")
+                    out=wi_codes[:].bitcast(E4M3X4), scales=wi_scales[:], in_=w_i[:].rearrange("s p u x -> s (p u x)")
                 )

@@ -22,7 +22,10 @@ FEATS = 512
 ROWS = 1024
 CHUNKS = ROWS // P
 QUAD = 32
-LAG = 3
+ROW_SPLIT = 1024
+LAG = 2
+LATE = 3
+WARM = (2, 3, 4)
 
 FLOPS = 2 * 2 * ROWS * SLOTS * FEATS
 BYTES = 4 * (FEATS * ROWS + FEATS * ITEMS + ROWS * SLOTS + ROWS + ITEMS + ROWS * FEATS) + 2 * P * SLOTS // 16
@@ -55,9 +58,10 @@ def tile_attend_gwel_x_ts_kernel(tc, xT, wT, y, wt, ts, offs, out):
         for q in range(P // QUAD):
             band = slice(q * QUAD, (q + 1) * QUAD)
             nc.vector.tensor_tensor(out=ident[band, band], in0=column[band, :], in1=row[band, :], op=IS_EQUAL)
+        nc.scalar.copy(out=ts_window[0:1, ROW_SPLIT:], in_=ts_row[:, ROW_SPLIT:])
         ident_bf = keep.tile([P, P], BF16, name="ident_bf")
         nc.scalar.copy(out=ident_bf[:], in_=ident[:])
-        nc.vector.tensor_copy(out=ts_window[0:1, :], in_=ts_row[:])
+        nc.vector.tensor_copy(out=ts_window[0:1, :ROW_SPLIT], in_=ts_row[:, :ROW_SPLIT])
 
 
         w_planes = wT.rearrange("(p t) n -> t p n", t=PACK)
@@ -70,11 +74,13 @@ def tile_attend_gwel_x_ts_kernel(tc, xT, wT, y, wt, ts, offs, out):
         x_view = xT[0].rearrange("(p t) r -> p t r", t=PACK)
         y_view = y[0].rearrange("(c p) n -> p c n", p=P)
         x_raw = {}
+        x_load = {}
         y_raw = {}
 
         def load_x(first, count, tag):
             raw = keep.tile([P, PACK, count * P], F32, name="x_raw", tag=tag, align_bytes=64)
             nc.sync.dma_start(out=raw[:], in_=x_view[:, :, first * P : (first + count) * P])
+            x_load[first] = raw
             for c in range(first, first + count):
                 x_raw[c] = raw[:, :, (c - first) * P : (c - first + 1) * P]
 
@@ -119,7 +125,6 @@ def tile_attend_gwel_x_ts_kernel(tc, xT, wT, y, wt, ts, offs, out):
         wd_scales = keep.tile([P, SLOTS], U8, name="wd_scales", align_bytes=64)
         w_pair = [
             keep.tile([P, 2, SLOTS], BF16, name="w_pair0", tag="stage1", align_bytes=64),
-            keep.tile([P, 2, SLOTS], BF16, name="w_pair1"),
         ]
 
         def gather_plane(t):
@@ -137,24 +142,46 @@ def tile_attend_gwel_x_ts_kernel(tc, xT, wT, y, wt, ts, offs, out):
                 for j in range(PACK):
                     columns = w_pair[0][:, e, j::PACK] if u == 0 else w_d[:, j * P : (j + 1) * P, 2 + e]
                     nc.tensor.transpose(turned[:, e, j, :], columns, ident_bf[:])
-            nc.scalar.copy(
-                out=w_i[:, :, u, :].rearrange("s p (e j) -> s p e j", j=PACK), in_=turned[:].rearrange("s e j p -> s p e j")
+            w_i[u] = keep.tile([P, P, 2, PACK], BF16, name="w_i", tag="w_i0" if u == 0 else "x_rows0", align_bytes=64)
+            nc.scalar.copy(out=w_i[u][:], in_=turned[:].rearrange("s e j p -> s p e j"))
+
+        def quantize_turned(u):
+            cols = slice(2 * u * P, 2 * (u + 1) * P)
+            nc.vector.quantize_mx(
+                out=wi_codes[:, cols].bitcast(E4M3X4),
+                scales=wi_scales[:, cols],
+                in_=w_i[u][:].rearrange("s p e j -> s (p e j)"),
             )
 
         x_bf, x_codes, x_scales, y_dealt = ({} for i in range(4))
         score, scaled, resid, square, bell, weighted, h, h_codes, h_scales, grad = ({} for i in range(10))
 
         def cast_x(c):
-            if c == 0:
-                x_bf[c] = keep.tile([P, P, PACK], BF16, name="x_bf_first", tag="first_rows", align_bytes=64)
-            else:
-                x_bf[c] = work.tile([P, P, PACK], BF16, name="x_bf", align_bytes=64, bufs=3)
+            if c >= 2:
+                if c % 2 == 0:
+                    pair = work.tile([P, 2 * P, PACK], BF16, name="x_pair", align_bytes=64, bufs=2)
+                    nc.scalar.copy(
+                        out=pair[:].rearrange("p (a i) t -> p a t i", i=4),
+                        in_=x_load[c][:].rearrange("p t (a i) -> p a t i", i=4),
+                    )
+                    x_bf[c] = pair
+                return
+            x_bf[c] = work.tile([P, P, PACK], BF16, name="x_bf", align_bytes=64, bufs=2)
             nc.scalar.copy(
                 out=x_bf[c][:].rearrange("p (a i) t -> p a t i", i=4),
                 in_=x_raw[c].rearrange("p t (a i) -> p a t i", i=4),
             )
 
         def quantize_x(c):
+            if c >= 2:
+                if c % 2 == 0:
+                    codes = keep.tile([P, 2 * P], U32, name="x_codes%d" % c, align_bytes=64)
+                    scales = keep.tile([P, 2 * P], U8, name="x_scales%d" % c, align_bytes=64)
+                    nc.vector.quantize_mx(out=codes[:].bitcast(E4M3X4), scales=scales[:], in_=x_bf[c][:].rearrange("p r t -> p (r t)"))
+                    for e in range(2):
+                        x_codes[c + e] = codes[:, e * P : (e + 1) * P]
+                        x_scales[c + e] = scales[:, e * P : (e + 1) * P]
+                return
             x_codes[c] = keep.tile([P, P], U32, name="x_codes%d" % c, align_bytes=64)
             x_scales[c] = keep.tile([P, P], U8, name="x_scales%d" % c, align_bytes=64)
             nc.vector.quantize_mx(
@@ -170,15 +197,26 @@ def tile_attend_gwel_x_ts_kernel(tc, xT, wT, y, wt, ts, offs, out):
 
         def multiply_scores(c):
             score[c] = psum.tile([P, SLOTS], F32, name="score", tag="score", bufs=2)
-            nc.tensor.matmul_mx(
-                out=score[c][:],
-                lhsT=x_codes[c][:].bitcast(E4M3X4),
-                lhsT_scale=x_scales[c][:],
-                rhs=wd_codes[:].bitcast(E4M3X4),
-                rhs_scale=wd_scales[:],
-                start=True,
-                stop=True,
-            )
+            if c == 0:
+                nc.tensor.matmul_mx(
+                    out=score[c][:],
+                    lhsT=wd_codes[:, :P].bitcast(E4M3X4),
+                    lhsT_scale=wd_scales[:, :P],
+                    rhs=wd_codes[:].bitcast(E4M3X4),
+                    rhs_scale=wd_scales[:],
+                    start=True,
+                    stop=True,
+                )
+            for repeat in range(2 if c in WARM else 1):
+                nc.tensor.matmul_mx(
+                    out=score[c][:],
+                    lhsT=x_codes[c][:].bitcast(E4M3X4),
+                    lhsT_scale=x_scales[c][:],
+                    rhs=wd_codes[:].bitcast(E4M3X4),
+                    rhs_scale=wd_scales[:],
+                    start=True,
+                    stop=True,
+                )
 
         def scale_scores(c):
             scaled[c] = work.tile([P, SLOTS], F32, name="scaled")
@@ -204,11 +242,11 @@ def tile_attend_gwel_x_ts_kernel(tc, xT, wT, y, wt, ts, offs, out):
             nc.scalar.activation(out=square[c][:], in_=resid[c][:], func=ACT.Square)
 
         def exponentiate(c):
-            bell[c] = work.tile([P, PACK, P], F32, name="bell", bufs=LAG + 2)
+            bell[c] = work.tile([P, PACK, P], F32, name="bell", bufs=LAG + 3)
             nc.scalar.activation(out=bell[c][:], in_=square[c][:], func=ACT.Exp, scale=-0.5)
 
         def weigh_residual(c):
-            weighted[c] = work.tile([P, PACK, P], F32, name="weighted", bufs=LAG + 2)
+            weighted[c] = work.tile([P, PACK, P], F32, name="weighted", bufs=LAG + 3)
             nc.vector.tensor_tensor(
                 out=weighted[c][:], in0=resid[c][:], in1=factor[:, :, c * P : (c + 1) * P], op=MULT
             )
@@ -243,24 +281,31 @@ def tile_attend_gwel_x_ts_kernel(tc, xT, wT, y, wt, ts, offs, out):
 
         def store_gradient(c):
             result = work.tile([P, FEATS], F32, name="result")
-            nc.scalar.copy(out=result[:], in_=grad[c][:])
+            copy = nc.vector.tensor_copy if c == CHUNKS - 2 else nc.scalar.copy
+            copy(
+                out=result[:].rearrange("r (p u e) -> r p u e", u=2, e=2),
+                in_=grad[c][:].rearrange("r (u p e) -> r p u e", u=2, e=2),
+            )
             nc.sync.dma_start(out=out[0, c * P : (c + 1) * P, :], in_=result[:])
 
-        w_i = keep.tile([P, P, 2, 2 * PACK], BF16, name="w_i", align_bytes=64)
+        w_i = {}
         gather_plane(0)
         gather_plane(1)
         weave_pair(0)
         turn_pair(0)
-        gather_plane(2)
-        gather_plane(3)
-        weave_pair(1)
+        for t in (2, 3):
+            nc.vector.tensor_copy(
+                out=w_d[:, :, t].rearrange("p (j s) -> p s j", j=PACK), in_=w_window[t][:].indirect(offsets[:])
+            )
         cast_x(0)
-        quantize_x(0)
-        wd_codes = keep.tile([P, SLOTS], U32, name="wd_codes", tag="first_rows", align_bytes=64)
+        wd_codes = keep.tile([P, SLOTS], U32, name="wd_codes", align_bytes=64)
         nc.vector.quantize_mx(
             out=wd_codes[:].bitcast(E4M3X4), scales=wd_scales[:], in_=w_d[:].rearrange("p i t -> p (i t)")
         )
+        quantize_x(0)
         multiply_scores(0)
+        wi_codes = keep.tile([P, FEATS], U32, name="wi_codes", tag="plane3", align_bytes=64)
+        quantize_turned(0)
         deal_targets(0)
         turn_targets(0)
         cast_x(1)
@@ -283,14 +328,16 @@ def tile_attend_gwel_x_ts_kernel(tc, xT, wT, y, wt, ts, offs, out):
             (weigh_residual, -1),
             (store_gradient, -LAG - 1),
         )
-        for step in range(CHUNKS + LAG + 1):
+        for step in range(CHUNKS + LAG + 2):
             for stage, shift in pipeline:
-                if 0 <= step + shift < CHUNKS:
-                    stage(step + shift)
+                chunk = step + shift
+                if shift <= -LAG and chunk >= LATE:
+                    chunk -= 1
+                    if chunk < LATE:
+                        continue
+                if 0 <= chunk < CHUNKS:
+                    stage(chunk)
             if step == 0:
                 turn_pair(1)
             if step == 1:
-                wi_codes = keep.tile([P, FEATS], U32, name="wi_codes", tag="y_rows0", align_bytes=64)
-                nc.vector.quantize_mx(
-                    out=wi_codes[:].bitcast(E4M3X4), scales=wi_scales[:], in_=w_i[:].rearrange("s p u x -> s (p u x)")
-                )
+                quantize_turned(1)

@@ -23,9 +23,7 @@ ROWS = 1024
 CHUNKS = ROWS // P
 QUAD = 32
 ROW_SPLIT = 1024
-LAG = 2
-LATE = 3
-WARM = (2, 3, 4)
+LAG = 3
 
 FLOPS = 2 * 2 * ROWS * SLOTS * FEATS
 BYTES = 4 * (FEATS * ROWS + FEATS * ITEMS + ROWS * SLOTS + ROWS + ITEMS + ROWS * FEATS) + 2 * P * SLOTS // 16
@@ -45,12 +43,12 @@ def tile_attend_gwel_x_ts_kernel(tc, xT, wT, y, wt, ts, offs, out):
         wt_runs = keep.tile([P, CHUNKS], F32, name="wt_runs")
         nc.sync.dma_start(out=wt_runs[:], in_=wt[0].rearrange("(p k) o -> p (k o)", k=CHUNKS))
         ts_window = keep.tile([P, ITEMS], F32, name="ts_window", tag="stage1", align_bytes=64)
-        nc.gpsimd.memset(ts_window[:], 0.0)
 
         ones = keep.tile([P, QUAD], F32, name="ones")
-        nc.vector.memset(ones[:], 1.0)
+        nc.gpsimd.memset(ones[:], 1.0)
         ident = keep.tile([P, P], F32, name="ident")
-        nc.vector.memset(ident[:], 0.0)
+        nc.gpsimd.memset(ident[:], 0.0)
+        nc.gpsimd.memset(ts_window[:], 0.0)
         column = keep.tile([P, QUAD], F32, name="column", align_bytes=64)
         nc.vector.tensor_tensor_scan(out=column[:], data0=ones[:], data1=ones[:], initial=0.0, op0=MULT, op1=ADD)
         row = keep.tile([P, QUAD], F32, name="row", align_bytes=64)
@@ -143,7 +141,10 @@ def tile_attend_gwel_x_ts_kernel(tc, xT, wT, y, wt, ts, offs, out):
                     columns = w_pair[0][:, e, j::PACK] if u == 0 else w_d[:, j * P : (j + 1) * P, 2 + e]
                     nc.tensor.transpose(turned[:, e, j, :], columns, ident_bf[:])
             w_i[u] = keep.tile([P, P, 2, PACK], BF16, name="w_i", tag="w_i0" if u == 0 else "x_rows0", align_bytes=64)
-            nc.scalar.copy(out=w_i[u][:], in_=turned[:].rearrange("s e j p -> s p e j"))
+            nc.scalar.copy(
+                out=w_i[u][:].rearrange("s (a i) e j -> s a (e j) i", i=2),
+                in_=turned[:].rearrange("s e j (a i) -> s a (e j) i", i=2),
+            )
 
         def quantize_turned(u):
             cols = slice(2 * u * P, 2 * (u + 1) * P)
@@ -161,15 +162,15 @@ def tile_attend_gwel_x_ts_kernel(tc, xT, wT, y, wt, ts, offs, out):
                 if c % 2 == 0:
                     pair = work.tile([P, 2 * P, PACK], BF16, name="x_pair", align_bytes=64, bufs=2)
                     nc.scalar.copy(
-                        out=pair[:].rearrange("p (a i) t -> p a t i", i=4),
-                        in_=x_load[c][:].rearrange("p t (a i) -> p a t i", i=4),
+                        out=pair[:].rearrange("p (a i) t -> p a t i", i=2),
+                        in_=x_load[c][:].rearrange("p t (a i) -> p a t i", i=2),
                     )
                     x_bf[c] = pair
                 return
             x_bf[c] = work.tile([P, P, PACK], BF16, name="x_bf", align_bytes=64, bufs=2)
             nc.scalar.copy(
-                out=x_bf[c][:].rearrange("p (a i) t -> p a t i", i=4),
-                in_=x_raw[c].rearrange("p t (a i) -> p a t i", i=4),
+                out=x_bf[c][:].rearrange("p (a i) t -> p a t i", i=2),
+                in_=x_raw[c].rearrange("p t (a i) -> p a t i", i=2),
             )
 
         def quantize_x(c):
@@ -191,32 +192,21 @@ def tile_attend_gwel_x_ts_kernel(tc, xT, wT, y, wt, ts, offs, out):
         def deal_targets(c):
             y_dealt[c] = work.tile([P, SLOTS], F32, name="y_dealt", bufs=2)
             nc.vector.tensor_copy(
-                out=y_dealt[c][:].rearrange("r (j a i) -> r a j i", j=PACK, i=4),
-                in_=y_raw[c].rearrange("r (a i j) -> r a j i", j=PACK, i=4),
+                out=y_dealt[c][:].rearrange("r (v e a i) -> r a v i e", v=2, e=2, i=4),
+                in_=y_raw[c].rearrange("r (a i v e) -> r a v i e", v=2, e=2, i=4),
             )
 
         def multiply_scores(c):
             score[c] = psum.tile([P, SLOTS], F32, name="score", tag="score", bufs=2)
-            if c == 0:
-                nc.tensor.matmul_mx(
-                    out=score[c][:],
-                    lhsT=wd_codes[:, :P].bitcast(E4M3X4),
-                    lhsT_scale=wd_scales[:, :P],
-                    rhs=wd_codes[:].bitcast(E4M3X4),
-                    rhs_scale=wd_scales[:],
-                    start=True,
-                    stop=True,
-                )
-            for repeat in range(2 if c in WARM else 1):
-                nc.tensor.matmul_mx(
-                    out=score[c][:],
-                    lhsT=x_codes[c][:].bitcast(E4M3X4),
-                    lhsT_scale=x_scales[c][:],
-                    rhs=wd_codes[:].bitcast(E4M3X4),
-                    rhs_scale=wd_scales[:],
-                    start=True,
-                    stop=True,
-                )
+            nc.tensor.matmul_mx(
+                out=score[c][:],
+                lhsT=x_codes[c][:].bitcast(E4M3X4),
+                lhsT_scale=x_scales[c][:],
+                rhs=wd_codes[:].bitcast(E4M3X4),
+                rhs_scale=wd_scales[:],
+                start=True,
+                stop=True,
+            )
 
         def scale_scores(c):
             scaled[c] = work.tile([P, SLOTS], F32, name="scaled")
@@ -242,11 +232,11 @@ def tile_attend_gwel_x_ts_kernel(tc, xT, wT, y, wt, ts, offs, out):
             nc.scalar.activation(out=square[c][:], in_=resid[c][:], func=ACT.Square)
 
         def exponentiate(c):
-            bell[c] = work.tile([P, PACK, P], F32, name="bell", bufs=LAG + 3)
+            bell[c] = work.tile([P, PACK, P], F32, name="bell", bufs=LAG + 2)
             nc.scalar.activation(out=bell[c][:], in_=square[c][:], func=ACT.Exp, scale=-0.5)
 
         def weigh_residual(c):
-            weighted[c] = work.tile([P, PACK, P], F32, name="weighted", bufs=LAG + 3)
+            weighted[c] = work.tile([P, PACK, P], F32, name="weighted", bufs=LAG + 2)
             nc.vector.tensor_tensor(
                 out=weighted[c][:], in0=resid[c][:], in1=factor[:, :, c * P : (c + 1) * P], op=MULT
             )
@@ -254,9 +244,9 @@ def tile_attend_gwel_x_ts_kernel(tc, xT, wT, y, wt, ts, offs, out):
         def form_h(c):
             h[c] = work.tile([P, P, PACK], BF16, name="h", align_bytes=64)
             nc.vector.tensor_tensor(
-                out=h[c][:].rearrange("s (a i) j -> s a j i", i=4),
-                in0=weighted[c][:].rearrange("s j (a i) -> s a j i", i=4),
-                in1=bell[c][:].rearrange("s j (a i) -> s a j i", i=4),
+                out=h[c][:].rearrange("s (a i) j -> s a j i", i=2),
+                in0=weighted[c][:].rearrange("s j (a i) -> s a j i", i=2),
+                in1=bell[c][:].rearrange("s j (a i) -> s a j i", i=2),
                 op=MULT,
             )
 
@@ -328,15 +318,10 @@ def tile_attend_gwel_x_ts_kernel(tc, xT, wT, y, wt, ts, offs, out):
             (weigh_residual, -1),
             (store_gradient, -LAG - 1),
         )
-        for step in range(CHUNKS + LAG + 2):
+        for step in range(CHUNKS + LAG + 1):
             for stage, shift in pipeline:
-                chunk = step + shift
-                if shift <= -LAG and chunk >= LATE:
-                    chunk -= 1
-                    if chunk < LATE:
-                        continue
-                if 0 <= chunk < CHUNKS:
-                    stage(chunk)
+                if 0 <= step + shift < CHUNKS:
+                    stage(step + shift)
             if step == 0:
                 turn_pair(1)
             if step == 1:

@@ -22,8 +22,10 @@ FEATS = 512
 ROWS = 1024
 CHUNKS = ROWS // P
 QUAD = 32
-ROW_SPLIT = 1024
-LAG = 3
+LAG = 2
+DEALT_ON_SCALAR = (0, 1, 7)
+DEALT_TAGS = ["dealt0", "dealt1"] * 4
+ROW_GROUPS = {0: 2, 2: 2, 4: 2, 6: 2}
 
 FLOPS = 2 * 2 * ROWS * SLOTS * FEATS
 BYTES = 4 * (FEATS * ROWS + FEATS * ITEMS + ROWS * SLOTS + ROWS + ITEMS + ROWS * FEATS) + 2 * P * SLOTS // 16
@@ -41,14 +43,16 @@ def tile_attend_gwel_x_ts_kernel(tc, xT, wT, y, wt, ts, offs, out):
         ts_row = keep.tile([1, ITEMS], F32, name="ts_row")
         nc.sync.dma_start(out=ts_row[:], in_=ts[0:1, :])
         wt_runs = keep.tile([P, CHUNKS], F32, name="wt_runs")
-        nc.sync.dma_start(out=wt_runs[:], in_=wt[0].rearrange("(p k) o -> p (k o)", k=CHUNKS))
+        nc.sync.dma_start(
+            out=wt_runs[:].rearrange("p (b k) -> p b k", k=PACK), in_=wt[0].rearrange("(b p k) o -> p b (k o)", p=P, k=PACK)
+        )
         ts_window = keep.tile([P, ITEMS], F32, name="ts_window", tag="stage1", align_bytes=64)
 
         ones = keep.tile([P, QUAD], F32, name="ones")
         nc.gpsimd.memset(ones[:], 1.0)
         ident = keep.tile([P, P], F32, name="ident")
         nc.gpsimd.memset(ident[:], 0.0)
-        nc.gpsimd.memset(ts_window[:], 0.0)
+        nc.gpsimd.memset(ts_window[:, : ITEMS // 2], 0.0)
         column = keep.tile([P, QUAD], F32, name="column", align_bytes=64)
         nc.vector.tensor_tensor_scan(out=column[:], data0=ones[:], data1=ones[:], initial=0.0, op0=MULT, op1=ADD)
         row = keep.tile([P, QUAD], F32, name="row", align_bytes=64)
@@ -56,11 +60,8 @@ def tile_attend_gwel_x_ts_kernel(tc, xT, wT, y, wt, ts, offs, out):
         for q in range(P // QUAD):
             band = slice(q * QUAD, (q + 1) * QUAD)
             nc.vector.tensor_tensor(out=ident[band, band], in0=column[band, :], in1=row[band, :], op=IS_EQUAL)
-        nc.scalar.copy(out=ts_window[0:1, ROW_SPLIT:], in_=ts_row[:, ROW_SPLIT:])
-        ident_bf = keep.tile([P, P], BF16, name="ident_bf")
-        nc.scalar.copy(out=ident_bf[:], in_=ident[:])
-        nc.vector.tensor_copy(out=ts_window[0:1, :ROW_SPLIT], in_=ts_row[:, :ROW_SPLIT])
-
+        nc.vector.memset(ts_window[:, ITEMS // 2 :], 0.0)
+        nc.vector.tensor_copy(out=ts_window[0:1, :], in_=ts_row[:])
 
         w_planes = wT.rearrange("(p t) n -> t p n", t=PACK)
         w_window = []
@@ -72,35 +73,34 @@ def tile_attend_gwel_x_ts_kernel(tc, xT, wT, y, wt, ts, offs, out):
         x_view = xT[0].rearrange("(p t) r -> p t r", t=PACK)
         y_view = y[0].rearrange("(c p) n -> p c n", p=P)
         x_raw = {}
-        x_load = {}
         y_raw = {}
 
-        def load_x(first, count, tag):
-            raw = keep.tile([P, PACK, count * P], F32, name="x_raw", tag=tag, align_bytes=64)
-            nc.sync.dma_start(out=raw[:], in_=x_view[:, :, first * P : (first + count) * P])
-            x_load[first] = raw
-            for c in range(first, first + count):
-                x_raw[c] = raw[:, :, (c - first) * P : (c - first + 1) * P]
+        def load_x(first):
+            raw = keep.tile([P, PACK, 2 * P], F32, name="x_raw", tag="x_rows%d" % first, align_bytes=64)
+            nc.sync.dma_start(out=raw[:], in_=x_view[:, :, first * P : (first + 2) * P])
+            for e in range(2):
+                x_raw[first + e] = raw[:, :, e * P :]
 
-        def load_y(first, count, tag):
-            raw = keep.tile([P, count, SLOTS], F32, name="y_raw", tag=tag, align_bytes=64)
-            nc.sync.dma_start(out=raw[:], in_=y_view[:, first : first + count, :])
-            for c in range(first, first + count):
-                y_raw[c] = raw[:, c - first, :]
-
+        def load_y(first):
+            raw = keep.tile([P, 2, SLOTS], F32, name="y_raw", tag="y_rows%d" % first, align_bytes=64)
+            nc.sync.dma_start(out=raw[:], in_=y_view[:, first : first + 2, :])
+            for e in range(2):
+                y_raw[first + e] = raw[:, e, :]
 
         for first in range(0, CHUNKS, 2):
-            load_x(first, 2, "x_rows%d" % first)
-            load_y(first, 2, "y_rows%d" % first)
+            load_x(first)
+            load_y(first)
 
         wt_row = keep.tile([P, ROWS], F32, name="wt_row")
-        wt_lines = wt_row[:].rearrange("s (p b k) -> s p b k", b=CHUNKS // PACK, k=PACK)
         for b in range(CHUNKS // PACK):
-            spread = psum.tile([P, PACK, P], F32, name="spread", tag="resid", bufs=4)
+            bank = psum.tile([P, PACK, P], F32, name="spread", tag="resid", bufs=4)
             for k in range(PACK):
                 col = PACK * b + k
-                nc.tensor.transpose(spread[:, k, :], wt_runs[:, col : col + 1].to_broadcast([P, P]), ident[:])
-            nc.scalar.copy(out=wt_lines[:, :, b, :], in_=spread[:].rearrange("s k p -> s p k"))
+                nc.tensor.transpose(bank[:, k, :], wt_runs[:, col : col + 1].to_broadcast([P, P]), ident[:])
+            nc.scalar.copy(
+                out=wt_row[:, b * SLOTS : (b + 1) * SLOTS].rearrange("s (a i k) -> s a k i", i=2, k=PACK),
+                in_=bank[:].rearrange("s k (a i) -> s a k i", i=2),
+            )
 
         ts_listed = keep.tile([P, SLOTS], F32, name="ts_listed")
         nc.vector.tensor_copy(out=ts_listed[:], in_=ts_window[:].indirect(offsets[:]))
@@ -109,41 +109,47 @@ def tile_attend_gwel_x_ts_kernel(tc, xT, wT, y, wt, ts, offs, out):
             nc.tensor.transpose(ts_turned[:, j, :], ts_listed[:, j::PACK], ident[:])
         nts_col = keep.tile([P, PACK], F32, name="nts_col")
         nc.scalar.activation(out=nts_col[:], in_=ts_turned[:, :, 0], func=ACT.Copy, scale=-1.0)
-        factor = keep.tile([P, PACK, ROWS], F32, name="factor")
-        for j in range(PACK):
-            nc.scalar.activation(out=factor[:, j, :], in_=wt_row[:], func=ACT.Copy, scale=nts_col[:, j : j + 1])
         ts_spread = psum.tile([P, PACK, P], F32, name="ts_spread", tag="resid", bufs=4)
         for j in range(PACK):
             nc.tensor.transpose(ts_spread[:, j, :], nts_col[:, j : j + 1].to_broadcast([P, P]), ident[:])
+        factor = keep.tile([P, PACK, ROWS], F32, name="factor")
         nts_row = keep.tile([P, SLOTS], F32, name="nts_row")
-        nc.scalar.copy(out=nts_row[:], in_=ts_spread[:].rearrange("r j s -> r (j s)"))
+
+        def make_factor(j):
+            nc.scalar.activation(out=factor[:, j, :], in_=wt_row[:], func=ACT.Copy, scale=nts_col[:, j : j + 1])
 
         w_d = keep.tile([P, SLOTS, PACK], BF16, name="w_d", align_bytes=64)
         wi_scales = keep.tile([P, FEATS], U8, name="wi_scales", align_bytes=64)
+        wd_codes = keep.tile([P, SLOTS], U32, name="wd_codes", align_bytes=64)
         wd_scales = keep.tile([P, SLOTS], U8, name="wd_scales", align_bytes=64)
-        w_pair = [
-            keep.tile([P, 2, SLOTS], BF16, name="w_pair0", tag="stage1", align_bytes=64),
+        w_listed = keep.tile([P, 2 * SLOTS], BF16, name="w_listed", tag="stage1", align_bytes=64)
+        w_i = [
+            keep.tile([P, 2, P, PACK], BF16, name="w_i0", align_bytes=64),
+            keep.tile([P, 2, P, PACK], BF16, name="w_i1", tag="x_rows0", align_bytes=64),
         ]
 
         def gather_plane(t):
-            nc.vector.tensor_copy(out=w_pair[t // 2][:, t % 2, :], in_=w_window[t][:].indirect(offsets[:]))
+            nc.vector.tensor_copy(out=w_listed[:, t * SLOTS : (t + 1) * SLOTS], in_=w_window[t][:].indirect(offsets[:]))
 
-        def weave_pair(u):
-            nc.vector.tensor_copy(
-                out=w_d[:, :, 2 * u : 2 * u + 2].rearrange("p (j s) e -> p j s e", j=PACK),
-                in_=w_pair[u][:].rearrange("p e (s j) -> p j s e", j=PACK),
+        def turn_plane(t):
+            turned = psum.tile([P, 2, P], F32, name="turned", tag="grad", bufs=2)
+            words = w_listed[:, t * SLOTS : (t + 1) * SLOTS].bitcast(F32)
+            for u in range(2):
+                nc.tensor.transpose(turned[:, u, :], words[:, u::2], ident[:])
+            nc.scalar.copy(
+                out=w_i[t // 2][:, t % 2, :, :].rearrange("s p j -> s (p j)").bitcast(F32).rearrange("s (a i u) -> s a u i", i=2, u=2),
+                in_=turned[:].rearrange("s u (a i) -> s a u i", i=2),
             )
 
-        def turn_pair(u):
-            turned = psum.tile([P, 2, PACK, P], BF16, name="turned", tag="grad", bufs=2)
-            for e in range(2):
-                for j in range(PACK):
-                    columns = w_pair[0][:, e, j::PACK] if u == 0 else w_d[:, j * P : (j + 1) * P, 2 + e]
-                    nc.tensor.transpose(turned[:, e, j, :], columns, ident_bf[:])
-            w_i[u] = keep.tile([P, P, 2, PACK], BF16, name="w_i", tag="w_i0" if u == 0 else "x_rows0", align_bytes=64)
+        def turn_last_planes():
+            turned = psum.tile([P, PACK, P], F32, name="turned", tag="grad", bufs=2)
+            words = w_d[:].rearrange("p i t -> p (i t)").bitcast(F32)
+            for j in range(PACK):
+                nc.tensor.transpose(turned[:, j, :], words[:, 2 * j * P + 1 : 2 * (j + 1) * P : 2], ident[:])
+            halves = turned[:].rearrange("s j p -> s (j p)").bitcast(BF16)
             nc.scalar.copy(
-                out=w_i[u][:].rearrange("s (a i) e j -> s a (e j) i", i=2),
-                in_=turned[:].rearrange("s e j (a i) -> s a (e j) i", i=2),
+                out=w_i[1][:].rearrange("s e (a i) j -> s a j i e", i=2),
+                in_=halves.rearrange("s (j a i e) -> s a j i e", j=PACK, i=2, e=2),
             )
 
         def quantize_turned(u):
@@ -151,57 +157,63 @@ def tile_attend_gwel_x_ts_kernel(tc, xT, wT, y, wt, ts, offs, out):
             nc.vector.quantize_mx(
                 out=wi_codes[:, cols].bitcast(E4M3X4),
                 scales=wi_scales[:, cols],
-                in_=w_i[u][:].rearrange("s p e j -> s (p e j)"),
+                in_=w_i[u][:].rearrange("s e p j -> s (e p j)"),
             )
 
         x_bf, x_codes, x_scales, y_dealt = ({} for i in range(4))
         score, scaled, resid, square, bell, weighted, h, h_codes, h_scales, grad = ({} for i in range(10))
 
         def cast_x(c):
-            if c >= 2:
-                if c % 2 == 0:
-                    pair = work.tile([P, 2 * P, PACK], BF16, name="x_pair", align_bytes=64, bufs=2)
-                    nc.scalar.copy(
-                        out=pair[:].rearrange("p (a i) t -> p a t i", i=2),
-                        in_=x_load[c][:].rearrange("p t (a i) -> p a t i", i=2),
-                    )
-                    x_bf[c] = pair
-                return
-            x_bf[c] = work.tile([P, P, PACK], BF16, name="x_bf", align_bytes=64, bufs=2)
+            count = ROW_GROUPS[c]
+            tag = {0: "x_bf0", 2: "x_bf2", 4: "scaled1", 6: "scaled2"}[c]
+            x_bf[c] = keep.tile([P, count * P, PACK], BF16, name="x_bf", tag=tag, align_bytes=64)
             nc.scalar.copy(
                 out=x_bf[c][:].rearrange("p (a i) t -> p a t i", i=2),
-                in_=x_raw[c].rearrange("p t (a i) -> p a t i", i=2),
+                in_=x_raw[c][:, :, : count * P].rearrange("p t (a i) -> p a t i", i=2),
             )
 
         def quantize_x(c):
-            if c >= 2:
-                if c % 2 == 0:
-                    codes = keep.tile([P, 2 * P], U32, name="x_codes%d" % c, align_bytes=64)
-                    scales = keep.tile([P, 2 * P], U8, name="x_scales%d" % c, align_bytes=64)
-                    nc.vector.quantize_mx(out=codes[:].bitcast(E4M3X4), scales=scales[:], in_=x_bf[c][:].rearrange("p r t -> p (r t)"))
-                    for e in range(2):
-                        x_codes[c + e] = codes[:, e * P : (e + 1) * P]
-                        x_scales[c + e] = scales[:, e * P : (e + 1) * P]
-                return
-            x_codes[c] = keep.tile([P, P], U32, name="x_codes%d" % c, align_bytes=64)
-            x_scales[c] = keep.tile([P, P], U8, name="x_scales%d" % c, align_bytes=64)
+            count = ROW_GROUPS[c]
+            codes = keep.tile([P, count * P], U32, name="x_codes", tag="x_codes%d" % c, align_bytes=64)
+            scales = keep.tile([P, count * P], U8, name="x_scales%d" % c, align_bytes=64)
             nc.vector.quantize_mx(
-                out=x_codes[c][:].bitcast(E4M3X4), scales=x_scales[c][:], in_=x_bf[c][:].rearrange("p r t -> p (r t)")
+                out=codes[:].bitcast(E4M3X4), scales=scales[:], in_=x_bf[c][:].rearrange("p r t -> p (r t)")
             )
+            for e in range(count):
+                x_codes[c + e] = codes[:, e * P : (e + 1) * P]
+                x_scales[c + e] = scales[:, e * P : (e + 1) * P]
+
+        def prepare_rows(c):
+            if c in ROW_GROUPS:
+                cast_x(c)
+                quantize_x(c)
+
+        def first_rows(c):
+            if c == 2:
+                quantize_x(c)
+
+        def later_rows(c):
+            if c > 2:
+                prepare_rows(c)
 
         def deal_targets(c):
-            y_dealt[c] = work.tile([P, SLOTS], F32, name="y_dealt", bufs=2)
-            nc.vector.tensor_copy(
+            y_dealt[c] = keep.tile([P, SLOTS], F32, name="y_dealt", tag=DEALT_TAGS[c], align_bytes=64)
+            copy = nc.scalar.copy if c in DEALT_ON_SCALAR else nc.vector.tensor_copy
+            copy(
                 out=y_dealt[c][:].rearrange("r (v e a i) -> r a v i e", v=2, e=2, i=4),
                 in_=y_raw[c].rearrange("r (a i v e) -> r a v i e", v=2, e=2, i=4),
             )
+
+        def deal_later(c):
+            if c > 1:
+                deal_targets(c)
 
         def multiply_scores(c):
             score[c] = psum.tile([P, SLOTS], F32, name="score", tag="score", bufs=2)
             nc.tensor.matmul_mx(
                 out=score[c][:],
-                lhsT=x_codes[c][:].bitcast(E4M3X4),
-                lhsT_scale=x_scales[c][:],
+                lhsT=x_codes[c].bitcast(E4M3X4),
+                lhsT_scale=x_scales[c],
                 rhs=wd_codes[:].bitcast(E4M3X4),
                 rhs_scale=wd_scales[:],
                 start=True,
@@ -209,7 +221,7 @@ def tile_attend_gwel_x_ts_kernel(tc, xT, wT, y, wt, ts, offs, out):
             )
 
         def scale_scores(c):
-            scaled[c] = work.tile([P, SLOTS], F32, name="scaled")
+            scaled[c] = keep.tile([P, SLOTS], F32, name="scaled", tag="scaled%d" % (c % 3), align_bytes=64)
             nc.vector.tensor_tensor(out=scaled[c][:], in0=score[c][:], in1=nts_row[:], op=MULT)
 
         def turn_targets(c):
@@ -271,58 +283,60 @@ def tile_attend_gwel_x_ts_kernel(tc, xT, wT, y, wt, ts, offs, out):
 
         def store_gradient(c):
             result = work.tile([P, FEATS], F32, name="result")
-            copy = nc.vector.tensor_copy if c == CHUNKS - 2 else nc.scalar.copy
-            copy(
-                out=result[:].rearrange("r (p u e) -> r p u e", u=2, e=2),
-                in_=grad[c][:].rearrange("r (u p e) -> r p u e", u=2, e=2),
+            nc.scalar.copy(
+                out=result[:].rearrange("r (a i t) -> r a t i", i=2, t=PACK),
+                in_=grad[c][:].rearrange("r (t a i) -> r a t i", i=2, t=PACK),
             )
             nc.sync.dma_start(out=out[0, c * P : (c + 1) * P, :], in_=result[:])
 
-        w_i = {}
-        gather_plane(0)
-        gather_plane(1)
-        weave_pair(0)
-        turn_pair(0)
-        for t in (2, 3):
+        for j in range(PACK):
+            make_factor(j)
+        nc.scalar.copy(out=nts_row[:], in_=ts_spread[:].rearrange("r j s -> r (j s)"))
+        for t in range(2):
+            gather_plane(t)
+            turn_plane(t)
+        nc.vector.tensor_copy(
+            out=w_d[:, :, :2].rearrange("p (j s) t -> p j s t", j=PACK),
+            in_=w_listed[:].rearrange("p (t s j) -> p j s t", t=2, j=PACK),
+        )
+        for t in range(2, PACK):
             nc.vector.tensor_copy(
                 out=w_d[:, :, t].rearrange("p (j s) -> p s j", j=PACK), in_=w_window[t][:].indirect(offsets[:])
             )
         cast_x(0)
-        wd_codes = keep.tile([P, SLOTS], U32, name="wd_codes", align_bytes=64)
         nc.vector.quantize_mx(
             out=wd_codes[:].bitcast(E4M3X4), scales=wd_scales[:], in_=w_d[:].rearrange("p i t -> p (i t)")
         )
         quantize_x(0)
         multiply_scores(0)
-        wi_codes = keep.tile([P, FEATS], U32, name="wi_codes", tag="plane3", align_bytes=64)
-        quantize_turned(0)
+        multiply_scores(1)
         deal_targets(0)
         turn_targets(0)
-        cast_x(1)
-        quantize_x(1)
+        turn_last_planes()
+        wi_codes = keep.tile([P, FEATS], U32, name="wi_codes", tag="x_bf0", align_bytes=64)
+        quantize_turned(0)
+        deal_targets(1)
         cast_x(2)
 
         pipeline = (
-            (cast_x, 3),
             (scale_scores, 0),
-            (quantize_h, -LAG - 1),
-            (multiply_scores, 1),
-            (multiply_gradient, -LAG - 1),
             (turn_scores, 0),
             (square_residual, 0),
             (exponentiate, 0),
-            (deal_targets, 1),
+            (quantize_h, -LAG - 1),
+            (multiply_gradient, -LAG - 1),
+            (first_rows, 2),
+            (multiply_scores, 2),
+            (deal_later, 1),
             (turn_targets, 1),
-            (quantize_x, 2),
             (form_h, -LAG),
             (weigh_residual, -1),
             (store_gradient, -LAG - 1),
+            (later_rows, 3),
         )
         for step in range(CHUNKS + LAG + 1):
             for stage, shift in pipeline:
                 if 0 <= step + shift < CHUNKS:
                     stage(step + shift)
             if step == 0:
-                turn_pair(1)
-            if step == 1:
                 quantize_turned(1)

@@ -23,8 +23,8 @@ ROWS = 1024
 CHUNKS = ROWS // P
 QUAD = 32
 LAG = 2
-DEALT_ON_SCALAR = (0, 1, 7)
-DEALT_TAGS = ["dealt0", "dealt1"] * 4
+DEALT_TAGS = ["x_codes0", "x_bf0"]
+SUMMED_ON_VECTOR = ()
 ROW_GROUPS = {0: 2, 2: 2, 4: 2, 6: 2}
 
 FLOPS = 2 * 2 * ROWS * SLOTS * FEATS
@@ -43,9 +43,7 @@ def tile_attend_gwel_x_ts_kernel(tc, xT, wT, y, wt, ts, offs, out):
         ts_row = keep.tile([1, ITEMS], F32, name="ts_row")
         nc.sync.dma_start(out=ts_row[:], in_=ts[0:1, :])
         wt_runs = keep.tile([P, CHUNKS], F32, name="wt_runs")
-        nc.sync.dma_start(
-            out=wt_runs[:].rearrange("p (b k) -> p b k", k=PACK), in_=wt[0].rearrange("(b p k) o -> p b (k o)", p=P, k=PACK)
-        )
+        nc.sync.dma_start(out=wt_runs[:], in_=wt[0].rearrange("(p k) o -> p (k o)", k=CHUNKS))
         ts_window = keep.tile([P, ITEMS], F32, name="ts_window", tag="stage1", align_bytes=64)
 
         ones = keep.tile([P, QUAD], F32, name="ones")
@@ -92,15 +90,13 @@ def tile_attend_gwel_x_ts_kernel(tc, xT, wT, y, wt, ts, offs, out):
             load_y(first)
 
         wt_row = keep.tile([P, ROWS], F32, name="wt_row")
+        wt_lines = wt_row[:].rearrange("s (p b k) -> s p b k", b=CHUNKS // PACK, k=PACK)
         for b in range(CHUNKS // PACK):
             bank = psum.tile([P, PACK, P], F32, name="spread", tag="resid", bufs=4)
             for k in range(PACK):
                 col = PACK * b + k
                 nc.tensor.transpose(bank[:, k, :], wt_runs[:, col : col + 1].to_broadcast([P, P]), ident[:])
-            nc.scalar.copy(
-                out=wt_row[:, b * SLOTS : (b + 1) * SLOTS].rearrange("s (a i k) -> s a k i", i=2, k=PACK),
-                in_=bank[:].rearrange("s k (a i) -> s a k i", i=2),
-            )
+            nc.scalar.copy(out=wt_lines[:, :, b, :], in_=bank[:].rearrange("s k p -> s p k"))
 
         ts_listed = keep.tile([P, SLOTS], F32, name="ts_listed")
         nc.vector.tensor_copy(out=ts_listed[:], in_=ts_window[:].indirect(offsets[:]))
@@ -123,23 +119,20 @@ def tile_attend_gwel_x_ts_kernel(tc, xT, wT, y, wt, ts, offs, out):
         wd_codes = keep.tile([P, SLOTS], U32, name="wd_codes", align_bytes=64)
         wd_scales = keep.tile([P, SLOTS], U8, name="wd_scales", align_bytes=64)
         w_listed = keep.tile([P, 2 * SLOTS], BF16, name="w_listed", tag="stage1", align_bytes=64)
-        w_i = [
-            keep.tile([P, 2, P, PACK], BF16, name="w_i0", align_bytes=64),
-            keep.tile([P, 2, P, PACK], BF16, name="w_i1", tag="x_rows0", align_bytes=64),
-        ]
+        w_i = keep.tile([P, P, PACK, PACK], BF16, name="w_i", tag="x_rows0", align_bytes=64)
 
         def gather_plane(t):
             nc.vector.tensor_copy(out=w_listed[:, t * SLOTS : (t + 1) * SLOTS], in_=w_window[t][:].indirect(offsets[:]))
 
-        def turn_plane(t):
-            turned = psum.tile([P, 2, P], F32, name="turned", tag="grad", bufs=2)
-            words = w_listed[:, t * SLOTS : (t + 1) * SLOTS].bitcast(F32)
-            for u in range(2):
-                nc.tensor.transpose(turned[:, u, :], words[:, u::2], ident[:])
-            nc.scalar.copy(
-                out=w_i[t // 2][:, t % 2, :, :].rearrange("s p j -> s (p j)").bitcast(F32).rearrange("s (a i u) -> s a u i", i=2, u=2),
-                in_=turned[:].rearrange("s u (a i) -> s a u i", i=2),
-            )
+        def turn_first_planes():
+            turned = psum.tile([P, PACK, P], F32, name="turned", tag="grad", bufs=2)
+            words = w_listed[:].bitcast(F32)
+            for t in range(2):
+                for u in range(2):
+                    first = t * SLOTS // 2 + u
+                    nc.tensor.transpose(turned[:, 2 * t + u, :], words[:, first : (t + 1) * SLOTS // 2 : 2], ident[:])
+            lines = w_i[:].rearrange("s p t j -> s (p t j)").bitcast(F32).rearrange("s (p h k) -> s p h k", h=2, k=PACK)
+            nc.scalar.copy(out=lines[:, :, 0, :], in_=turned[:].rearrange("s k p -> s p k"))
 
         def turn_last_planes():
             turned = psum.tile([P, PACK, P], F32, name="turned", tag="grad", bufs=2)
@@ -148,16 +141,13 @@ def tile_attend_gwel_x_ts_kernel(tc, xT, wT, y, wt, ts, offs, out):
                 nc.tensor.transpose(turned[:, j, :], words[:, 2 * j * P + 1 : 2 * (j + 1) * P : 2], ident[:])
             halves = turned[:].rearrange("s j p -> s (j p)").bitcast(BF16)
             nc.scalar.copy(
-                out=w_i[1][:].rearrange("s e (a i) j -> s a j i e", i=2),
-                in_=halves.rearrange("s (j a i e) -> s a j i e", j=PACK, i=2, e=2),
+                out=w_i[:, :, 2:, :].rearrange("s p e j -> s p j e"),
+                in_=halves.rearrange("s (j p e) -> s p j e", j=PACK, e=2),
             )
 
-        def quantize_turned(u):
-            cols = slice(2 * u * P, 2 * (u + 1) * P)
+        def quantize_turned():
             nc.vector.quantize_mx(
-                out=wi_codes[:, cols].bitcast(E4M3X4),
-                scales=wi_scales[:, cols],
-                in_=w_i[u][:].rearrange("s e p j -> s (e p j)"),
+                out=wi_codes[:].bitcast(E4M3X4), scales=wi_scales[:], in_=w_i[:].rearrange("s p t j -> s (p t j)")
             )
 
         x_bf, x_codes, x_scales, y_dealt = ({} for i in range(4))
@@ -197,16 +187,40 @@ def tile_attend_gwel_x_ts_kernel(tc, xT, wT, y, wt, ts, offs, out):
                 prepare_rows(c)
 
         def deal_targets(c):
-            y_dealt[c] = keep.tile([P, SLOTS], F32, name="y_dealt", tag=DEALT_TAGS[c], align_bytes=64)
-            copy = nc.scalar.copy if c in DEALT_ON_SCALAR else nc.vector.tensor_copy
-            copy(
-                out=y_dealt[c][:].rearrange("r (v e a i) -> r a v i e", v=2, e=2, i=4),
-                in_=y_raw[c].rearrange("r (a i v e) -> r a v i e", v=2, e=2, i=4),
-            )
+            count = 2 if c == 0 else 1
+            dealt = keep.tile([P, count * SLOTS], F32, name="y_dealt", tag=DEALT_TAGS[(c + count - 1) % 2], align_bytes=64)
+            for e in range(count):
+                y_dealt[c + e] = dealt[:, e * SLOTS : (e + 1) * SLOTS]
+                nc.vector.tensor_copy(
+                    out=y_dealt[c + e].rearrange("r (v e a i) -> r a v i e", v=2, e=2, i=4),
+                    in_=y_raw[c + e].rearrange("r (a i v e) -> r a v i e", v=2, e=2, i=4),
+                )
 
         def deal_later(c):
-            if c > 1:
+            if c > 1 and c not in SUMMED_ON_VECTOR:
                 deal_targets(c)
+
+        def add_targets(c):
+            y_dealt[c] = keep.tile([P, SLOTS], F32, name="y_dealt", tag=DEALT_TAGS[c % 2], align_bytes=64)
+            nc.vector.tensor_tensor(
+                out=y_dealt[c][:].rearrange("r (j a i) -> r a j i", j=PACK, i=2),
+                in0=scaled[c][:].rearrange("r (j a i) -> r a j i", j=PACK, i=2),
+                in1=y_raw[c].rearrange("r (a i j) -> r a j i", j=PACK, i=2),
+                op=ADD,
+            )
+
+        def turn_residual(c):
+            if c not in SUMMED_ON_VECTOR:
+                turn_scores(c)
+                return
+            add_targets(c)
+            resid[c] = psum.tile([P, PACK, P], F32, name="resid", tag="resid", bufs=4)
+            for j in range(PACK):
+                nc.tensor.transpose(resid[c][:, j, :], y_dealt[c][:, j * P : (j + 1) * P], ident[:])
+
+        def turn_later(c):
+            if c not in SUMMED_ON_VECTOR:
+                turn_targets(c)
 
         def multiply_scores(c):
             score[c] = psum.tile([P, SLOTS], F32, name="score", tag="score", bufs=2)
@@ -283,10 +297,7 @@ def tile_attend_gwel_x_ts_kernel(tc, xT, wT, y, wt, ts, offs, out):
 
         def store_gradient(c):
             result = work.tile([P, FEATS], F32, name="result")
-            nc.scalar.copy(
-                out=result[:].rearrange("r (a i t) -> r a t i", i=2, t=PACK),
-                in_=grad[c][:].rearrange("r (t a i) -> r a t i", i=2, t=PACK),
-            )
+            nc.scalar.copy(out=result[:], in_=grad[c][:])
             nc.sync.dma_start(out=out[0, c * P : (c + 1) * P, :], in_=result[:])
 
         for j in range(PACK):
@@ -294,7 +305,6 @@ def tile_attend_gwel_x_ts_kernel(tc, xT, wT, y, wt, ts, offs, out):
         nc.scalar.copy(out=nts_row[:], in_=ts_spread[:].rearrange("r j s -> r (j s)"))
         for t in range(2):
             gather_plane(t)
-            turn_plane(t)
         nc.vector.tensor_copy(
             out=w_d[:, :, :2].rearrange("p (j s) t -> p j s t", j=PACK),
             in_=w_listed[:].rearrange("p (t s j) -> p j s t", t=2, j=PACK),
@@ -312,15 +322,13 @@ def tile_attend_gwel_x_ts_kernel(tc, xT, wT, y, wt, ts, offs, out):
         multiply_scores(1)
         deal_targets(0)
         turn_targets(0)
+        turn_first_planes()
         turn_last_planes()
-        wi_codes = keep.tile([P, FEATS], U32, name="wi_codes", tag="x_bf0", align_bytes=64)
-        quantize_turned(0)
-        deal_targets(1)
         cast_x(2)
 
         pipeline = (
             (scale_scores, 0),
-            (turn_scores, 0),
+            (turn_residual, 0),
             (square_residual, 0),
             (exponentiate, 0),
             (quantize_h, -LAG - 1),
@@ -328,7 +336,7 @@ def tile_attend_gwel_x_ts_kernel(tc, xT, wT, y, wt, ts, offs, out):
             (first_rows, 2),
             (multiply_scores, 2),
             (deal_later, 1),
-            (turn_targets, 1),
+            (turn_later, 1),
             (form_h, -LAG),
             (weigh_residual, -1),
             (store_gradient, -LAG - 1),
@@ -338,5 +346,6 @@ def tile_attend_gwel_x_ts_kernel(tc, xT, wT, y, wt, ts, offs, out):
             for stage, shift in pipeline:
                 if 0 <= step + shift < CHUNKS:
                     stage(step + shift)
-            if step == 0:
-                quantize_turned(1)
+            if step == 1:
+                wi_codes = keep.tile([P, FEATS], U32, name="wi_codes", align_bytes=64)
+                quantize_turned()

@@ -23,8 +23,12 @@ ROWS = 1024
 CHUNKS = ROWS // P
 QUAD = 32
 LAG = 2
-DEALT_TAGS = ["x_codes0", "x_bf0"]
-SUMMED_ON_VECTOR = ()
+DEALT_TAGS = {0: "x_bf0", 1: "x_codes0", 2: "x_bf0", 3: "x_codes0", 4: "weighted0", 5: "weighted1", 6: "weighted2", 7: "weighted3"}
+CAST_TAGS = {0: "x_bf0", 2: "x_bf2", 4: "scaled1", 6: "scaled2"}
+CAST_ON_POOL = ()
+DEALT_ON_SCALAR = ()
+DEALT_ON_POOL = (4, 5, 6, 7)
+LAST_PIECES = 2
 ROW_GROUPS = {0: 2, 2: 2, 4: 2, 6: 2}
 
 FLOPS = 2 * 2 * ROWS * SLOTS * FEATS
@@ -92,11 +96,11 @@ def tile_attend_gwel_x_ts_kernel(tc, xT, wT, y, wt, ts, offs, out):
         wt_row = keep.tile([P, ROWS], F32, name="wt_row")
         wt_lines = wt_row[:].rearrange("s (p b k) -> s p b k", b=CHUNKS // PACK, k=PACK)
         for b in range(CHUNKS // PACK):
-            bank = psum.tile([P, PACK, P], F32, name="spread", tag="resid", bufs=4)
+            bank = psum.tile([P, P, PACK], F32, name="spread", tag="resid", bufs=4)
             for k in range(PACK):
                 col = PACK * b + k
-                nc.tensor.transpose(bank[:, k, :], wt_runs[:, col : col + 1].to_broadcast([P, P]), ident[:])
-            nc.scalar.copy(out=wt_lines[:, :, b, :], in_=bank[:].rearrange("s k p -> s p k"))
+                nc.tensor.transpose(bank[:, :, k], wt_runs[:, col : col + 1].to_broadcast([P, P]), ident[:])
+            nc.scalar.copy(out=wt_lines[:, :, b, :], in_=bank[:])
 
         ts_listed = keep.tile([P, SLOTS], F32, name="ts_listed")
         nc.vector.tensor_copy(out=ts_listed[:], in_=ts_window[:].indirect(offsets[:]))
@@ -125,24 +129,24 @@ def tile_attend_gwel_x_ts_kernel(tc, xT, wT, y, wt, ts, offs, out):
             nc.vector.tensor_copy(out=w_listed[:, t * SLOTS : (t + 1) * SLOTS], in_=w_window[t][:].indirect(offsets[:]))
 
         def turn_first_planes():
-            turned = psum.tile([P, PACK, P], F32, name="turned", tag="grad", bufs=2)
+            turned = psum.tile([P, P, PACK], F32, name="turned", tag="grad", bufs=2)
             words = w_listed[:].bitcast(F32)
             for t in range(2):
                 for u in range(2):
                     first = t * SLOTS // 2 + u
-                    nc.tensor.transpose(turned[:, 2 * t + u, :], words[:, first : (t + 1) * SLOTS // 2 : 2], ident[:])
+                    nc.tensor.transpose(turned[:, :, 2 * t + u], words[:, first : (t + 1) * SLOTS // 2 : 2], ident[:])
             lines = w_i[:].rearrange("s p t j -> s (p t j)").bitcast(F32).rearrange("s (p h k) -> s p h k", h=2, k=PACK)
-            nc.scalar.copy(out=lines[:, :, 0, :], in_=turned[:].rearrange("s k p -> s p k"))
+            nc.scalar.copy(out=lines[:, :, 0, :], in_=turned[:])
 
         def turn_last_planes():
-            turned = psum.tile([P, PACK, P], F32, name="turned", tag="grad", bufs=2)
+            turned = psum.tile([P, P, PACK], F32, name="turned", tag="grad", bufs=2)
             words = w_d[:].rearrange("p i t -> p (i t)").bitcast(F32)
             for j in range(PACK):
-                nc.tensor.transpose(turned[:, j, :], words[:, 2 * j * P + 1 : 2 * (j + 1) * P : 2], ident[:])
-            halves = turned[:].rearrange("s j p -> s (j p)").bitcast(BF16)
+                nc.tensor.transpose(turned[:, :, j], words[:, 2 * j * P + 1 : 2 * (j + 1) * P : 2], ident[:])
+            halves = turned[:].rearrange("s p j -> s (p j)").bitcast(BF16)
             nc.scalar.copy(
                 out=w_i[:, :, 2:, :].rearrange("s p e j -> s p j e"),
-                in_=halves.rearrange("s (j p e) -> s p j e", j=PACK, e=2),
+                in_=halves.rearrange("s (p j e) -> s p j e", j=PACK, e=2),
             )
 
         def quantize_turned():
@@ -155,8 +159,18 @@ def tile_attend_gwel_x_ts_kernel(tc, xT, wT, y, wt, ts, offs, out):
 
         def cast_x(c):
             count = ROW_GROUPS[c]
-            tag = {0: "x_bf0", 2: "x_bf2", 4: "scaled1", 6: "scaled2"}[c]
+            tag = CAST_TAGS[c]
             x_bf[c] = keep.tile([P, count * P, PACK], BF16, name="x_bf", tag=tag, align_bytes=64)
+            if c in CAST_ON_POOL:
+                nc.gpsimd.tensor_scalar(
+                    out=x_bf[c][:],
+                    in0=x_raw[c][:, :, : count * P].rearrange("p t r -> p r t"),
+                    scalar1=1.0,
+                    scalar2=0.0,
+                    op0=MULT,
+                    op1=ADD,
+                )
+                return
             nc.scalar.copy(
                 out=x_bf[c][:].rearrange("p (a i) t -> p a t i", i=2),
                 in_=x_raw[c][:, :, : count * P].rearrange("p t (a i) -> p a t i", i=2),
@@ -187,40 +201,27 @@ def tile_attend_gwel_x_ts_kernel(tc, xT, wT, y, wt, ts, offs, out):
                 prepare_rows(c)
 
         def deal_targets(c):
-            count = 2 if c == 0 else 1
-            dealt = keep.tile([P, count * SLOTS], F32, name="y_dealt", tag=DEALT_TAGS[(c + count - 1) % 2], align_bytes=64)
-            for e in range(count):
-                y_dealt[c + e] = dealt[:, e * SLOTS : (e + 1) * SLOTS]
-                nc.vector.tensor_copy(
-                    out=y_dealt[c + e].rearrange("r (v e a i) -> r a v i e", v=2, e=2, i=4),
-                    in_=y_raw[c + e].rearrange("r (a i v e) -> r a v i e", v=2, e=2, i=4),
-                )
-
-        def deal_later(c):
-            if c > 1 and c not in SUMMED_ON_VECTOR:
-                deal_targets(c)
-
-        def add_targets(c):
-            y_dealt[c] = keep.tile([P, SLOTS], F32, name="y_dealt", tag=DEALT_TAGS[c % 2], align_bytes=64)
-            nc.vector.tensor_tensor(
-                out=y_dealt[c][:].rearrange("r (j a i) -> r a j i", j=PACK, i=2),
-                in0=scaled[c][:].rearrange("r (j a i) -> r a j i", j=PACK, i=2),
-                in1=y_raw[c].rearrange("r (a i j) -> r a j i", j=PACK, i=2),
-                op=ADD,
-            )
-
-        def turn_residual(c):
-            if c not in SUMMED_ON_VECTOR:
-                turn_scores(c)
-                return
-            add_targets(c)
-            resid[c] = psum.tile([P, PACK, P], F32, name="resid", tag="resid", bufs=4)
-            for j in range(PACK):
-                nc.tensor.transpose(resid[c][:, j, :], y_dealt[c][:, j * P : (j + 1) * P], ident[:])
-
-        def turn_later(c):
-            if c not in SUMMED_ON_VECTOR:
-                turn_targets(c)
+            y_dealt[c] = keep.tile([P, SLOTS], F32, name="y_dealt", tag=DEALT_TAGS[c], align_bytes=64)
+            for e in range(1):
+                if c in DEALT_ON_SCALAR:
+                    nc.scalar.copy(
+                        out=y_dealt[c][:].rearrange("r (j a i) -> r a j i", j=PACK, i=2),
+                        in_=y_raw[c].rearrange("r (a i j) -> r a j i", j=PACK, i=2),
+                    )
+                elif c in DEALT_ON_POOL:
+                    nc.gpsimd.tensor_scalar(
+                        out=y_dealt[c][:].rearrange("r (j a i) -> r a j i", j=PACK, i=PACK),
+                        in0=y_raw[c].rearrange("r (a i j) -> r a j i", j=PACK, i=PACK),
+                        scalar1=1.0,
+                        scalar2=0.0,
+                        op0=MULT,
+                        op1=ADD,
+                    )
+                else:
+                    nc.vector.tensor_copy(
+                        out=y_dealt[c][:].rearrange("r (v e a i) -> r a v i e", v=2, e=2, i=4),
+                        in_=y_raw[c].rearrange("r (a i v e) -> r a v i e", v=2, e=2, i=4),
+                    )
 
         def multiply_scores(c):
             score[c] = psum.tile([P, SLOTS], F32, name="score", tag="score", bufs=2)
@@ -262,7 +263,7 @@ def tile_attend_gwel_x_ts_kernel(tc, xT, wT, y, wt, ts, offs, out):
             nc.scalar.activation(out=bell[c][:], in_=square[c][:], func=ACT.Exp, scale=-0.5)
 
         def weigh_residual(c):
-            weighted[c] = work.tile([P, PACK, P], F32, name="weighted", bufs=LAG + 2)
+            weighted[c] = keep.tile([P, PACK, P], F32, name="weighted", tag="weighted%d" % c, align_bytes=64)
             nc.vector.tensor_tensor(
                 out=weighted[c][:], in0=resid[c][:], in1=factor[:, :, c * P : (c + 1) * P], op=MULT
             )
@@ -296,9 +297,13 @@ def tile_attend_gwel_x_ts_kernel(tc, xT, wT, y, wt, ts, offs, out):
             )
 
         def store_gradient(c):
-            result = work.tile([P, FEATS], F32, name="result")
-            nc.scalar.copy(out=result[:], in_=grad[c][:])
-            nc.sync.dma_start(out=out[0, c * P : (c + 1) * P, :], in_=result[:])
+            pieces = LAST_PIECES if c == CHUNKS - 1 else 1
+            width = FEATS // pieces
+            for piece in range(pieces):
+                cols = slice(piece * width, (piece + 1) * width)
+                result = keep.tile([P, width], F32, name="result%d_%d" % (c, piece))
+                nc.scalar.copy(out=result[:], in_=grad[c][:, cols])
+                nc.sync.dma_start(out=out[0, c * P : (c + 1) * P, cols], in_=result[:])
 
         for j in range(PACK):
             make_factor(j)
@@ -328,15 +333,15 @@ def tile_attend_gwel_x_ts_kernel(tc, xT, wT, y, wt, ts, offs, out):
 
         pipeline = (
             (scale_scores, 0),
-            (turn_residual, 0),
+            (turn_scores, 0),
             (square_residual, 0),
             (exponentiate, 0),
             (quantize_h, -LAG - 1),
             (multiply_gradient, -LAG - 1),
             (first_rows, 2),
             (multiply_scores, 2),
-            (deal_later, 1),
-            (turn_later, 1),
+            (deal_targets, 1),
+            (turn_targets, 1),
             (form_h, -LAG),
             (weigh_residual, -1),
             (store_gradient, -LAG - 1),
@@ -347,5 +352,5 @@ def tile_attend_gwel_x_ts_kernel(tc, xT, wT, y, wt, ts, offs, out):
                 if 0 <= step + shift < CHUNKS:
                     stage(step + shift)
             if step == 1:
-                wi_codes = keep.tile([P, FEATS], U32, name="wi_codes", align_bytes=64)
+                wi_codes = keep.tile([P, FEATS], U32, name="wi_codes", tag="x_bf2", align_bytes=64)
                 quantize_turned()

@@ -22,14 +22,15 @@ FEATS = 512
 ROWS = 1024
 CHUNKS = ROWS // P
 QUAD = 32
-LAG = 2
-DEALT_TAGS = {0: "x_bf0", 1: "x_codes0", 2: "x_bf0", 3: "x_codes0", 4: "weighted0", 5: "weighted1", 6: "weighted2", 7: "weighted3"}
-CAST_TAGS = {0: "x_bf0", 2: "x_bf2", 4: "scaled1", 6: "scaled2"}
+LAG = 3
+DEALT_TAGS = {0: "x_bf0", 1: "x_codes1", 2: "x_bf0", 3: "x_rows0", 4: "dealt4", 5: "dealt5", 6: "weighted0", 7: "weighted1"}
+CAST_TAGS = {0: "x_bf0", 1: "x_bf1", 2: "x_bf2", 4: "scaled1", 6: "scaled2"}
 CAST_ON_POOL = ()
 DEALT_ON_SCALAR = ()
-DEALT_ON_POOL = (4, 5, 6, 7)
+DEALT_ON_POOL = (3, 4, 5, 6, 7)
 LAST_PIECES = 2
-ROW_GROUPS = {0: 2, 2: 2, 4: 2, 6: 2}
+STORED_BY_VECTOR = (6,)
+ROW_GROUPS = {0: 1, 1: 1, 2: 2, 4: 2, 6: 2}
 
 FLOPS = 2 * 2 * ROWS * SLOTS * FEATS
 BYTES = 4 * (FEATS * ROWS + FEATS * ITEMS + ROWS * SLOTS + ROWS + ITEMS + ROWS * FEATS) + 2 * P * SLOTS // 16
@@ -96,7 +97,7 @@ def tile_attend_gwel_x_ts_kernel(tc, xT, wT, y, wt, ts, offs, out):
         wt_row = keep.tile([P, ROWS], F32, name="wt_row")
         wt_lines = wt_row[:].rearrange("s (p b k) -> s p b k", b=CHUNKS // PACK, k=PACK)
         for b in range(CHUNKS // PACK):
-            bank = psum.tile([P, P, PACK], F32, name="spread", tag="resid", bufs=4)
+            bank = psum.tile([P, P, PACK], F32, name="spread", tag="resid", bufs=3)
             for k in range(PACK):
                 col = PACK * b + k
                 nc.tensor.transpose(bank[:, :, k], wt_runs[:, col : col + 1].to_broadcast([P, P]), ident[:])
@@ -104,12 +105,12 @@ def tile_attend_gwel_x_ts_kernel(tc, xT, wT, y, wt, ts, offs, out):
 
         ts_listed = keep.tile([P, SLOTS], F32, name="ts_listed")
         nc.vector.tensor_copy(out=ts_listed[:], in_=ts_window[:].indirect(offsets[:]))
-        ts_turned = psum.tile([P, PACK, P], F32, name="ts_turned", tag="resid", bufs=4)
+        ts_turned = psum.tile([P, PACK, P], F32, name="ts_turned", tag="resid", bufs=3)
         for j in range(PACK):
             nc.tensor.transpose(ts_turned[:, j, :], ts_listed[:, j::PACK], ident[:])
         nts_col = keep.tile([P, PACK], F32, name="nts_col")
         nc.scalar.activation(out=nts_col[:], in_=ts_turned[:, :, 0], func=ACT.Copy, scale=-1.0)
-        ts_spread = psum.tile([P, PACK, P], F32, name="ts_spread", tag="resid", bufs=4)
+        ts_spread = psum.tile([P, PACK, P], F32, name="ts_spread", tag="resid", bufs=3)
         for j in range(PACK):
             nc.tensor.transpose(ts_spread[:, j, :], nts_col[:, j : j + 1].to_broadcast([P, P]), ident[:])
         factor = keep.tile([P, PACK, ROWS], F32, name="factor")
@@ -240,7 +241,7 @@ def tile_attend_gwel_x_ts_kernel(tc, xT, wT, y, wt, ts, offs, out):
             nc.vector.tensor_tensor(out=scaled[c][:], in0=score[c][:], in1=nts_row[:], op=MULT)
 
         def turn_targets(c):
-            resid[c] = psum.tile([P, PACK, P], F32, name="resid", tag="resid", bufs=4)
+            resid[c] = psum.tile([P, PACK, P], F32, name="resid", tag="resid", bufs=3)
             for j in range(PACK):
                 nc.tensor.matmul(
                     resid[c][:, j, :], y_dealt[c][:, j * P : (j + 1) * P], ident[:],
@@ -302,8 +303,10 @@ def tile_attend_gwel_x_ts_kernel(tc, xT, wT, y, wt, ts, offs, out):
             for piece in range(pieces):
                 cols = slice(piece * width, (piece + 1) * width)
                 result = keep.tile([P, width], F32, name="result%d_%d" % (c, piece))
-                nc.scalar.copy(out=result[:], in_=grad[c][:, cols])
-                nc.sync.dma_start(out=out[0, c * P : (c + 1) * P, cols], in_=result[:])
+                copy = nc.vector.tensor_copy if c in STORED_BY_VECTOR else nc.scalar.copy
+                copy(out=result[:], in_=grad[c][:, cols])
+                queue = nc.scalar if c == CHUNKS - 1 else nc.sync
+                queue.dma_start(out=out[0, c * P : (c + 1) * P, cols], in_=result[:])
 
         for j in range(PACK):
             make_factor(j)
@@ -319,11 +322,13 @@ def tile_attend_gwel_x_ts_kernel(tc, xT, wT, y, wt, ts, offs, out):
                 out=w_d[:, :, t].rearrange("p (j s) -> p s j", j=PACK), in_=w_window[t][:].indirect(offsets[:])
             )
         cast_x(0)
+        cast_x(1)
         nc.vector.quantize_mx(
             out=wd_codes[:].bitcast(E4M3X4), scales=wd_scales[:], in_=w_d[:].rearrange("p i t -> p (i t)")
         )
         quantize_x(0)
         multiply_scores(0)
+        quantize_x(1)
         multiply_scores(1)
         deal_targets(0)
         turn_targets(0)
@@ -351,6 +356,6 @@ def tile_attend_gwel_x_ts_kernel(tc, xT, wT, y, wt, ts, offs, out):
             for stage, shift in pipeline:
                 if 0 <= step + shift < CHUNKS:
                     stage(step + shift)
-            if step == 1:
+            if step == 0:
                 wi_codes = keep.tile([P, FEATS], U32, name="wi_codes", tag="x_bf2", align_bytes=64)
                 quantize_turned()

@@ -101,7 +101,7 @@ def tile_attend_gwel_x_ts_kernel(tc, xT, wT, y, wt, ts, offs, out):
             for k in range(PACK):
                 col = PACK * b + k
                 nc.tensor.transpose(bank[:, :, k], wt_runs[:, col : col + 1].to_broadcast([P, P]), ident[:])
-            nc.scalar.copy(out=wt_lines[:, :, b, :], in_=bank[:])
+            nc.scalar.activation(out=wt_lines[:, :, b, :], in_=bank[:], func=ACT.Copy)
 
         ts_listed = keep.tile([P, SLOTS], F32, name="ts_listed")
         nc.vector.tensor_copy(out=ts_listed[:], in_=ts_window[:].indirect(offsets[:]))
@@ -172,9 +172,10 @@ def tile_attend_gwel_x_ts_kernel(tc, xT, wT, y, wt, ts, offs, out):
                     op1=ADD,
                 )
                 return
-            nc.scalar.copy(
+            nc.scalar.activation(
                 out=x_bf[c][:].rearrange("p (a i) t -> p a t i", i=2),
                 in_=x_raw[c][:, :, : count * P].rearrange("p t (a i) -> p a t i", i=2),
+                func=ACT.Copy,
             )
 
         def quantize_x(c):
@@ -303,14 +304,16 @@ def tile_attend_gwel_x_ts_kernel(tc, xT, wT, y, wt, ts, offs, out):
             for piece in range(pieces):
                 cols = slice(piece * width, (piece + 1) * width)
                 result = keep.tile([P, width], F32, name="result%d_%d" % (c, piece))
-                copy = nc.vector.tensor_copy if c in STORED_BY_VECTOR else nc.scalar.copy
-                copy(out=result[:], in_=grad[c][:, cols])
+                if c in STORED_BY_VECTOR:
+                    nc.vector.tensor_copy(out=result[:], in_=grad[c][:, cols])
+                else:
+                    nc.scalar.activation(out=result[:], in_=grad[c][:, cols], func=ACT.Copy)
                 queue = nc.scalar if c == CHUNKS - 1 else nc.sync
                 queue.dma_start(out=out[0, c * P : (c + 1) * P, cols], in_=result[:])
 
         for j in range(PACK):
             make_factor(j)
-        nc.scalar.copy(out=nts_row[:], in_=ts_spread[:].rearrange("r j s -> r (j s)"))
+        nc.scalar.activation(out=nts_row[:], in_=ts_spread[:].rearrange("r j s -> r (j s)"), func=ACT.Copy)
         for t in range(2):
             gather_plane(t)
         nc.vector.tensor_copy(

@@ -22,14 +22,11 @@ FEATS = 512
 ROWS = 1024
 CHUNKS = ROWS // P
 QUAD = 32
+DEALT = (0, 1)
+WEIGHED_ON_POOL = ()
+STORED_BY_VECTOR = ()
+LATE = 5
 LAG = 3
-DEALT_TAGS = {0: "x_bf0", 1: "x_codes1", 2: "x_bf0", 3: "x_rows0", 4: "dealt4", 5: "dealt5", 6: "weighted0", 7: "weighted1"}
-CAST_TAGS = {0: "x_bf0", 1: "x_bf1", 2: "x_bf2", 4: "scaled1", 6: "scaled2"}
-CAST_ON_POOL = ()
-DEALT_ON_SCALAR = ()
-DEALT_ON_POOL = (3, 4, 5, 6, 7)
-LAST_PIECES = 2
-STORED_BY_VECTOR = (6,)
 ROW_GROUPS = {0: 1, 1: 1, 2: 2, 4: 2, 6: 2}
 
 FLOPS = 2 * 2 * ROWS * SLOTS * FEATS
@@ -52,18 +49,18 @@ def tile_attend_gwel_x_ts_kernel(tc, xT, wT, y, wt, ts, offs, out):
         ts_window = keep.tile([P, ITEMS], F32, name="ts_window", tag="stage1", align_bytes=64)
 
         ones = keep.tile([P, QUAD], F32, name="ones")
-        nc.gpsimd.memset(ones[:], 1.0)
+        nc.vector.memset(ones[:], 1.0)
         ident = keep.tile([P, P], F32, name="ident")
-        nc.gpsimd.memset(ident[:], 0.0)
-        nc.gpsimd.memset(ts_window[:, : ITEMS // 2], 0.0)
+        nc.vector.memset(ident[:], 0.0)
         column = keep.tile([P, QUAD], F32, name="column", align_bytes=64)
         nc.vector.tensor_tensor_scan(out=column[:], data0=ones[:], data1=ones[:], initial=0.0, op0=MULT, op1=ADD)
+        nc.vector.memset(ts_window[:, : ITEMS // 2], 0.0)
         row = keep.tile([P, QUAD], F32, name="row", align_bytes=64)
         nc.vector.transpose(out=row[:], in_=column[:])
+        nc.vector.memset(ts_window[:, ITEMS // 2 :], 0.0)
         for q in range(P // QUAD):
             band = slice(q * QUAD, (q + 1) * QUAD)
             nc.vector.tensor_tensor(out=ident[band, band], in0=column[band, :], in1=row[band, :], op=IS_EQUAL)
-        nc.vector.memset(ts_window[:, ITEMS // 2 :], 0.0)
         nc.vector.tensor_copy(out=ts_window[0:1, :], in_=ts_row[:])
 
         w_planes = wT.rearrange("(p t) n -> t p n", t=PACK)
@@ -84,70 +81,91 @@ def tile_attend_gwel_x_ts_kernel(tc, xT, wT, y, wt, ts, offs, out):
             for e in range(2):
                 x_raw[first + e] = raw[:, :, e * P :]
 
-        def load_y(first):
-            raw = keep.tile([P, 2, SLOTS], F32, name="y_raw", tag="y_rows%d" % first, align_bytes=64)
-            nc.sync.dma_start(out=raw[:], in_=y_view[:, first : first + 2, :])
-            for e in range(2):
+        def load_y(first, count):
+            raw = keep.tile([P, count, SLOTS], F32, name="y_raw", tag="y_rows%d" % first, align_bytes=64)
+            nc.sync.dma_start(out=raw[:], in_=y_view[:, first : first + count, :])
+            for e in range(count):
                 y_raw[first + e] = raw[:, e, :]
 
-        for first in range(0, CHUNKS, 2):
+        load_x(0)
+        load_x(2)
+        load_y(0, 1)
+        load_y(1, 1)
+        load_y(2, 2)
+        for first in range(4, CHUNKS, 2):
             load_x(first)
-            load_y(first)
+            load_y(first, 2)
 
         wt_row = keep.tile([P, ROWS], F32, name="wt_row")
         wt_lines = wt_row[:].rearrange("s (p b k) -> s p b k", b=CHUNKS // PACK, k=PACK)
         for b in range(CHUNKS // PACK):
-            bank = psum.tile([P, P, PACK], F32, name="spread", tag="resid", bufs=3)
+            bank = psum.tile([P, PACK, P], F32, name="spread", tag="resid", bufs=4)
             for k in range(PACK):
                 col = PACK * b + k
-                nc.tensor.transpose(bank[:, :, k], wt_runs[:, col : col + 1].to_broadcast([P, P]), ident[:])
-            nc.scalar.activation(out=wt_lines[:, :, b, :], in_=bank[:], func=ACT.Copy)
+                nc.tensor.transpose(bank[:, k, :], wt_runs[:, col : col + 1].to_broadcast([P, P]), ident[:])
+            nc.scalar.activation(out=wt_lines[:, :, b, :], in_=bank[:].rearrange("s k p -> s p k"), func=ACT.Copy)
 
-        ts_listed = keep.tile([P, SLOTS], F32, name="ts_listed")
-        nc.vector.tensor_copy(out=ts_listed[:], in_=ts_window[:].indirect(offsets[:]))
-        ts_turned = psum.tile([P, PACK, P], F32, name="ts_turned", tag="resid", bufs=3)
+        ts_dealt = keep.tile([P, SLOTS], F32, name="ts_dealt")
+        nc.vector.tensor_copy(
+            out=ts_dealt[:].rearrange("p (j s) -> p s j", j=PACK), in_=ts_window[:].indirect(offsets[:])
+        )
+        ts_turned = psum.tile([P, PACK, P], F32, name="ts_turned", tag="resid", bufs=4)
         for j in range(PACK):
-            nc.tensor.transpose(ts_turned[:, j, :], ts_listed[:, j::PACK], ident[:])
+            nc.tensor.transpose(ts_turned[:, j, :], ts_dealt[:, j * P : (j + 1) * P], ident[:])
         nts_col = keep.tile([P, PACK], F32, name="nts_col")
         nc.scalar.activation(out=nts_col[:], in_=ts_turned[:, :, 0], func=ACT.Copy, scale=-1.0)
-        ts_spread = psum.tile([P, PACK, P], F32, name="ts_spread", tag="resid", bufs=3)
+        ts_spread = psum.tile([P, PACK, P], F32, name="ts_spread", tag="resid", bufs=4)
         for j in range(PACK):
             nc.tensor.transpose(ts_spread[:, j, :], nts_col[:, j : j + 1].to_broadcast([P, P]), ident[:])
         factor = keep.tile([P, PACK, ROWS], F32, name="factor")
         nts_row = keep.tile([P, SLOTS], F32, name="nts_row")
-
-        def make_factor(j):
+        for j in range(PACK):
             nc.scalar.activation(out=factor[:, j, :], in_=wt_row[:], func=ACT.Copy, scale=nts_col[:, j : j + 1])
+        nc.scalar.activation(out=nts_row[:], in_=ts_spread[:].rearrange("r j s -> r (j s)"), func=ACT.Copy)
 
         w_d = keep.tile([P, SLOTS, PACK], BF16, name="w_d", align_bytes=64)
-        wi_scales = keep.tile([P, FEATS], U8, name="wi_scales", align_bytes=64)
         wd_codes = keep.tile([P, SLOTS], U32, name="wd_codes", align_bytes=64)
         wd_scales = keep.tile([P, SLOTS], U8, name="wd_scales", align_bytes=64)
-        w_listed = keep.tile([P, 2 * SLOTS], BF16, name="w_listed", tag="stage1", align_bytes=64)
+        wi_codes = keep.tile([P, FEATS], U32, name="wi_codes", align_bytes=64)
+        wi_scales = keep.tile([P, FEATS], U8, name="wi_scales", align_bytes=64)
+        w_paired = keep.tile([P, 2 * SLOTS], BF16, name="w_paired", tag="stage1", align_bytes=64)
         w_i = keep.tile([P, P, PACK, PACK], BF16, name="w_i", tag="x_rows0", align_bytes=64)
 
-        def gather_plane(t):
-            nc.vector.tensor_copy(out=w_listed[:, t * SLOTS : (t + 1) * SLOTS], in_=w_window[t][:].indirect(offsets[:]))
+        for t in range(2):
+            nc.vector.tensor_copy(out=w_paired[:, t * SLOTS : (t + 1) * SLOTS], in_=w_window[t][:].indirect(offsets[:]))
+        nc.vector.tensor_copy(
+            out=w_d[:, :, :2].rearrange("p (j s) t -> p j s t", j=PACK),
+            in_=w_paired[:].rearrange("p (t s j) -> p j s t", t=2, j=PACK),
+        )
+        for t in range(2, PACK):
+            nc.vector.tensor_copy(
+                out=w_d[:, :, t].rearrange("p (j s) -> p s j", j=PACK), in_=w_window[t][:].indirect(offsets[:])
+            )
+
+        first_turned = psum.tile([P, PACK, P], F32, name="turned", tag="grad", bufs=2)
+        last_turned = psum.tile([P, PACK, P], F32, name="turned", tag="grad", bufs=2)
 
         def turn_first_planes():
-            turned = psum.tile([P, P, PACK], F32, name="turned", tag="grad", bufs=2)
-            words = w_listed[:].bitcast(F32)
+            words = w_paired[:].bitcast(F32)
             for t in range(2):
                 for u in range(2):
                     first = t * SLOTS // 2 + u
-                    nc.tensor.transpose(turned[:, :, 2 * t + u], words[:, first : (t + 1) * SLOTS // 2 : 2], ident[:])
-            lines = w_i[:].rearrange("s p t j -> s (p t j)").bitcast(F32).rearrange("s (p h k) -> s p h k", h=2, k=PACK)
-            nc.scalar.copy(out=lines[:, :, 0, :], in_=turned[:])
+                    nc.tensor.transpose(first_turned[:, 2 * t + u, :], words[:, first : (t + 1) * SLOTS // 2 : 2], ident[:])
 
         def turn_last_planes():
-            turned = psum.tile([P, P, PACK], F32, name="turned", tag="grad", bufs=2)
             words = w_d[:].rearrange("p i t -> p (i t)").bitcast(F32)
             for j in range(PACK):
-                nc.tensor.transpose(turned[:, :, j], words[:, 2 * j * P + 1 : 2 * (j + 1) * P : 2], ident[:])
-            halves = turned[:].rearrange("s p j -> s (p j)").bitcast(BF16)
+                nc.tensor.transpose(last_turned[:, j, :], words[:, 2 * j * P + 1 : 2 * (j + 1) * P : 2], ident[:])
+
+        def copy_first_planes():
+            lines = w_i[:].rearrange("s p t j -> s (p t j)").bitcast(F32).rearrange("s (p h k) -> s p h k", h=2, k=PACK)
+            nc.scalar.copy(out=lines[:, :, 0, :], in_=first_turned[:].rearrange("s k p -> s p k"))
+
+        def copy_last_planes():
+            halves = last_turned[:].rearrange("s j p -> s (j p)").bitcast(BF16)
             nc.scalar.copy(
                 out=w_i[:, :, 2:, :].rearrange("s p e j -> s p j e"),
-                in_=halves.rearrange("s (p j e) -> s p j e", j=PACK, e=2),
+                in_=halves.rearrange("s (j p e) -> s p j e", j=PACK, e=2),
             )
 
         def quantize_turned():
@@ -155,23 +173,12 @@ def tile_attend_gwel_x_ts_kernel(tc, xT, wT, y, wt, ts, offs, out):
                 out=wi_codes[:].bitcast(E4M3X4), scales=wi_scales[:], in_=w_i[:].rearrange("s p t j -> s (p t j)")
             )
 
-        x_bf, x_codes, x_scales, y_dealt = ({} for i in range(4))
+        x_bf, x_codes, x_scales, summand = ({} for i in range(4))
         score, scaled, resid, square, bell, weighted, h, h_codes, h_scales, grad = ({} for i in range(10))
 
         def cast_x(c):
             count = ROW_GROUPS[c]
-            tag = CAST_TAGS[c]
-            x_bf[c] = keep.tile([P, count * P, PACK], BF16, name="x_bf", tag=tag, align_bytes=64)
-            if c in CAST_ON_POOL:
-                nc.gpsimd.tensor_scalar(
-                    out=x_bf[c][:],
-                    in0=x_raw[c][:, :, : count * P].rearrange("p t r -> p r t"),
-                    scalar1=1.0,
-                    scalar2=0.0,
-                    op0=MULT,
-                    op1=ADD,
-                )
-                return
+            x_bf[c] = keep.tile([P, count * P, PACK], BF16, name="x_bf%d" % c, align_bytes=64)
             nc.scalar.activation(
                 out=x_bf[c][:].rearrange("p (a i) t -> p a t i", i=2),
                 in_=x_raw[c][:, :, : count * P].rearrange("p t (a i) -> p a t i", i=2),
@@ -180,7 +187,7 @@ def tile_attend_gwel_x_ts_kernel(tc, xT, wT, y, wt, ts, offs, out):
 
         def quantize_x(c):
             count = ROW_GROUPS[c]
-            codes = keep.tile([P, count * P], U32, name="x_codes", tag="x_codes%d" % c, align_bytes=64)
+            codes = keep.tile([P, count * P], U32, name="x_codes%d" % c, align_bytes=64)
             scales = keep.tile([P, count * P], U8, name="x_scales%d" % c, align_bytes=64)
             nc.vector.quantize_mx(
                 out=codes[:].bitcast(E4M3X4), scales=scales[:], in_=x_bf[c][:].rearrange("p r t -> p (r t)")
@@ -189,41 +196,13 @@ def tile_attend_gwel_x_ts_kernel(tc, xT, wT, y, wt, ts, offs, out):
                 x_codes[c + e] = codes[:, e * P : (e + 1) * P]
                 x_scales[c + e] = scales[:, e * P : (e + 1) * P]
 
-        def prepare_rows(c):
-            if c in ROW_GROUPS:
-                cast_x(c)
-                quantize_x(c)
-
-        def first_rows(c):
-            if c == 2:
-                quantize_x(c)
-
-        def later_rows(c):
-            if c > 2:
-                prepare_rows(c)
-
         def deal_targets(c):
-            y_dealt[c] = keep.tile([P, SLOTS], F32, name="y_dealt", tag=DEALT_TAGS[c], align_bytes=64)
-            for e in range(1):
-                if c in DEALT_ON_SCALAR:
-                    nc.scalar.copy(
-                        out=y_dealt[c][:].rearrange("r (j a i) -> r a j i", j=PACK, i=2),
-                        in_=y_raw[c].rearrange("r (a i j) -> r a j i", j=PACK, i=2),
-                    )
-                elif c in DEALT_ON_POOL:
-                    nc.gpsimd.tensor_scalar(
-                        out=y_dealt[c][:].rearrange("r (j a i) -> r a j i", j=PACK, i=PACK),
-                        in0=y_raw[c].rearrange("r (a i j) -> r a j i", j=PACK, i=PACK),
-                        scalar1=1.0,
-                        scalar2=0.0,
-                        op0=MULT,
-                        op1=ADD,
-                    )
-                else:
-                    nc.vector.tensor_copy(
-                        out=y_dealt[c][:].rearrange("r (v e a i) -> r a v i e", v=2, e=2, i=4),
-                        in_=y_raw[c].rearrange("r (a i v e) -> r a v i e", v=2, e=2, i=4),
-                    )
+            if c in DEALT:
+                summand[c] = keep.tile([P, SLOTS], F32, name="summand%d" % c, align_bytes=64)
+                nc.vector.tensor_copy(
+                    out=summand[c][:].rearrange("r (v e a i) -> r a v i e", v=2, e=2, i=4),
+                    in_=y_raw[c].rearrange("r (a i v e) -> r a v i e", v=2, e=2, i=4),
+                )
 
         def multiply_scores(c):
             score[c] = psum.tile([P, SLOTS], F32, name="score", tag="score", bufs=2)
@@ -238,16 +217,14 @@ def tile_attend_gwel_x_ts_kernel(tc, xT, wT, y, wt, ts, offs, out):
             )
 
         def scale_scores(c):
-            scaled[c] = keep.tile([P, SLOTS], F32, name="scaled", tag="scaled%d" % (c % 3), align_bytes=64)
+            scaled[c] = work.tile([P, SLOTS], F32, name="scaled", align_bytes=64)
             nc.vector.tensor_tensor(out=scaled[c][:], in0=score[c][:], in1=nts_row[:], op=MULT)
 
         def turn_targets(c):
-            resid[c] = psum.tile([P, PACK, P], F32, name="resid", tag="resid", bufs=3)
+            resid[c] = psum.tile([P, PACK, P], F32, name="resid", tag="resid", bufs=4)
             for j in range(PACK):
-                nc.tensor.matmul(
-                    resid[c][:, j, :], y_dealt[c][:, j * P : (j + 1) * P], ident[:],
-                    start=(j == 0), stop=False, is_transpose=True,
-                )
+                source = summand[c][:, j * P : (j + 1) * P] if c in DEALT else y_raw[c][:, j::PACK]
+                nc.tensor.matmul(resid[c][:, j, :], source, ident[:], start=(j == 0), stop=False, is_transpose=True)
 
         def turn_scores(c):
             for j in range(PACK):
@@ -264,18 +241,27 @@ def tile_attend_gwel_x_ts_kernel(tc, xT, wT, y, wt, ts, offs, out):
             bell[c] = work.tile([P, PACK, P], F32, name="bell", bufs=LAG + 2)
             nc.scalar.activation(out=bell[c][:], in_=square[c][:], func=ACT.Exp, scale=-0.5)
 
+        def weigh_bell(c):
+            if c in WEIGHED_ON_POOL:
+                weighted[c] = work.tile([P, PACK, P], F32, name="weighted", bufs=LAG + 2, align_bytes=64)
+                nc.gpsimd.tensor_tensor(
+                    out=weighted[c][:], in0=bell[c][:], in1=factor[:, :, c * P : (c + 1) * P], op=MULT
+                )
+
         def weigh_residual(c):
-            weighted[c] = keep.tile([P, PACK, P], F32, name="weighted", tag="weighted%d" % c, align_bytes=64)
-            nc.vector.tensor_tensor(
-                out=weighted[c][:], in0=resid[c][:], in1=factor[:, :, c * P : (c + 1) * P], op=MULT
-            )
+            if c not in WEIGHED_ON_POOL:
+                weighted[c] = work.tile([P, PACK, P], F32, name="weighted", bufs=LAG + 2, align_bytes=64)
+                nc.vector.tensor_tensor(
+                    out=weighted[c][:], in0=resid[c][:], in1=factor[:, :, c * P : (c + 1) * P], op=MULT
+                )
 
         def form_h(c):
+            other = resid[c] if c in WEIGHED_ON_POOL else bell[c]
             h[c] = work.tile([P, P, PACK], BF16, name="h", align_bytes=64)
             nc.vector.tensor_tensor(
                 out=h[c][:].rearrange("s (a i) j -> s a j i", i=2),
-                in0=weighted[c][:].rearrange("s j (a i) -> s a j i", i=2),
-                in1=bell[c][:].rearrange("s j (a i) -> s a j i", i=2),
+                in0=other[:].rearrange("s j (a i) -> s a j i", i=2),
+                in1=weighted[c][:].rearrange("s j (a i) -> s a j i", i=2),
                 op=MULT,
             )
 
@@ -286,79 +272,100 @@ def tile_attend_gwel_x_ts_kernel(tc, xT, wT, y, wt, ts, offs, out):
                 out=h_codes[c][:].bitcast(E5M2X4), scales=h_scales[c][:], in_=h[c][:].rearrange("s r j -> s (r j)")
             )
 
-        def multiply_gradient(c):
-            grad[c] = psum.tile([P, FEATS], F32, name="grad", tag="grad", bufs=2)
+        def multiply_columns(c, bank, cols):
             nc.tensor.matmul_mx(
-                out=grad[c][:],
+                out=bank[:],
                 lhsT=h_codes[c][:].bitcast(E5M2X4),
                 lhsT_scale=h_scales[c][:],
-                rhs=wi_codes[:].bitcast(E4M3X4),
-                rhs_scale=wi_scales[:],
+                rhs=wi_codes[:, cols].bitcast(E4M3X4),
+                rhs_scale=wi_scales[:, cols],
                 start=True,
                 stop=True,
             )
 
-        def store_gradient(c):
-            pieces = LAST_PIECES if c == CHUNKS - 1 else 1
-            width = FEATS // pieces
-            for piece in range(pieces):
-                cols = slice(piece * width, (piece + 1) * width)
-                result = keep.tile([P, width], F32, name="result%d_%d" % (c, piece))
-                if c in STORED_BY_VECTOR:
-                    nc.vector.tensor_copy(out=result[:], in_=grad[c][:, cols])
-                else:
-                    nc.scalar.activation(out=result[:], in_=grad[c][:, cols], func=ACT.Copy)
-                queue = nc.scalar if c == CHUNKS - 1 else nc.sync
-                queue.dma_start(out=out[0, c * P : (c + 1) * P, cols], in_=result[:])
+        def multiply_gradient(c):
+            tag = "score" if c >= LATE else "grad"
+            grad[c] = psum.tile([P, FEATS], F32, name="grad", tag=tag, bufs=2)
+            multiply_columns(c, grad[c], slice(0, FEATS))
 
-        for j in range(PACK):
-            make_factor(j)
-        nc.scalar.activation(out=nts_row[:], in_=ts_spread[:].rearrange("r j s -> r (j s)"), func=ACT.Copy)
-        for t in range(2):
-            gather_plane(t)
-        nc.vector.tensor_copy(
-            out=w_d[:, :, :2].rearrange("p (j s) t -> p j s t", j=PACK),
-            in_=w_listed[:].rearrange("p (t s j) -> p j s t", t=2, j=PACK),
-        )
-        for t in range(2, PACK):
-            nc.vector.tensor_copy(
-                out=w_d[:, :, t].rearrange("p (j s) -> p s j", j=PACK), in_=w_window[t][:].indirect(offsets[:])
-            )
+        def store_gradient(c):
+            result = keep.tile([P, FEATS], F32, name="result%d" % c)
+            if c in STORED_BY_VECTOR:
+                nc.vector.tensor_copy(out=result[:], in_=grad[c][:])
+            else:
+                nc.scalar.activation(out=result[:], in_=grad[c][:], func=ACT.Copy)
+            nc.sync.dma_start(out=out[0, c * P : (c + 1) * P, :], in_=result[:])
+
+        def finish_in_halves(c):
+            width = FEATS // 2
+            for half in range(2):
+                cols = slice(half * width, (half + 1) * width)
+                bank = psum.tile([P, width], F32, name="last_grad", tag="resid", bufs=4)
+                multiply_columns(c, bank, cols)
+                result = keep.tile([P, width], F32, name="last_result%d" % half)
+                if half == 0:
+                    nc.vector.tensor_copy(out=result[:], in_=bank[:])
+                    nc.sync.dma_start(out=out[0, c * P : (c + 1) * P, cols], in_=result[:])
+                else:
+                    nc.scalar.activation(out=result[:], in_=bank[:], func=ACT.Copy)
+                    nc.scalar.dma_start(out=out[0, c * P : (c + 1) * P, cols], in_=result[:])
+
+        def cast_group(c):
+            if c in ROW_GROUPS:
+                cast_x(c)
+
+        def quantize_group(c):
+            if c in ROW_GROUPS:
+                quantize_x(c)
+
+        turn_first_planes()
         cast_x(0)
         cast_x(1)
+        turn_last_planes()
         nc.vector.quantize_mx(
             out=wd_codes[:].bitcast(E4M3X4), scales=wd_scales[:], in_=w_d[:].rearrange("p i t -> p (i t)")
         )
-        quantize_x(0)
-        multiply_scores(0)
-        quantize_x(1)
-        multiply_scores(1)
+        for c in range(2):
+            quantize_x(c)
+            multiply_scores(c)
+        cast_x(2)
+        copy_first_planes()
         deal_targets(0)
         turn_targets(0)
-        turn_first_planes()
-        turn_last_planes()
-        cast_x(2)
+        copy_last_planes()
 
         pipeline = (
-            (scale_scores, 0),
-            (turn_scores, 0),
-            (square_residual, 0),
-            (exponentiate, 0),
-            (quantize_h, -LAG - 1),
-            (multiply_gradient, -LAG - 1),
-            (first_rows, 2),
-            (multiply_scores, 2),
-            (deal_targets, 1),
-            (turn_targets, 1),
-            (form_h, -LAG),
-            (weigh_residual, -1),
-            (store_gradient, -LAG - 1),
-            (later_rows, 3),
+            (scale_scores, 0, 0),
+            (turn_scores, 0, 0),
+            (square_residual, 0, 0),
+            (exponentiate, 0, 0),
+            (quantize_h, -LAG - 1, 0),
+            (multiply_gradient, -LAG - 1, 0),
+            (quantize_group, 2, 0),
+            (multiply_scores, 2, 0),
+            (deal_targets, 1, 0),
+            (turn_targets, 1, 0),
+            (form_h, -LAG, 0),
+            (weigh_residual, -1, 0),
+            (store_gradient, -LAG - 1, 0),
+            (cast_group, 3, 4),
         )
-        for step in range(CHUNKS + LAG + 1):
-            for stage, shift in pipeline:
-                if 0 <= step + shift < CHUNKS:
+        for step in range(CHUNKS):
+            for stage, shift, first in pipeline:
+                if first <= step + shift < CHUNKS:
                     stage(step + shift)
-            if step == 0:
-                wi_codes = keep.tile([P, FEATS], U32, name="wi_codes", tag="x_bf2", align_bytes=64)
+            if step == 1:
                 quantize_turned()
+
+        last = CHUNKS - 1
+        for c in range(last - LAG, last):
+            if c + 1 < last:
+                form_h(c + 1)
+            else:
+                weigh_residual(last)
+            quantize_h(c)
+            multiply_gradient(c)
+            store_gradient(c)
+        form_h(last)
+        quantize_h(last)
+        finish_in_halves(last)

@@ -16,18 +16,23 @@ IS_EQUAL = mybir.AluOpType.is_equal
 
 P = 128
 PACK = 4
+RUN = 8
 SLOTS = 512
 ITEMS = 2048
 FEATS = 512
 ROWS = 1024
 CHUNKS = ROWS // P
 QUAD = 32
-DEALT = (0, 1)
+ROW_GROUPS = {0: 1, 1: 1, 2: 2, 4: 2, 6: 2}
+TARGET_GROUPS = {0: 1, 1: 1, 2: 2, 4: 2, 6: 2}
+DEALT_ON_POOL = ()
+DEALT_ON_SCALAR = (6,)
+CAST_ON_POOL = ()
+CAST_ON_VECTOR = ()
 WEIGHED_ON_POOL = ()
 STORED_BY_VECTOR = ()
 LATE = 5
-LAG = 3
-ROW_GROUPS = {0: 1, 1: 1, 2: 2, 4: 2, 6: 2}
+TAGS = {}
 
 FLOPS = 2 * 2 * ROWS * SLOTS * FEATS
 BYTES = 4 * (FEATS * ROWS + FEATS * ITEMS + ROWS * SLOTS + ROWS + ITEMS + ROWS * FEATS) + 2 * P * SLOTS // 16
@@ -39,6 +44,9 @@ def tile_attend_gwel_x_ts_kernel(tc, xT, wT, y, wt, ts, offs, out):
         keep = ctx.enter_context(tc.tile_pool(name="keep", bufs=1))
         work = ctx.enter_context(tc.tile_pool(name="work", bufs=3))
         psum = ctx.enter_context(tc.psum_pool(name="psum", bufs=1))
+
+        def tag_of(kind, c):
+            return TAGS.get((kind, c), "%s%d" % (kind, c))
 
         offsets = keep.tile([P, SLOTS // 16], U16, name="offsets")
         nc.sync.dma_start(offsets[:], offs)
@@ -73,28 +81,30 @@ def tile_attend_gwel_x_ts_kernel(tc, xT, wT, y, wt, ts, offs, out):
         x_view = xT[0].rearrange("(p t) r -> p t r", t=PACK)
         y_view = y[0].rearrange("(c p) n -> p c n", p=P)
         x_raw = {}
-        y_raw = {}
+        y_group = {}
 
-        def load_x(first):
-            raw = keep.tile([P, PACK, 2 * P], F32, name="x_raw", tag="x_rows%d" % first, align_bytes=64)
-            nc.sync.dma_start(out=raw[:], in_=x_view[:, :, first * P : (first + 2) * P])
-            for e in range(2):
+        def load_x(first, count):
+            raw = keep.tile([P, PACK, count * P], F32, name="x_raw", tag="x_rows%d" % first, align_bytes=64)
+            nc.sync.dma_start(out=raw[:], in_=x_view[:, :, first * P : (first + count) * P])
+            for e in range(count):
                 x_raw[first + e] = raw[:, :, e * P :]
 
         def load_y(first, count):
             raw = keep.tile([P, count, SLOTS], F32, name="y_raw", tag="y_rows%d" % first, align_bytes=64)
             nc.sync.dma_start(out=raw[:], in_=y_view[:, first : first + count, :])
-            for e in range(count):
-                y_raw[first + e] = raw[:, e, :]
+            for c in range(first, first + count):
+                if c in TARGET_GROUPS:
+                    y_group[c] = raw[:, c - first : c - first + TARGET_GROUPS[c], :]
 
-        load_x(0)
-        load_x(2)
+        load_x(0, 2)
+        load_x(2, 2)
         load_y(0, 1)
         load_y(1, 1)
         load_y(2, 2)
-        for first in range(4, CHUNKS, 2):
-            load_x(first)
-            load_y(first, 2)
+        load_x(4, 2)
+        load_y(4, 2)
+        load_x(6, 2)
+        load_y(6, 2)
 
         wt_row = keep.tile([P, ROWS], F32, name="wt_row")
         wt_lines = wt_row[:].rearrange("s (p b k) -> s p b k", b=CHUNKS // PACK, k=PACK)
@@ -107,7 +117,7 @@ def tile_attend_gwel_x_ts_kernel(tc, xT, wT, y, wt, ts, offs, out):
 
         ts_dealt = keep.tile([P, SLOTS], F32, name="ts_dealt")
         nc.vector.tensor_copy(
-            out=ts_dealt[:].rearrange("p (j s) -> p s j", j=PACK), in_=ts_window[:].indirect(offsets[:])
+            out=ts_dealt[:].rearrange("p (j b i) -> p b j i", j=PACK, i=RUN), in_=ts_window[:].indirect(offsets[:])
         )
         ts_turned = psum.tile([P, PACK, P], F32, name="ts_turned", tag="resid", bufs=4)
         for j in range(PACK):
@@ -126,31 +136,33 @@ def tile_attend_gwel_x_ts_kernel(tc, xT, wT, y, wt, ts, offs, out):
         w_d = keep.tile([P, SLOTS, PACK], BF16, name="w_d", align_bytes=64)
         wd_codes = keep.tile([P, SLOTS], U32, name="wd_codes", align_bytes=64)
         wd_scales = keep.tile([P, SLOTS], U8, name="wd_scales", align_bytes=64)
-        wi_codes = keep.tile([P, FEATS], U32, name="wi_codes", align_bytes=64)
         wi_scales = keep.tile([P, FEATS], U8, name="wi_scales", align_bytes=64)
         w_paired = keep.tile([P, 2 * SLOTS], BF16, name="w_paired", tag="stage1", align_bytes=64)
         w_i = keep.tile([P, P, PACK, PACK], BF16, name="w_i", tag="x_rows0", align_bytes=64)
 
         for t in range(2):
-            nc.vector.tensor_copy(out=w_paired[:, t * SLOTS : (t + 1) * SLOTS], in_=w_window[t][:].indirect(offsets[:]))
+            nc.vector.tensor_copy(
+                out=w_paired[:, t * SLOTS : (t + 1) * SLOTS].rearrange("p (u b i e) -> p b u e i", u=2, i=RUN, e=2),
+                in_=w_window[t][:].indirect(offsets[:]),
+            )
         nc.vector.tensor_copy(
-            out=w_d[:, :, :2].rearrange("p (j s) t -> p j s t", j=PACK),
-            in_=w_paired[:].rearrange("p (t s j) -> p j s t", t=2, j=PACK),
+            out=w_d[:, :, :2].rearrange("p (u e s) t -> p u e s t", u=2, e=2),
+            in_=w_paired[:].rearrange("p (t u s e) -> p u e s t", t=2, u=2, e=2),
         )
         for t in range(2, PACK):
             nc.vector.tensor_copy(
-                out=w_d[:, :, t].rearrange("p (j s) -> p s j", j=PACK), in_=w_window[t][:].indirect(offsets[:])
+                out=w_d[:, :, t].rearrange("p (j b i) -> p b j i", j=PACK, i=RUN),
+                in_=w_window[t][:].indirect(offsets[:]),
             )
 
         first_turned = psum.tile([P, PACK, P], F32, name="turned", tag="grad", bufs=2)
         last_turned = psum.tile([P, PACK, P], F32, name="turned", tag="grad", bufs=2)
+        wi_codes = {}
 
         def turn_first_planes():
             words = w_paired[:].bitcast(F32)
-            for t in range(2):
-                for u in range(2):
-                    first = t * SLOTS // 2 + u
-                    nc.tensor.transpose(first_turned[:, 2 * t + u, :], words[:, first : (t + 1) * SLOTS // 2 : 2], ident[:])
+            for k in range(PACK):
+                nc.tensor.transpose(first_turned[:, k, :], words[:, k * P : (k + 1) * P], ident[:])
 
         def turn_last_planes():
             words = w_d[:].rearrange("p i t -> p (i t)").bitcast(F32)
@@ -169,8 +181,9 @@ def tile_attend_gwel_x_ts_kernel(tc, xT, wT, y, wt, ts, offs, out):
             )
 
         def quantize_turned():
+            wi_codes[0] = keep.tile([P, FEATS], U32, name="wi_codes", tag=tag_of("wi_codes", 0), align_bytes=64)
             nc.vector.quantize_mx(
-                out=wi_codes[:].bitcast(E4M3X4), scales=wi_scales[:], in_=w_i[:].rearrange("s p t j -> s (p t j)")
+                out=wi_codes[0][:].bitcast(E4M3X4), scales=wi_scales[:], in_=w_i[:].rearrange("s p t j -> s (p t j)")
             )
 
         x_bf, x_codes, x_scales, summand = ({} for i in range(4))
@@ -178,16 +191,19 @@ def tile_attend_gwel_x_ts_kernel(tc, xT, wT, y, wt, ts, offs, out):
 
         def cast_x(c):
             count = ROW_GROUPS[c]
-            x_bf[c] = keep.tile([P, count * P, PACK], BF16, name="x_bf%d" % c, align_bytes=64)
-            nc.scalar.activation(
-                out=x_bf[c][:].rearrange("p (a i) t -> p a t i", i=2),
-                in_=x_raw[c][:, :, : count * P].rearrange("p t (a i) -> p a t i", i=2),
-                func=ACT.Copy,
-            )
+            x_bf[c] = keep.tile([P, count * P, PACK], BF16, name="x_bf", tag=tag_of("x_bf", c), align_bytes=64)
+            target = x_bf[c][:].rearrange("p (a i) t -> p a t i", i=2)
+            source = x_raw[c][:, :, : count * P].rearrange("p t (a i) -> p a t i", i=2)
+            if c in CAST_ON_POOL:
+                nc.gpsimd.tensor_scalar(out=target, in0=source, scalar1=1.0, scalar2=0.0, op0=MULT, op1=ADD)
+            elif c in CAST_ON_VECTOR:
+                nc.vector.tensor_copy(out=target, in_=source)
+            else:
+                nc.scalar.activation(out=target, in_=source, func=ACT.Copy)
 
         def quantize_x(c):
             count = ROW_GROUPS[c]
-            codes = keep.tile([P, count * P], U32, name="x_codes%d" % c, align_bytes=64)
+            codes = keep.tile([P, count * P], U32, name="x_codes", tag=tag_of("x_codes", c), align_bytes=64)
             scales = keep.tile([P, count * P], U8, name="x_scales%d" % c, align_bytes=64)
             nc.vector.quantize_mx(
                 out=codes[:].bitcast(E4M3X4), scales=scales[:], in_=x_bf[c][:].rearrange("p r t -> p (r t)")
@@ -197,12 +213,18 @@ def tile_attend_gwel_x_ts_kernel(tc, xT, wT, y, wt, ts, offs, out):
                 x_scales[c + e] = scales[:, e * P : (e + 1) * P]
 
         def deal_targets(c):
-            if c in DEALT:
-                summand[c] = keep.tile([P, SLOTS], F32, name="summand%d" % c, align_bytes=64)
-                nc.vector.tensor_copy(
-                    out=summand[c][:].rearrange("r (v e a i) -> r a v i e", v=2, e=2, i=4),
-                    in_=y_raw[c].rearrange("r (a i v e) -> r a v i e", v=2, e=2, i=4),
-                )
+            count = TARGET_GROUPS[c]
+            dealt = keep.tile([P, PACK, count * P], F32, name="dealt", tag=tag_of("dealt", c), align_bytes=64)
+            for e in range(count):
+                summand[c + e] = dealt[:, :, e * P : (e + 1) * P]
+            source = y_group[c].rearrange("r c (b j i) -> r (c b) j i", j=PACK, i=RUN)
+            target = dealt[:].rearrange("r j (b i) -> r b j i", i=RUN)
+            if c in DEALT_ON_POOL:
+                nc.gpsimd.tensor_scalar(out=target, in0=source, scalar1=1.0, scalar2=0.0, op0=MULT, op1=ADD)
+            elif c in DEALT_ON_SCALAR:
+                nc.scalar.activation(out=target, in_=source, func=ACT.Copy)
+            else:
+                nc.vector.tensor_copy(out=target, in_=source)
 
         def multiply_scores(c):
             score[c] = psum.tile([P, SLOTS], F32, name="score", tag="score", bufs=2)
@@ -223,8 +245,9 @@ def tile_attend_gwel_x_ts_kernel(tc, xT, wT, y, wt, ts, offs, out):
         def turn_targets(c):
             resid[c] = psum.tile([P, PACK, P], F32, name="resid", tag="resid", bufs=4)
             for j in range(PACK):
-                source = summand[c][:, j * P : (j + 1) * P] if c in DEALT else y_raw[c][:, j::PACK]
-                nc.tensor.matmul(resid[c][:, j, :], source, ident[:], start=(j == 0), stop=False, is_transpose=True)
+                nc.tensor.matmul(
+                    resid[c][:, j, :], summand[c][:, j, :], ident[:], start=(j == 0), stop=False, is_transpose=True
+                )
 
         def turn_scores(c):
             for j in range(PACK):
@@ -238,26 +261,20 @@ def tile_attend_gwel_x_ts_kernel(tc, xT, wT, y, wt, ts, offs, out):
             nc.scalar.activation(out=square[c][:], in_=resid[c][:], func=ACT.Square)
 
         def exponentiate(c):
-            bell[c] = work.tile([P, PACK, P], F32, name="bell", bufs=LAG + 2)
+            bell[c] = keep.tile([P, PACK, P], F32, name="bell", tag=tag_of("bell", c), align_bytes=64)
             nc.scalar.activation(out=bell[c][:], in_=square[c][:], func=ACT.Exp, scale=-0.5)
 
         def weigh_bell(c):
-            if c in WEIGHED_ON_POOL:
-                weighted[c] = work.tile([P, PACK, P], F32, name="weighted", bufs=LAG + 2, align_bytes=64)
-                nc.gpsimd.tensor_tensor(
-                    out=weighted[c][:], in0=bell[c][:], in1=factor[:, :, c * P : (c + 1) * P], op=MULT
-                )
+            weighted[c] = keep.tile([P, PACK, P], F32, name="weighted", tag=tag_of("weighted", c), align_bytes=64)
+            nc.gpsimd.tensor_tensor(out=weighted[c][:], in0=bell[c][:], in1=factor[:, :, c * P : (c + 1) * P], op=MULT)
 
         def weigh_residual(c):
-            if c not in WEIGHED_ON_POOL:
-                weighted[c] = work.tile([P, PACK, P], F32, name="weighted", bufs=LAG + 2, align_bytes=64)
-                nc.vector.tensor_tensor(
-                    out=weighted[c][:], in0=resid[c][:], in1=factor[:, :, c * P : (c + 1) * P], op=MULT
-                )
+            weighted[c] = keep.tile([P, PACK, P], F32, name="weighted", tag=tag_of("weighted", c), align_bytes=64)
+            nc.vector.tensor_tensor(out=weighted[c][:], in0=resid[c][:], in1=factor[:, :, c * P : (c + 1) * P], op=MULT)
 
         def form_h(c):
             other = resid[c] if c in WEIGHED_ON_POOL else bell[c]
-            h[c] = work.tile([P, P, PACK], BF16, name="h", align_bytes=64)
+            h[c] = keep.tile([P, P, PACK], BF16, name="h", tag=tag_of("h", c), align_bytes=64)
             nc.vector.tensor_tensor(
                 out=h[c][:].rearrange("s (a i) j -> s a j i", i=2),
                 in0=other[:].rearrange("s j (a i) -> s a j i", i=2),
@@ -266,8 +283,8 @@ def tile_attend_gwel_x_ts_kernel(tc, xT, wT, y, wt, ts, offs, out):
             )
 
         def quantize_h(c):
-            h_codes[c] = work.tile([P, P], U32, name="h_codes", align_bytes=64)
-            h_scales[c] = work.tile([P, P], U8, name="h_scales", align_bytes=64)
+            h_codes[c] = keep.tile([P, P], U32, name="h_codes", tag=tag_of("h_codes", c), align_bytes=64)
+            h_scales[c] = keep.tile([P, P], U8, name="h_scales%d" % c, align_bytes=64)
             nc.vector.quantize_mx(
                 out=h_codes[c][:].bitcast(E5M2X4), scales=h_scales[c][:], in_=h[c][:].rearrange("s r j -> s (r j)")
             )
@@ -277,7 +294,7 @@ def tile_attend_gwel_x_ts_kernel(tc, xT, wT, y, wt, ts, offs, out):
                 out=bank[:],
                 lhsT=h_codes[c][:].bitcast(E5M2X4),
                 lhsT_scale=h_scales[c][:],
-                rhs=wi_codes[:, cols].bitcast(E4M3X4),
+                rhs=wi_codes[0][:, cols].bitcast(E4M3X4),
                 rhs_scale=wi_scales[:, cols],
                 start=True,
                 stop=True,
@@ -310,62 +327,116 @@ def tile_attend_gwel_x_ts_kernel(tc, xT, wT, y, wt, ts, offs, out):
                     nc.scalar.activation(out=result[:], in_=bank[:], func=ACT.Copy)
                     nc.scalar.dma_start(out=out[0, c * P : (c + 1) * P, cols], in_=result[:])
 
-        def cast_group(c):
-            if c in ROW_GROUPS:
-                cast_x(c)
-
-        def quantize_group(c):
-            if c in ROW_GROUPS:
-                quantize_x(c)
+        def quantize_columns():
+            nc.vector.quantize_mx(
+                out=wd_codes[:].bitcast(E4M3X4), scales=wd_scales[:], in_=w_d[:].rearrange("p i t -> p (i t)")
+            )
 
         turn_first_planes()
         cast_x(0)
         cast_x(1)
         turn_last_planes()
-        nc.vector.quantize_mx(
-            out=wd_codes[:].bitcast(E4M3X4), scales=wd_scales[:], in_=w_d[:].rearrange("p i t -> p (i t)")
-        )
-        for c in range(2):
-            quantize_x(c)
-            multiply_scores(c)
+        quantize_columns()
+        quantize_x(0)
+        multiply_scores(0)
+        quantize_x(1)
+        multiply_scores(1)
         cast_x(2)
         copy_first_planes()
         deal_targets(0)
         turn_targets(0)
         copy_last_planes()
-
-        pipeline = (
-            (scale_scores, 0, 0),
-            (turn_scores, 0, 0),
-            (square_residual, 0, 0),
-            (exponentiate, 0, 0),
-            (quantize_h, -LAG - 1, 0),
-            (multiply_gradient, -LAG - 1, 0),
-            (quantize_group, 2, 0),
-            (multiply_scores, 2, 0),
-            (deal_targets, 1, 0),
-            (turn_targets, 1, 0),
-            (form_h, -LAG, 0),
-            (weigh_residual, -1, 0),
-            (store_gradient, -LAG - 1, 0),
-            (cast_group, 3, 4),
-        )
-        for step in range(CHUNKS):
-            for stage, shift, first in pipeline:
-                if first <= step + shift < CHUNKS:
-                    stage(step + shift)
-            if step == 1:
-                quantize_turned()
-
-        last = CHUNKS - 1
-        for c in range(last - LAG, last):
-            if c + 1 < last:
-                form_h(c + 1)
-            else:
-                weigh_residual(last)
-            quantize_h(c)
-            multiply_gradient(c)
-            store_gradient(c)
-        form_h(last)
-        quantize_h(last)
-        finish_in_halves(last)
+        scale_scores(0)
+        turn_scores(0)
+        square_residual(0)
+        exponentiate(0)
+        quantize_x(2)
+        multiply_scores(2)
+        deal_targets(1)
+        turn_targets(1)
+        scale_scores(1)
+        turn_scores(1)
+        square_residual(1)
+        exponentiate(1)
+        multiply_scores(3)
+        deal_targets(2)
+        turn_targets(2)
+        weigh_residual(0)
+        cast_x(4)
+        quantize_turned()
+        scale_scores(2)
+        turn_scores(2)
+        square_residual(2)
+        exponentiate(2)
+        quantize_x(4)
+        multiply_scores(4)
+        turn_targets(3)
+        weigh_residual(1)
+        scale_scores(3)
+        turn_scores(3)
+        square_residual(3)
+        exponentiate(3)
+        multiply_scores(5)
+        deal_targets(4)
+        turn_targets(4)
+        form_h(0)
+        weigh_residual(2)
+        cast_x(6)
+        scale_scores(4)
+        turn_scores(4)
+        square_residual(4)
+        exponentiate(4)
+        quantize_h(0)
+        multiply_gradient(0)
+        quantize_x(6)
+        multiply_scores(6)
+        turn_targets(5)
+        form_h(1)
+        weigh_residual(3)
+        store_gradient(0)
+        scale_scores(5)
+        turn_scores(5)
+        square_residual(5)
+        exponentiate(5)
+        quantize_h(1)
+        multiply_gradient(1)
+        multiply_scores(7)
+        deal_targets(6)
+        turn_targets(6)
+        form_h(2)
+        weigh_residual(4)
+        store_gradient(1)
+        scale_scores(6)
+        turn_scores(6)
+        square_residual(6)
+        exponentiate(6)
+        quantize_h(2)
+        multiply_gradient(2)
+        turn_targets(7)
+        form_h(3)
+        weigh_residual(5)
+        store_gradient(2)
+        scale_scores(7)
+        turn_scores(7)
+        square_residual(7)
+        exponentiate(7)
+        quantize_h(3)
+        multiply_gradient(3)
+        form_h(4)
+        weigh_residual(6)
+        store_gradient(3)
+        form_h(5)
+        quantize_h(4)
+        multiply_gradient(4)
+        store_gradient(4)
+        form_h(6)
+        quantize_h(5)
+        multiply_gradient(5)
+        store_gradient(5)
+        weigh_residual(7)
+        quantize_h(6)
+        multiply_gradient(6)
+        store_gradient(6)
+        form_h(7)
+        quantize_h(7)
+        finish_in_halves(7)

@@ -32,7 +32,7 @@ CAST_ON_VECTOR = ()
 WEIGHED_ON_POOL = ()
 STORED_BY_VECTOR = ()
 LATE = 5
-TAGS = {}
+TAGS = {("w_i", 0): "x_rows0"}
 
 FLOPS = 2 * 2 * ROWS * SLOTS * FEATS
 BYTES = 4 * (FEATS * ROWS + FEATS * ITEMS + ROWS * SLOTS + ROWS + ITEMS + ROWS * FEATS) + 2 * P * SLOTS // 16
@@ -46,7 +46,7 @@ def tile_attend_gwel_x_ts_kernel(tc, xT, wT, y, wt, ts, offs, out):
         psum = ctx.enter_context(tc.psum_pool(name="psum", bufs=1))
 
         def tag_of(kind, c):
-            return TAGS.get((kind, c), "%s%d" % (kind, c))
+            return TAGS.get((kind, c), "%s%d" % (kind, c % 3 if kind in ("scaled", "square") else c))
 
         offsets = keep.tile([P, SLOTS // 16], U16, name="offsets")
         nc.sync.dma_start(offsets[:], offs)
@@ -57,18 +57,18 @@ def tile_attend_gwel_x_ts_kernel(tc, xT, wT, y, wt, ts, offs, out):
         ts_window = keep.tile([P, ITEMS], F32, name="ts_window", tag="stage1", align_bytes=64)
 
         ones = keep.tile([P, QUAD], F32, name="ones")
-        nc.vector.memset(ones[:], 1.0)
+        nc.gpsimd.memset(ones[:], 1.0)
         ident = keep.tile([P, P], F32, name="ident")
-        nc.vector.memset(ident[:], 0.0)
+        nc.gpsimd.memset(ident[:], 0.0)
+        nc.gpsimd.memset(ts_window[:, : ITEMS // 2], 0.0)
         column = keep.tile([P, QUAD], F32, name="column", align_bytes=64)
         nc.vector.tensor_tensor_scan(out=column[:], data0=ones[:], data1=ones[:], initial=0.0, op0=MULT, op1=ADD)
-        nc.vector.memset(ts_window[:, : ITEMS // 2], 0.0)
         row = keep.tile([P, QUAD], F32, name="row", align_bytes=64)
         nc.vector.transpose(out=row[:], in_=column[:])
-        nc.vector.memset(ts_window[:, ITEMS // 2 :], 0.0)
         for q in range(P // QUAD):
             band = slice(q * QUAD, (q + 1) * QUAD)
             nc.vector.tensor_tensor(out=ident[band, band], in0=column[band, :], in1=row[band, :], op=IS_EQUAL)
+        nc.vector.memset(ts_window[:, ITEMS // 2 :], 0.0)
         nc.vector.tensor_copy(out=ts_window[0:1, :], in_=ts_row[:])
 
         w_planes = wT.rearrange("(p t) n -> t p n", t=PACK)
@@ -137,19 +137,10 @@ def tile_attend_gwel_x_ts_kernel(tc, xT, wT, y, wt, ts, offs, out):
         wd_codes = keep.tile([P, SLOTS], U32, name="wd_codes", align_bytes=64)
         wd_scales = keep.tile([P, SLOTS], U8, name="wd_scales", align_bytes=64)
         wi_scales = keep.tile([P, FEATS], U8, name="wi_scales", align_bytes=64)
-        w_paired = keep.tile([P, 2 * SLOTS], BF16, name="w_paired", tag="stage1", align_bytes=64)
-        w_i = keep.tile([P, P, PACK, PACK], BF16, name="w_i", tag="x_rows0", align_bytes=64)
+        wi_first = keep.tile([P, P, 2, PACK], BF16, name="wi_first", align_bytes=64)
+        w_i = keep.tile([P, P, PACK, PACK], BF16, name="w_i", tag=tag_of("w_i", 0), align_bytes=64)
 
-        for t in range(2):
-            nc.vector.tensor_copy(
-                out=w_paired[:, t * SLOTS : (t + 1) * SLOTS].rearrange("p (u b i e) -> p b u e i", u=2, i=RUN, e=2),
-                in_=w_window[t][:].indirect(offsets[:]),
-            )
-        nc.vector.tensor_copy(
-            out=w_d[:, :, :2].rearrange("p (u e s) t -> p u e s t", u=2, e=2),
-            in_=w_paired[:].rearrange("p (t u s e) -> p u e s t", t=2, u=2, e=2),
-        )
-        for t in range(2, PACK):
+        def gather_plane(t):
             nc.vector.tensor_copy(
                 out=w_d[:, :, t].rearrange("p (j b i) -> p b j i", j=PACK, i=RUN),
                 in_=w_window[t][:].indirect(offsets[:]),
@@ -159,26 +150,32 @@ def tile_attend_gwel_x_ts_kernel(tc, xT, wT, y, wt, ts, offs, out):
         last_turned = psum.tile([P, PACK, P], F32, name="turned", tag="grad", bufs=2)
         wi_codes = {}
 
-        def turn_first_planes():
-            words = w_paired[:].bitcast(F32)
-            for k in range(PACK):
-                nc.tensor.transpose(first_turned[:, k, :], words[:, k * P : (k + 1) * P], ident[:])
-
-        def turn_last_planes():
+        def turn_planes(turned, word):
             words = w_d[:].rearrange("p i t -> p (i t)").bitcast(F32)
             for j in range(PACK):
-                nc.tensor.transpose(last_turned[:, j, :], words[:, 2 * j * P + 1 : 2 * (j + 1) * P : 2], ident[:])
+                nc.tensor.transpose(turned[:, j, :], words[:, 2 * j * P + word : 2 * (j + 1) * P : 2], ident[:])
 
-        def copy_first_planes():
-            lines = w_i[:].rearrange("s p t j -> s (p t j)").bitcast(F32).rearrange("s (p h k) -> s p h k", h=2, k=PACK)
-            nc.scalar.copy(out=lines[:, :, 0, :], in_=first_turned[:].rearrange("s k p -> s p k"))
+        def turn_first_planes():
+            turn_planes(first_turned, 0)
 
-        def copy_last_planes():
-            halves = last_turned[:].rearrange("s j p -> s (j p)").bitcast(BF16)
+        def turn_last_planes():
+            turn_planes(last_turned, 1)
+
+        def copy_planes(turned, target):
+            halves = turned[:].rearrange("s j p -> s (j p)").bitcast(BF16)
             nc.scalar.copy(
-                out=w_i[:, :, 2:, :].rearrange("s p e j -> s p j e"),
+                out=target.rearrange("s p e j -> s p j e"),
                 in_=halves.rearrange("s (j p e) -> s p j e", j=PACK, e=2),
             )
+
+        def copy_first_planes():
+            copy_planes(first_turned, wi_first[:])
+
+        def join_first_planes():
+            nc.vector.tensor_copy(out=w_i[:, :, :2, :], in_=wi_first[:])
+
+        def copy_last_planes():
+            copy_planes(last_turned, w_i[:, :, 2:, :])
 
         def quantize_turned():
             wi_codes[0] = keep.tile([P, FEATS], U32, name="wi_codes", tag=tag_of("wi_codes", 0), align_bytes=64)
@@ -239,7 +236,7 @@ def tile_attend_gwel_x_ts_kernel(tc, xT, wT, y, wt, ts, offs, out):
             )
 
         def scale_scores(c):
-            scaled[c] = work.tile([P, SLOTS], F32, name="scaled", align_bytes=64)
+            scaled[c] = keep.tile([P, SLOTS], F32, name="scaled", tag=tag_of("scaled", c), align_bytes=64)
             nc.vector.tensor_tensor(out=scaled[c][:], in0=score[c][:], in1=nts_row[:], op=MULT)
 
         def turn_targets(c):
@@ -257,7 +254,7 @@ def tile_attend_gwel_x_ts_kernel(tc, xT, wT, y, wt, ts, offs, out):
                 )
 
         def square_residual(c):
-            square[c] = work.tile([P, PACK, P], F32, name="square")
+            square[c] = keep.tile([P, PACK, P], F32, name="square", tag=tag_of("square", c), align_bytes=64)
             nc.scalar.activation(out=square[c][:], in_=resid[c][:], func=ACT.Square)
 
         def exponentiate(c):
@@ -306,7 +303,7 @@ def tile_attend_gwel_x_ts_kernel(tc, xT, wT, y, wt, ts, offs, out):
             multiply_columns(c, grad[c], slice(0, FEATS))
 
         def store_gradient(c):
-            result = keep.tile([P, FEATS], F32, name="result%d" % c)
+            result = keep.tile([P, FEATS], F32, name="result", tag=tag_of("result", c), align_bytes=64)
             if c in STORED_BY_VECTOR:
                 nc.vector.tensor_copy(out=result[:], in_=grad[c][:])
             else:
@@ -332,7 +329,12 @@ def tile_attend_gwel_x_ts_kernel(tc, xT, wT, y, wt, ts, offs, out):
                 out=wd_codes[:].bitcast(E4M3X4), scales=wd_scales[:], in_=w_d[:].rearrange("p i t -> p (i t)")
             )
 
+        gather_plane(0)
+        gather_plane(1)
         turn_first_planes()
+        gather_plane(2)
+        gather_plane(3)
+        copy_first_planes()
         cast_x(0)
         cast_x(1)
         turn_last_planes()
@@ -341,8 +343,8 @@ def tile_attend_gwel_x_ts_kernel(tc, xT, wT, y, wt, ts, offs, out):
         multiply_scores(0)
         quantize_x(1)
         multiply_scores(1)
+        join_first_planes()
         cast_x(2)
-        copy_first_planes()
         deal_targets(0)
         turn_targets(0)
         copy_last_planes()

@@ -57,18 +57,18 @@ def tile_attend_gwel_x_ts_kernel(tc, xT, wT, y, wt, ts, offs, out):
         ts_window = keep.tile([P, ITEMS], F32, name="ts_window", tag="stage1", align_bytes=64)
 
         ones = keep.tile([P, QUAD], F32, name="ones")
-        nc.gpsimd.memset(ones[:], 1.0)
+        nc.vector.memset(ones[:], 1.0)
         ident = keep.tile([P, P], F32, name="ident")
-        nc.gpsimd.memset(ident[:], 0.0)
-        nc.gpsimd.memset(ts_window[:, : ITEMS // 2], 0.0)
+        nc.vector.memset(ident[:], 0.0)
         column = keep.tile([P, QUAD], F32, name="column", align_bytes=64)
         nc.vector.tensor_tensor_scan(out=column[:], data0=ones[:], data1=ones[:], initial=0.0, op0=MULT, op1=ADD)
+        nc.vector.memset(ts_window[:, : ITEMS // 2], 0.0)
         row = keep.tile([P, QUAD], F32, name="row", align_bytes=64)
         nc.vector.transpose(out=row[:], in_=column[:])
+        nc.vector.memset(ts_window[:, ITEMS // 2 :], 0.0)
         for q in range(P // QUAD):
             band = slice(q * QUAD, (q + 1) * QUAD)
             nc.vector.tensor_tensor(out=ident[band, band], in0=column[band, :], in1=row[band, :], op=IS_EQUAL)
-        nc.vector.memset(ts_window[:, ITEMS // 2 :], 0.0)
         nc.vector.tensor_copy(out=ts_window[0:1, :], in_=ts_row[:])
 
         w_planes = wT.rearrange("(p t) n -> t p n", t=PACK)
@@ -129,7 +129,7 @@ def tile_attend_gwel_x_ts_kernel(tc, xT, wT, y, wt, ts, offs, out):
             nc.tensor.transpose(ts_spread[:, j, :], nts_col[:, j : j + 1].to_broadcast([P, P]), ident[:])
         factor = keep.tile([P, PACK, ROWS], F32, name="factor")
         nts_row = keep.tile([P, SLOTS], F32, name="nts_row")
-        for j in range(PACK):
+        for j in range(PACK - 1):
             nc.scalar.activation(out=factor[:, j, :], in_=wt_row[:], func=ACT.Copy, scale=nts_col[:, j : j + 1])
         nc.scalar.activation(out=nts_row[:], in_=ts_spread[:].rearrange("r j s -> r (j s)"), func=ACT.Copy)
 
@@ -324,6 +324,12 @@ def tile_attend_gwel_x_ts_kernel(tc, xT, wT, y, wt, ts, offs, out):
                     nc.scalar.activation(out=result[:], in_=bank[:], func=ACT.Copy)
                     nc.scalar.dma_start(out=out[0, c * P : (c + 1) * P, cols], in_=result[:])
 
+        def last_factor():
+            for j in range(PACK - 1, PACK):
+                nc.vector.tensor_scalar(
+                    out=factor[:, j, :], in0=wt_row[:], scalar1=nts_col[:, j : j + 1], scalar2=None, op0=MULT
+                )
+
         def quantize_columns():
             nc.vector.quantize_mx(
                 out=wd_codes[:].bitcast(E4M3X4), scales=wd_scales[:], in_=w_d[:].rearrange("p i t -> p (i t)")
@@ -332,9 +338,10 @@ def tile_attend_gwel_x_ts_kernel(tc, xT, wT, y, wt, ts, offs, out):
         gather_plane(0)
         gather_plane(1)
         turn_first_planes()
+        last_factor()
         gather_plane(2)
-        gather_plane(3)
         copy_first_planes()
+        gather_plane(3)
         cast_x(0)
         cast_x(1)
         turn_last_planes()
@@ -363,47 +370,47 @@ def tile_attend_gwel_x_ts_kernel(tc, xT, wT, y, wt, ts, offs, out):
         multiply_scores(3)
         deal_targets(2)
         turn_targets(2)
-        weigh_residual(0)
         cast_x(4)
+        quantize_x(4)
+        weigh_residual(0)
         quantize_turned()
         scale_scores(2)
         turn_scores(2)
+        multiply_scores(4)
         square_residual(2)
         exponentiate(2)
-        quantize_x(4)
-        multiply_scores(4)
         turn_targets(3)
         weigh_residual(1)
         scale_scores(3)
         turn_scores(3)
+        multiply_scores(5)
         square_residual(3)
         exponentiate(3)
-        multiply_scores(5)
+        cast_x(6)
+        quantize_x(6)
+        deal_targets(6)
         deal_targets(4)
         turn_targets(4)
         form_h(0)
         weigh_residual(2)
-        cast_x(6)
         scale_scores(4)
         turn_scores(4)
+        multiply_scores(6)
         square_residual(4)
         exponentiate(4)
         quantize_h(0)
         multiply_gradient(0)
-        quantize_x(6)
-        multiply_scores(6)
         turn_targets(5)
         form_h(1)
         weigh_residual(3)
         store_gradient(0)
         scale_scores(5)
         turn_scores(5)
+        multiply_scores(7)
         square_residual(5)
         exponentiate(5)
         quantize_h(1)
         multiply_gradient(1)
-        multiply_scores(7)
-        deal_targets(6)
         turn_targets(6)
         form_h(2)
         weigh_residual(4)

@@ -24,7 +24,7 @@ ROWS = 1024
 CHUNKS = ROWS // P
 QUAD = 32
 ROW_GROUPS = {0: 1, 1: 1, 2: 2, 4: 2, 6: 2}
-TARGET_GROUPS = {0: 1, 1: 1, 2: 2, 4: 2, 6: 2}
+TARGET_GROUPS = {0: 1, 1: 1, 2: 1, 3: 1, 4: 1, 5: 1, 6: 2}
 DEALT_ON_POOL = ()
 DEALT_ON_SCALAR = (6,)
 CAST_ON_POOL = ()
@@ -32,7 +32,7 @@ CAST_ON_VECTOR = ()
 WEIGHED_ON_POOL = ()
 STORED_BY_VECTOR = ()
 LATE = 5
-TAGS = {("w_i", 0): "x_rows0"}
+TAGS = {("w_i", 0): "x_rows0", ("dealt", 0): "x_bf1"}
 
 FLOPS = 2 * 2 * ROWS * SLOTS * FEATS
 BYTES = 4 * (FEATS * ROWS + FEATS * ITEMS + ROWS * SLOTS + ROWS + ITEMS + ROWS * FEATS) + 2 * P * SLOTS // 16
@@ -97,19 +97,20 @@ def tile_attend_gwel_x_ts_kernel(tc, xT, wT, y, wt, ts, offs, out):
                     y_group[c] = raw[:, c - first : c - first + TARGET_GROUPS[c], :]
 
         load_x(0, 2)
-        load_x(2, 2)
         load_y(0, 1)
+        load_x(2, 2)
         load_y(1, 1)
-        load_y(2, 2)
+        load_y(2, 1)
         load_x(4, 2)
-        load_y(4, 2)
+        load_y(3, 1)
         load_x(6, 2)
+        load_y(4, 2)
         load_y(6, 2)
 
         wt_row = keep.tile([P, ROWS], F32, name="wt_row")
         wt_lines = wt_row[:].rearrange("s (p b k) -> s p b k", b=CHUNKS // PACK, k=PACK)
         for b in range(CHUNKS // PACK):
-            bank = psum.tile([P, PACK, P], F32, name="spread", tag="resid", bufs=4)
+            bank = psum.tile([P, PACK, P], F32, name="spread", tag="resid", bufs=3)
             for k in range(PACK):
                 col = PACK * b + k
                 nc.tensor.transpose(bank[:, k, :], wt_runs[:, col : col + 1].to_broadcast([P, P]), ident[:])
@@ -119,12 +120,12 @@ def tile_attend_gwel_x_ts_kernel(tc, xT, wT, y, wt, ts, offs, out):
         nc.vector.tensor_copy(
             out=ts_dealt[:].rearrange("p (j b i) -> p b j i", j=PACK, i=RUN), in_=ts_window[:].indirect(offsets[:])
         )
-        ts_turned = psum.tile([P, PACK, P], F32, name="ts_turned", tag="resid", bufs=4)
+        ts_turned = psum.tile([P, PACK, P], F32, name="ts_turned", tag="resid", bufs=3)
         for j in range(PACK):
             nc.tensor.transpose(ts_turned[:, j, :], ts_dealt[:, j * P : (j + 1) * P], ident[:])
         nts_col = keep.tile([P, PACK], F32, name="nts_col")
         nc.scalar.activation(out=nts_col[:], in_=ts_turned[:, :, 0], func=ACT.Copy, scale=-1.0)
-        ts_spread = psum.tile([P, PACK, P], F32, name="ts_spread", tag="resid", bufs=4)
+        ts_spread = psum.tile([P, PACK, P], F32, name="ts_spread", tag="resid", bufs=3)
         for j in range(PACK):
             nc.tensor.transpose(ts_spread[:, j, :], nts_col[:, j : j + 1].to_broadcast([P, P]), ident[:])
         factor = keep.tile([P, PACK, ROWS], F32, name="factor")
@@ -240,7 +241,7 @@ def tile_attend_gwel_x_ts_kernel(tc, xT, wT, y, wt, ts, offs, out):
             nc.vector.tensor_tensor(out=scaled[c][:], in0=score[c][:], in1=nts_row[:], op=MULT)
 
         def turn_targets(c):
-            resid[c] = psum.tile([P, PACK, P], F32, name="resid", tag="resid", bufs=4)
+            resid[c] = psum.tile([P, PACK, P], F32, name="resid", tag="resid", bufs=3)
             for j in range(PACK):
                 nc.tensor.matmul(
                     resid[c][:, j, :], summand[c][:, j, :], ident[:], start=(j == 0), stop=False, is_transpose=True
@@ -314,7 +315,7 @@ def tile_attend_gwel_x_ts_kernel(tc, xT, wT, y, wt, ts, offs, out):
             width = FEATS // 2
             for half in range(2):
                 cols = slice(half * width, (half + 1) * width)
-                bank = psum.tile([P, width], F32, name="last_grad", tag="resid", bufs=4)
+                bank = psum.tile([P, width], F32, name="last_grad", tag="resid", bufs=3)
                 multiply_columns(c, bank, cols)
                 result = keep.tile([P, width], F32, name="last_result%d" % half)
                 if half == 0:
@@ -350,11 +351,11 @@ def tile_attend_gwel_x_ts_kernel(tc, xT, wT, y, wt, ts, offs, out):
         multiply_scores(0)
         quantize_x(1)
         multiply_scores(1)
-        join_first_planes()
-        cast_x(2)
         deal_targets(0)
+        join_first_planes()
         turn_targets(0)
         copy_last_planes()
+        cast_x(2)
         scale_scores(0)
         turn_scores(0)
         square_residual(0)
@@ -379,6 +380,7 @@ def tile_attend_gwel_x_ts_kernel(tc, xT, wT, y, wt, ts, offs, out):
         multiply_scores(4)
         square_residual(2)
         exponentiate(2)
+        deal_targets(3)
         turn_targets(3)
         weigh_residual(1)
         scale_scores(3)
@@ -400,6 +402,7 @@ def tile_attend_gwel_x_ts_kernel(tc, xT, wT, y, wt, ts, offs, out):
         exponentiate(4)
         quantize_h(0)
         multiply_gradient(0)
+        deal_targets(5)
         turn_targets(5)
         form_h(1)
         weigh_residual(3)

from contextlib import ExitStack

import concourse.mybir as mybir

F32 = mybir.dt.float32
BF16 = mybir.dt.bfloat16
U32 = mybir.dt.uint32
U16 = mybir.dt.uint16
U8 = mybir.dt.uint8
E4M3X4 = mybir.dt.float8_e4m3fn_x4
E5M2X4 = mybir.dt.float8_e5m2_x4
ACT = mybir.ActivationFunctionType
MULT = mybir.AluOpType.mult
ADD = mybir.AluOpType.add
IS_EQUAL = mybir.AluOpType.is_equal

P = 128
PACK = 4
RUN = 8
SLOTS = 512
ITEMS = 2048
FEATS = 512
ROWS = 1024
CHUNKS = ROWS // P
QUAD = 32
ROW_GROUPS = {0: 1, 1: 1, 2: 2, 4: 2, 6: 2}
TARGET_GROUPS = {0: 1, 1: 1, 2: 1, 3: 1, 4: 1, 5: 1, 6: 2}
DEALT_ON_POOL = ()
DEALT_ON_SCALAR = (6,)
CAST_ON_POOL = ()
CAST_ON_VECTOR = ()
WEIGHED_ON_POOL = ()
STORED_BY_VECTOR = ()
LATE = 5
TAGS = {("w_i", 0): "x_rows0", ("dealt", 0): "x_bf1"}

FLOPS = 2 * 2 * ROWS * SLOTS * FEATS
BYTES = 4 * (FEATS * ROWS + FEATS * ITEMS + ROWS * SLOTS + ROWS + ITEMS + ROWS * FEATS) + 2 * P * SLOTS // 16


def tile_attend_gwel_x_ts_kernel(tc, xT, wT, y, wt, ts, offs, out):
    nc = tc.nc
    with ExitStack() as ctx:
        keep = ctx.enter_context(tc.tile_pool(name="keep", bufs=1))
        work = ctx.enter_context(tc.tile_pool(name="work", bufs=3))
        psum = ctx.enter_context(tc.psum_pool(name="psum", bufs=1))

        def tag_of(kind, c):
            return TAGS.get((kind, c), "%s%d" % (kind, c % 3 if kind in ("scaled", "square") else c))

        offsets = keep.tile([P, SLOTS // 16], U16, name="offsets")
        nc.sync.dma_start(offsets[:], offs)
        ts_row = keep.tile([1, ITEMS], F32, name="ts_row")
        nc.sync.dma_start(out=ts_row[:], in_=ts[0:1, :])
        wt_runs = keep.tile([P, CHUNKS], F32, name="wt_runs")
        nc.sync.dma_start(out=wt_runs[:], in_=wt[0].rearrange("(p k) o -> p (k o)", k=CHUNKS))
        ts_window = keep.tile([P, ITEMS], F32, name="ts_window", tag="stage1", align_bytes=64)

        ones = keep.tile([P, QUAD], F32, name="ones")
        nc.vector.memset(ones[:], 1.0)
        ident = keep.tile([P, P], F32, name="ident")
        nc.vector.memset(ident[:], 0.0)
        column = keep.tile([P, QUAD], F32, name="column", align_bytes=64)
        nc.vector.tensor_tensor_scan(out=column[:], data0=ones[:], data1=ones[:], initial=0.0, op0=MULT, op1=ADD)
        nc.vector.memset(ts_window[:, : ITEMS // 2], 0.0)
        row = keep.tile([P, QUAD], F32, name="row", align_bytes=64)
        nc.vector.transpose(out=row[:], in_=column[:])
        nc.vector.memset(ts_window[:, ITEMS // 2 :], 0.0)
        for q in range(P // QUAD):
            band = slice(q * QUAD, (q + 1) * QUAD)
            nc.vector.tensor_tensor(out=ident[band, band], in0=column[band, :], in1=row[band, :], op=IS_EQUAL)
        nc.vector.tensor_copy(out=ts_window[0:1, :], in_=ts_row[:])

        w_planes = wT.rearrange("(p t) n -> t p n", t=PACK)
        w_window = []
        for t in range(PACK):
            plane = keep.tile([P, ITEMS], F32, name="w_window%d" % t, tag="plane%d" % t, align_bytes=64)
            nc.sync.dma_start(out=plane[:], in_=w_planes[t])
            w_window.append(plane)

        x_view = xT[0].rearrange("(p t) r -> p t r", t=PACK)
        y_view = y[0].rearrange("(c p) n -> p c n", p=P)
        x_raw = {}
        y_group = {}

        def load_x(first, count):
            raw = keep.tile([P, PACK, count * P], F32, name="x_raw", tag="x_rows%d" % first, align_bytes=64)
            nc.sync.dma_start(out=raw[:], in_=x_view[:, :, first * P : (first + count) * P])
            for e in range(count):
                x_raw[first + e] = raw[:, :, e * P :]

        def load_y(first, count):
            raw = keep.tile([P, count, SLOTS], F32, name="y_raw", tag="y_rows%d" % first, align_bytes=64)
            nc.sync.dma_start(out=raw[:], in_=y_view[:, first : first + count, :])
            for c in range(first, first + count):
                if c in TARGET_GROUPS:
                    y_group[c] = raw[:, c - first : c - first + TARGET_GROUPS[c], :]

        load_x(0, 2)
        load_y(0, 1)
        load_x(2, 2)
        load_y(1, 1)
        load_y(2, 1)
        load_x(4, 2)
        load_y(3, 1)
        load_x(6, 2)
        load_y(4, 2)
        load_y(6, 2)

        wt_row = keep.tile([P, ROWS], F32, name="wt_row")
        wt_lines = wt_row[:].rearrange("s (p b k) -> s p b k", b=CHUNKS // PACK, k=PACK)
        for b in range(CHUNKS // PACK):
            bank = psum.tile([P, PACK, P], F32, name="spread", tag="resid", bufs=3)
            for k in range(PACK):
                col = PACK * b + k
                nc.tensor.transpose(bank[:, k, :], wt_runs[:, col : col + 1].to_broadcast([P, P]), ident[:])
            nc.scalar.activation(out=wt_lines[:, :, b, :], in_=bank[:].rearrange("s k p -> s p k"), func=ACT.Copy)

        ts_dealt = keep.tile([P, SLOTS], F32, name="ts_dealt")
        nc.vector.tensor_copy(
            out=ts_dealt[:].rearrange("p (j b i) -> p b j i", j=PACK, i=RUN), in_=ts_window[:].indirect(offsets[:])
        )
        ts_turned = psum.tile([P, PACK, P], F32, name="ts_turned", tag="resid", bufs=3)
        for j in range(PACK):
            nc.tensor.transpose(ts_turned[:, j, :], ts_dealt[:, j * P : (j + 1) * P], ident[:])
        nts_col = keep.tile([P, PACK], F32, name="nts_col")
        nc.scalar.activation(out=nts_col[:], in_=ts_turned[:, :, 0], func=ACT.Copy, scale=-1.0)
        ts_spread = psum.tile([P, PACK, P], F32, name="ts_spread", tag="resid", bufs=3)
        for j in range(PACK):
            nc.tensor.transpose(ts_spread[:, j, :], nts_col[:, j : j + 1].to_broadcast([P, P]), ident[:])
        factor = keep.tile([P, PACK, ROWS], F32, name="factor")
        nts_row = keep.tile([P, SLOTS], F32, name="nts_row")
        for j in range(PACK - 1):
            nc.scalar.activation(out=factor[:, j, :], in_=wt_row[:], func=ACT.Copy, scale=nts_col[:, j : j + 1])
        nc.scalar.activation(out=nts_row[:], in_=ts_spread[:].rearrange("r j s -> r (j s)"), func=ACT.Copy)

        w_d = keep.tile([P, SLOTS, PACK], BF16, name="w_d", align_bytes=64)
        wd_codes = keep.tile([P, SLOTS], U32, name="wd_codes", align_bytes=64)
        wd_scales = keep.tile([P, SLOTS], U8, name="wd_scales", align_bytes=64)
        wi_scales = keep.tile([P, FEATS], U8, name="wi_scales", align_bytes=64)
        wi_first = keep.tile([P, P, 2, PACK], BF16, name="wi_first", align_bytes=64)
        w_i = keep.tile([P, P, PACK, PACK], BF16, name="w_i", tag=tag_of("w_i", 0), align_bytes=64)

        def gather_plane(t):
            nc.vector.tensor_copy(
                out=w_d[:, :, t].rearrange("p (j b i) -> p b j i", j=PACK, i=RUN),
                in_=w_window[t][:].indirect(offsets[:]),
            )

        first_turned = psum.tile([P, PACK, P], F32, name="turned", tag="grad", bufs=2)
        last_turned = psum.tile([P, PACK, P], F32, name="turned", tag="grad", bufs=2)
        wi_codes = {}

        def turn_planes(turned, word):
            words = w_d[:].rearrange("p i t -> p (i t)").bitcast(F32)
            for j in range(PACK):
                nc.tensor.transpose(turned[:, j, :], words[:, 2 * j * P + word : 2 * (j + 1) * P : 2], ident[:])

        def turn_first_planes():
            turn_planes(first_turned, 0)

        def turn_last_planes():
            turn_planes(last_turned, 1)

        def copy_planes(turned, target):
            halves = turned[:].rearrange("s j p -> s (j p)").bitcast(BF16)
            nc.scalar.copy(
                out=target.rearrange("s p e j -> s p j e"),
                in_=halves.rearrange("s (j p e) -> s p j e", j=PACK, e=2),
            )

        def copy_first_planes():
            copy_planes(first_turned, wi_first[:])

        def join_first_planes():
            nc.vector.tensor_copy(out=w_i[:, :, :2, :], in_=wi_first[:])

        def copy_last_planes():
            copy_planes(last_turned, w_i[:, :, 2:, :])

        def quantize_turned():
            wi_codes[0] = keep.tile([P, FEATS], U32, name="wi_codes", tag=tag_of("wi_codes", 0), align_bytes=64)
            nc.vector.quantize_mx(
                out=wi_codes[0][:].bitcast(E4M3X4), scales=wi_scales[:], in_=w_i[:].rearrange("s p t j -> s (p t j)")
            )

        x_bf, x_codes, x_scales, summand = ({} for i in range(4))
        score, scaled, resid, square, bell, weighted, h, h_codes, h_scales, grad = ({} for i in range(10))

        def cast_x(c):
            count = ROW_GROUPS[c]
            x_bf[c] = keep.tile([P, count * P, PACK], BF16, name="x_bf", tag=tag_of("x_bf", c), align_bytes=64)
            target = x_bf[c][:].rearrange("p (a i) t -> p a t i", i=2)
            source = x_raw[c][:, :, : count * P].rearrange("p t (a i) -> p a t i", i=2)
            if c in CAST_ON_POOL:
                nc.gpsimd.tensor_scalar(out=target, in0=source, scalar1=1.0, scalar2=0.0, op0=MULT, op1=ADD)
            elif c in CAST_ON_VECTOR:
                nc.vector.tensor_copy(out=target, in_=source)
            else:
                nc.scalar.activation(out=target, in_=source, func=ACT.Copy)

        def quantize_x(c):
            count = ROW_GROUPS[c]
            codes = keep.tile([P, count * P], U32, name="x_codes", tag=tag_of("x_codes", c), align_bytes=64)
            scales = keep.tile([P, count * P], U8, name="x_scales%d" % c, align_bytes=64)
            nc.vector.quantize_mx(
                out=codes[:].bitcast(E4M3X4), scales=scales[:], in_=x_bf[c][:].rearrange("p r t -> p (r t)")
            )
            for e in range(count):
                x_codes[c + e] = codes[:, e * P : (e + 1) * P]
                x_scales[c + e] = scales[:, e * P : (e + 1) * P]

        def deal_targets(c):
            count = TARGET_GROUPS[c]
            dealt = keep.tile([P, PACK, count * P], F32, name="dealt", tag=tag_of("dealt", c), align_bytes=64)
            for e in range(count):
                summand[c + e] = dealt[:, :, e * P : (e + 1) * P]
            source = y_group[c].rearrange("r c (b j i) -> r (c b) j i", j=PACK, i=RUN)
            target = dealt[:].rearrange("r j (b i) -> r b j i", i=RUN)
            if c in DEALT_ON_POOL:
                nc.gpsimd.tensor_scalar(out=target, in0=source, scalar1=1.0, scalar2=0.0, op0=MULT, op1=ADD)
            elif c in DEALT_ON_SCALAR:
                nc.scalar.activation(out=target, in_=source, func=ACT.Copy)
            else:
                nc.vector.tensor_copy(out=target, in_=source)

        def multiply_scores(c):
            score[c] = psum.tile([P, SLOTS], F32, name="score", tag="score", bufs=2)
            nc.tensor.matmul_mx(
                out=score[c][:],
                lhsT=x_codes[c].bitcast(E4M3X4),
                lhsT_scale=x_scales[c],
                rhs=wd_codes[:].bitcast(E4M3X4),
                rhs_scale=wd_scales[:],
                start=True,
                stop=True,
            )

        def scale_scores(c):
            scaled[c] = keep.tile([P, SLOTS], F32, name="scaled", tag=tag_of("scaled", c), align_bytes=64)
            nc.vector.tensor_tensor(out=scaled[c][:], in0=score[c][:], in1=nts_row[:], op=MULT)

        def turn_targets(c):
            resid[c] = psum.tile([P, PACK, P], F32, name="resid", tag="resid", bufs=3)
            for j in range(PACK):
                nc.tensor.matmul(
                    resid[c][:, j, :], summand[c][:, j, :], ident[:], start=(j == 0), stop=False, is_transpose=True
                )

        def turn_scores(c):
            for j in range(PACK):
                nc.tensor.matmul(
                    resid[c][:, j, :], scaled[c][:, j * P : (j + 1) * P], ident[:],
                    start=False, stop=(j == PACK - 1), is_transpose=True,
                )

        def square_residual(c):
            square[c] = keep.tile([P, PACK, P], F32, name="square", tag=tag_of("square", c), align_bytes=64)
            nc.scalar.activation(out=square[c][:], in_=resid[c][:], func=ACT.Square)

        def exponentiate(c):
            bell[c] = keep.tile([P, PACK, P], F32, name="bell", tag=tag_of("bell", c), align_bytes=64)
            nc.scalar.activation(out=bell[c][:], in_=square[c][:], func=ACT.Exp, scale=-0.5)

        def weigh_bell(c):
            weighted[c] = keep.tile([P, PACK, P], F32, name="weighted", tag=tag_of("weighted", c), align_bytes=64)
            nc.gpsimd.tensor_tensor(out=weighted[c][:], in0=bell[c][:], in1=factor[:, :, c * P : (c + 1) * P], op=MULT)

        def weigh_residual(c):
            weighted[c] = keep.tile([P, PACK, P], F32, name="weighted", tag=tag_of("weighted", c), align_bytes=64)
            nc.vector.tensor_tensor(out=weighted[c][:], in0=resid[c][:], in1=factor[:, :, c * P : (c + 1) * P], op=MULT)

        def form_h(c):
            other = resid[c] if c in WEIGHED_ON_POOL else bell[c]
            h[c] = keep.tile([P, P, PACK], BF16, name="h", tag=tag_of("h", c), align_bytes=64)
            nc.vector.tensor_tensor(
                out=h[c][:].rearrange("s (a i) j -> s a j i", i=2),
                in0=other[:].rearrange("s j (a i) -> s a j i", i=2),
                in1=weighted[c][:].rearrange("s j (a i) -> s a j i", i=2),
                op=MULT,
            )

        def quantize_h(c):
            h_codes[c] = keep.tile([P, P], U32, name="h_codes", tag=tag_of("h_codes", c), align_bytes=64)
            h_scales[c] = keep.tile([P, P], U8, name="h_scales%d" % c, align_bytes=64)
            nc.vector.quantize_mx(
                out=h_codes[c][:].bitcast(E5M2X4), scales=h_scales[c][:], in_=h[c][:].rearrange("s r j -> s (r j)")
            )

        def multiply_columns(c, bank, cols):
            nc.tensor.matmul_mx(
                out=bank[:],
                lhsT=h_codes[c][:].bitcast(E5M2X4),
                lhsT_scale=h_scales[c][:],
                rhs=wi_codes[0][:, cols].bitcast(E4M3X4),
                rhs_scale=wi_scales[:, cols],
                start=True,
                stop=True,
            )

        def multiply_gradient(c):
            tag = "score" if c >= LATE else "grad"
            grad[c] = psum.tile([P, FEATS], F32, name="grad", tag=tag, bufs=2)
            multiply_columns(c, grad[c], slice(0, FEATS))

        def store_gradient(c):
            result = keep.tile([P, FEATS], F32, name="result", tag=tag_of("result", c), align_bytes=64)
            if c in STORED_BY_VECTOR:
                nc.vector.tensor_copy(out=result[:], in_=grad[c][:])
            else:
                nc.scalar.activation(out=result[:], in_=grad[c][:], func=ACT.Copy)
            nc.sync.dma_start(out=out[0, c * P : (c + 1) * P, :], in_=result[:])

        def finish_in_halves(c):
            width = FEATS // 2
            for half in range(2):
                cols = slice(half * width, (half + 1) * width)
                bank = psum.tile([P, width], F32, name="last_grad", tag="resid", bufs=3)
                multiply_columns(c, bank, cols)
                result = keep.tile([P, width], F32, name="last_result%d" % half)
                if half == 0:
                    nc.vector.tensor_copy(out=result[:], in_=bank[:])
                    nc.sync.dma_start(out=out[0, c * P : (c + 1) * P, cols], in_=result[:])
                else:
                    nc.scalar.activation(out=result[:], in_=bank[:], func=ACT.Copy)
                    nc.scalar.dma_start(out=out[0, c * P : (c + 1) * P, cols], in_=result[:])

        def last_factor():
            for j in range(PACK - 1, PACK):
                nc.vector.tensor_scalar(
                    out=factor[:, j, :], in0=wt_row[:], scalar1=nts_col[:, j : j + 1], scalar2=None, op0=MULT
                )

        def quantize_columns():
            nc.vector.quantize_mx(
                out=wd_codes[:].bitcast(E4M3X4), scales=wd_scales[:], in_=w_d[:].rearrange("p i t -> p (i t)")
            )

        gather_plane(0)
        gather_plane(1)
        turn_first_planes()
        last_factor()
        gather_plane(2)
        copy_first_planes()
        gather_plane(3)
        cast_x(0)
        cast_x(1)
        turn_last_planes()
        quantize_columns()
        quantize_x(0)
        multiply_scores(0)
        quantize_x(1)
        multiply_scores(1)
        deal_targets(0)
        join_first_planes()
        turn_targets(0)
        copy_last_planes()
        cast_x(2)
        scale_scores(0)
        turn_scores(0)
        square_residual(0)
        exponentiate(0)
        quantize_x(2)
        multiply_scores(2)
        deal_targets(1)
        turn_targets(1)
        scale_scores(1)
        turn_scores(1)
        square_residual(1)
        exponentiate(1)
        multiply_scores(3)
        deal_targets(2)
        turn_targets(2)
        cast_x(4)
        quantize_x(4)
        weigh_residual(0)
        quantize_turned()
        scale_scores(2)
        turn_scores(2)
        multiply_scores(4)
        square_residual(2)
        exponentiate(2)
        deal_targets(3)
        turn_targets(3)
        weigh_residual(1)
        scale_scores(3)
        turn_scores(3)
        multiply_scores(5)
        square_residual(3)
        exponentiate(3)
        cast_x(6)
        quantize_x(6)
        deal_targets(6)
        deal_targets(4)
        turn_targets(4)
        form_h(0)
        weigh_residual(2)
        scale_scores(4)
        turn_scores(4)
        multiply_scores(6)
        square_residual(4)
        exponentiate(4)
        quantize_h(0)
        multiply_gradient(0)
        deal_targets(5)
        turn_targets(5)
        form_h(1)
        weigh_residual(3)
        store_gradient(0)
        scale_scores(5)
        turn_scores(5)
        multiply_scores(7)
        square_residual(5)
        exponentiate(5)
        quantize_h(1)
        multiply_gradient(1)
        turn_targets(6)
        form_h(2)
        weigh_residual(4)
        store_gradient(1)
        scale_scores(6)
        turn_scores(6)
        square_residual(6)
        exponentiate(6)
        quantize_h(2)
        multiply_gradient(2)
        turn_targets(7)
        form_h(3)
        weigh_residual(5)
        store_gradient(2)
        scale_scores(7)
        turn_scores(7)
        square_residual(7)
        exponentiate(7)
        quantize_h(3)
        multiply_gradient(3)
        form_h(4)
        weigh_residual(6)
        store_gradient(3)
        form_h(5)
        quantize_h(4)
        multiply_gradient(4)
        store_gradient(4)
        form_h(6)
        quantize_h(5)
        multiply_gradient(5)
        store_gradient(5)
        weigh_residual(7)
        quantize_h(6)
        multiply_gradient(6)
        store_gradient(6)
        form_h(7)
        quantize_h(7)
        finish_in_halves(7)
